import numpy as np
import ml_dtypes


def mxq(x, axis, fmt="e4m3"):
    dtype, down = {"e4m3": (ml_dtypes.float8_e4m3fn, 7), "e5m2": (ml_dtypes.float8_e5m2, 14)}[fmt]
    v = np.moveaxis(np.asarray(x, np.float32).astype(ml_dtypes.bfloat16).astype(np.float64), axis, -1)
    blocks = v.reshape(v.shape[:-1] + (-1, 32))
    amax = np.abs(blocks).max(-1, keepdims=True)
    byte = np.maximum(np.where(amax > 0, np.frexp(amax)[1] - 1 + 127, 0) - down, 1)
    scale = np.exp2(byte - 127.0)
    codes = (blocks / scale).astype(np.float32).astype(dtype).astype(np.float64)
    return np.moveaxis((codes * scale).reshape(v.shape), -1, axis)


WIDE = False


def mx_kscale(k):
    if not WIDE:
        return np.ones(k)
    levels = np.array([10, -10, 5, -5, 0])
    if k % 512:
        return np.exp2(np.random.permutation(np.resize(levels, k // 32))).repeat(32)
    a = np.empty((k // 512, 16))
    for p in range(k // 512):
        a[p, :8] = np.random.permutation(np.resize(levels, 8))
        for g in range(8):
            far = levels[np.abs(levels - a[p, g]) >= 10]
            a[p, g + 8] = far[np.random.randint(len(far))]
    return np.exp2(a.ravel()).repeat(32)


BF16 = ml_dtypes.bfloat16


def bf(x):
    return np.asarray(x, np.float32).astype(BF16)


def f64(x):
    return np.asarray(x).astype(np.float64)

def planes(Y):
    n, m = Y.shape
    b = f64(bf(Y)).reshape(n // 32, 32, m)
    amax = np.abs(b).max(1)
    byte = np.clip(np.where(amax > 0, np.frexp(amax)[1] - 1 + 127 - 7, 1), 1, 254)
    codes = (b * np.exp2(127.0 - byte)[:, None, :]).reshape(n, m).astype(np.float32).astype(ml_dtypes.float8_e4m3fn).view(np.uint8)
    words = codes.reshape(n // 512, 128, 4, m).transpose(0, 1, 3, 2)
    return np.ascontiguousarray(words), np.ascontiguousarray(byte.astype(np.uint8).reshape(n // 512, 16, m))


N, M, D, E = 1024, 2048, 512, 1024

EPS = 1e-6
U_SIZE = 0.005


def setup_inputs():
    s, t = mx_kscale(N), mx_kscale(D)
    ds = np.random.standard_normal((N, M)) * (U_SIZE * np.sqrt(D / N))
    q = 0.5 + np.random.standard_normal((N, D))
    u = (0.5 + np.random.standard_normal((M, D))) * U_SIZE
    gamma = 1.0 + 0.1 * np.random.standard_normal(D)
    l = 1.0 + 0.1 * np.random.standard_normal(D)
    wk = np.random.standard_normal((E, D)) / np.sqrt(D)
    return {"ds": bf(ds * s[:, None]), "q": bf(q / s[:, None]), "u": bf(u), "gamma": bf(gamma),
            "l": bf(l * t), "wk": bf(wk / t[None, :])}


def rms_norm_backward(u, gamma, dk):
    rho = np.sqrt(np.mean(u * u, axis=-1, keepdims=True) + EPS)
    uh = u / rho
    e = dk * gamma[None, :]
    return (e - uh * np.mean(e * uh, axis=-1, keepdims=True)) / rho


def core(ds, q, u, gamma, l, wk):
    dk = (mxq(f64(ds).T, 1, "e4m3") @ mxq(f64(q), 0, "e4m3")) / np.sqrt(D)
    du = rms_norm_backward(f64(u), f64(gamma), dk)
    dz = du * f64(l)[None, :]
    return mxq(dz, 1, "e4m3") @ mxq(f64(wk), 1, "e4m3").T


def reference(ds, q, u, gamma, l, wk):
    R_out = core(ds, q, u, gamma, l, wk)
    words, scales = planes(R_out.T)
    return R_out, words, scales

@@ -1,0 +1,367 @@
+from contextlib import ExitStack
+
+import concourse.mybir as mybir
+from concourse.masks import make_identity
+
+N, M, D, E = 1024, 2048, 512, 1024
+FLOPS = 2 * N * M * D + 2 * M * D * E
+
+F32 = mybir.dt.float32
+BF16 = mybir.dt.bfloat16
+U32 = mybir.dt.uint32
+I32 = mybir.dt.int32
+U8 = mybir.dt.uint8
+X4 = mybir.dt.float8_e4m3fn_x4
+ALU = mybir.AluOpType
+ACT = mybir.ActivationFunctionType
+
+P = 128
+EPS = 1e-6
+Q_DVE = 320
+CUB = 4
+ILV = {0: 'v', 1: 'a', (6, 1): 'v', (3, 1): 'v', (5, 1): 'a', (7, 1): 'a', (4, 1): 'a', (0, 1): 'v', (6, 0): 'v', (2, 1): 'a', (3, 0): 'v', (0, 0): 'v', (2, 0): 'v', (1, 0): 'v', (1, 1): 'a', (4, 0): 'v', (5, 0): 'v'}
+DVE_PLANES = [3, 7, 13, 14, 15]
+DSL = 3
+WK0 = 0
+DSI = {0: [1], 1: [], 3: [], 5: [], 7: [5], 9: [6], 11: [7], 4: [3], 2: [2], 10: [], 8: [], 6: [4]}
+SQ = {0: [3, 2], 1: [4, 5], 2: [6, 7, 8], 3: [10, 9], 4: [], 5: [11], 6: [12], 7: [], 8: [], 9: [13], 10: [15, 14]}
+ST = {6: 3, 10: 4, 1: 1, 2: 2}
+GROUPS = [(0, 2), (2, 2), (4, 4), (8, 4), (12, 4)]
+TILES = M // P
+UNIT = 256
+CHUNKS = [(0, 256), (256, 256), (512, 512), (1024, 512), (1536, 512)]
+
+
+def tile_ia3scaledqknormkeybackwardtoinput_x1_kernel(tc, ds, q, u, gamma, l, wk, out_0, out_1, out_2):
+    nc = tc.nc
+    with ExitStack() as ctx:
+        keep = ctx.enter_context(tc.tile_pool(name="keep", bufs=1))
+        work = ctx.enter_context(tc.tile_pool(name="work", bufs=3))
+        ps_dk = ctx.enter_context(tc.psum_pool(name="ps_dk", bufs=2))
+        ps_tr = ctx.enter_context(tc.psum_pool(name="ps_tr", bufs=2))
+        ps_out = ctx.enter_context(tc.psum_pool(name="ps_out", bufs=4))
+        ctx.enter_context(tc.manual_schedule())
+
+        q_raw = [keep.tile([P, 4, D], BF16, name="q_raw%d" % g) for g in range(2)]
+        ds_raw = [keep.tile([P, 2, 4, w], BF16, name="ds_raw%d" % c) for c, (a, w) in enumerate(CHUNKS)]
+        u_raw = [keep.tile([P, 2, D], BF16, name="u_raw%d" % c) for c in range(TILES // 2)]
+        wk_raw = keep.tile([P, 2, 4, D], BF16, name="wk_raw")
+        g_row = keep.tile([P, D], BF16, name="g_row")
+        ones = keep.tile([P, P], BF16, name="ones")
+        l_col = keep.tile([P, 4], BF16, name="l_col")
+        ident = keep.tile([P, P], F32, name="ident")
+        warm = keep.tile([P, 1], F32, name="warm")
+        eps = keep.tile([P, 1], F32, name="eps")
+
+        def load_ds(c):
+            a, w = CHUNKS[c]
+            for g in range(2):
+                nc.sync.dma_start(
+                    out=ds_raw[c][:, g, :, :],
+                    in_=ds[512 * g : 512 * (g + 1), a : a + w].rearrange("(p j) m -> p j m", j=4),
+                )
+
+        def load_u(c):
+            nc.sync.dma_start(
+                out=u_raw[c][:], in_=u[256 * c : 256 * (c + 1), :].rearrange("(i p) d -> p i d", i=2)
+            )
+
+        nc.vector.memset(g_row[:], 0.0)
+        nc.vector.memset(ones[:], 1.0)
+        nc.vector.memset(warm[:], 1.0)
+        nc.vector.tensor_scalar(eps[:], warm[:], 0.0, D * EPS, ALU.mult, ALU.add)
+        nc.scalar.activation(warm[:], warm[:], ACT.Sqrt)
+        make_identity(nc, ident[:])
+        nc.scalar.dma_start(out=l_col[:], in_=l.rearrange("(p t) -> p t", t=4))
+        nc.scalar.dma_start(out=g_row[0:1, :], in_=gamma.rearrange("(o d) -> o d", o=1))
+
+        def load_q(g):
+            nc.sync.dma_start(
+                out=q_raw[g][:], in_=q[512 * g : 512 * (g + 1), :].rearrange("(p j) d -> p j d", j=4)
+            )
+
+        load_q(0)
+        load_q(1)
+        load_ds(0)
+        load_u(0)
+        nc.sync.dma_start(out=wk_raw[:], in_=wk.rearrange("(g p t) d -> p g t d", g=2, t=4))
+        load_ds(1)
+        load_u(1)
+        load_ds(2)
+        load_u(2)
+        load_u(3)
+        load_ds(3)
+        load_u(4)
+        load_u(5)
+        load_ds(4)
+        load_u(6)
+        load_u(7)
+
+        def spread(x):
+            return x.rearrange("p (c i) t -> p c t i", i=4)
+
+        def gather(x):
+            return x.rearrange("p t (c i) -> p c t i", i=4)
+
+        ssq = [keep.tile([P, w], F32, name="ssq%d" % c) for c, (a, w) in enumerate(GROUPS)]
+        zz = [keep.tile([P, w], F32, name="zz%d" % c) for c, (a, w) in enumerate(GROUPS)]
+        ir = [keep.tile([P, w], F32, name="ir%d" % c) for c, (a, w) in enumerate(GROUPS)]
+        k2 = [keep.tile([P, w], F32, name="k2%d" % c) for c, (a, w) in enumerate(GROUPS)]
+
+        def column(x, i):
+            c = [n for n, (a, w) in enumerate(GROUPS) if a <= i < a + w][0]
+            return x[c][:, i - GROUPS[c][0] : i - GROUPS[c][0] + 1]
+
+        def u_square(i):
+            c, h = divmod(i, 2)
+            sq = work.tile([P, D], BF16, name="sq")
+            nc.scalar.activation(sq[:], u_raw[c][:, h, :], ACT.Square, accum_out=column(ssq, i))
+
+        def u_stats(c):
+            nc.scalar.activation(zz[c][:], ssq[c][:], ACT.Sqrt, bias=eps[:])
+            nc.vector.reciprocal(ir[c][:], zz[c][:])
+            nc.vector.scalar_tensor_tensor(k2[c][:], ir[c][:], -1.0, ir[c][:], ALU.mult, ALU.mult)
+
+        qg = [keep.tile([P, D, 4], BF16, name="qg%d" % g, align_bytes=64) for g in range(2)]
+        qc = keep.tile([P, 2, D], U32, name="qc", align_bytes=64)
+        qs = keep.tile([P, 2, D], U8, name="qs", align_bytes=64)
+        for g in range(2):
+            nc.vector.tensor_copy(out=spread(qg[g][:, 0:Q_DVE, :]), in_=gather(q_raw[g][:, :, 0:Q_DVE]))
+            nc.scalar.copy(spread(qg[g][:, Q_DVE:D, :]), gather(q_raw[g][:, :, Q_DVE:D]))
+        for g in range(2):
+            nc.vector.quantize_mx(
+                out=qc[:, g, :].bitcast(X4), scales=qs[:, g, :], in_=qg[g][:].rearrange("p c t -> p (c t)")
+            )
+
+        dsc = [keep.tile([P, 2, UNIT], U32, name="dsc%d" % k, align_bytes=64) for k in range(M // UNIT)]
+        dss = [keep.tile([P, 2, UNIT], U8, name="dss%d" % k, align_bytes=64) for k in range(M // UNIT)]
+        grouped = {}
+
+        def ds_interleave(k):
+            c = [i for i, (a, w) in enumerate(CHUNKS) if a <= k * UNIT < a + w][0]
+            off = k * UNIT - CHUNKS[c][0]
+            g0 = work.tile([P, UNIT, 4], BF16, bufs=4, name="g0", align_bytes=64)
+            g1 = work.tile([P, UNIT, 4], BF16, bufs=4, name="g1", align_bytes=64)
+            for g, t in ((0, g0), (1, g1)):
+                src = gather(ds_raw[c][:, g, :, off : off + UNIT])
+                eng = ILV.get((k, g), ILV[g])
+                if eng == "v":
+                    nc.vector.tensor_copy(out=spread(t[:]), in_=src)
+                elif eng == "a":
+                    nc.scalar.copy(spread(t[:]), src)
+                else:
+                    nc.gpsimd.tensor_scalar(spread(t[:]), src, 1.0, 1.0, ALU.mult, ALU.mult)
+            grouped[k] = (g0, g1)
+
+        def ds_quantize(k):
+            for g in range(2):
+                nc.vector.quantize_mx(
+                    out=dsc[k][:, g, :].bitcast(X4),
+                    scales=dss[k][:, g, :],
+                    in_=grouped[k][g][:].rearrange("p c t -> p (c t)"),
+                )
+
+        dk, gr, cu, coef, tr, dzg, dzc, dzs = {}, {}, {}, {}, {}, {}, {}, {}
+        gam = keep.tile([P, D], F32, name="gam")
+        wkc = keep.tile([P, E], U32, name="wkc", align_bytes=64)
+        wks = keep.tile([P, E], U8, name="wks", align_bytes=64)
+        pls = keep.tile([P, 2, M], U8, name="pls", align_bytes=64)
+
+        def mx1(i):
+            k, h = divmod(i, 2)
+            bank = ps_dk.tile([P, D], F32, name="dk")
+            for g in range(2):
+                nc.tensor.matmul_mx(
+                    out=bank[:],
+                    lhsT=dsc[k][:, g, h * P : (h + 1) * P].bitcast(X4),
+                    lhsT_scale=dss[k][:, g, h * P : (h + 1) * P],
+                    rhs=qc[:, g, :].bitcast(X4),
+                    rhs_scale=qs[:, g, :],
+                    start=(g == 0),
+                    stop=(g == 1),
+                )
+            dk[i] = bank
+
+        def p2(i):
+            t = work.tile([P, D], F32, bufs=6, name="gr")
+            nc.vector.scalar_tensor_tensor(t[:], dk[i][:], column(ir, i), gam[:], ALU.mult, ALU.mult)
+            gr[i] = t
+
+        def p1(i):
+            c, h = divmod(i, 2)
+            junk = work.tile([P, D], BF16, bufs=3, name="junk")
+            ncoef = work.tile([P, 1], F32, bufs=6, name="ncoef")
+            nc.vector.scalar_tensor_tensor(
+                junk[:], gr[i][:], column(k2, i), u_raw[c][:, h, :], ALU.mult, ALU.mult, accum_out=ncoef[:]
+            )
+            coef[i] = ncoef
+
+        def cu_make(i):
+            c, h = divmod(i, 2)
+            t = work.tile([P, 4, P], F32, bufs=CUB, name="cu")
+            src = u_raw[c][:, h, :].rearrange("m (p t) -> m t p", t=4)
+            nc.scalar.activation(t[:], src, ACT.Copy, scale=coef[i][:])
+            cu[i] = t
+
+        def transposes(i):
+            bank = ps_tr.tile([P, 4, P], F32, name="tr")
+            for t in range(4):
+                nc.tensor.matmul(bank[:, t, :], gr[i][:, t:D:4], ident[:], start=True, stop=False, is_transpose=True)
+                nc.tensor.matmul(bank[:, t, :], cu[i][:, t, :], ident[:], start=False, stop=True, is_transpose=True)
+            tr[i] = bank
+
+        def times_l(i):
+            t = work.tile([P, P, 4], BF16, bufs=5, name="dzg", align_bytes=64)
+            nc.vector.tensor_tensor(
+                t[:],
+                tr[i][:].rearrange("p t m -> p m t"),
+                l_col[:].unsqueeze(1).to_broadcast([P, P, 4]),
+                ALU.mult,
+            )
+            dzg[i] = t
+
+        def quantize_dz(i):
+            c = work.tile([P, P], U32, bufs=6, name="dzc", align_bytes=64)
+            s = work.tile([P, P], U8, bufs=6, name="dzs", align_bytes=64)
+            nc.vector.quantize_mx(out=c[:].bitcast(X4), scales=s[:], in_=dzg[i][:].rearrange("p m t -> p (m t)"))
+            dzc[i], dzs[i] = c, s
+
+        ob_banks, p_sb, p_codes = {}, {}, {}
+
+        def mx2(i):
+            banks = []
+            for g in range(2):
+                pl = ps_out.tile([P, 4, P], F32, name="ob")
+                for t in range(4):
+                    cols = slice(g * 512 + t * P, g * 512 + (t + 1) * P)
+                    nc.tensor.matmul_mx(
+                        out=pl[:, t, :],
+                        lhsT=wkc[:, cols].bitcast(X4),
+                        lhsT_scale=wks[:, cols],
+                        rhs=dzc[i][:].bitcast(X4),
+                        rhs_scale=dzs[i][:],
+                        start=True,
+                        stop=True,
+                    )
+                ob = ps_out.tile([P, 4, P], F32, name="ob")
+                cols = slice(g * 512, (g + 1) * 512)
+                nc.tensor.matmul_mx(
+                    out=ob[:].rearrange("p t m -> p (t m)"),
+                    lhsT=dzc[i][:].bitcast(X4),
+                    lhsT_scale=dzs[i][:],
+                    rhs=wkc[:, cols].bitcast(X4),
+                    rhs_scale=wks[:, cols],
+                    start=True,
+                    stop=True,
+                )
+                banks.append((pl, ob))
+            ob_banks[i] = banks
+
+        def evacuate(i):
+            banks = ob_banks[i]
+            o = work.tile([P, 2, P, 4], F32, name="o")
+            p = work.tile([P, 2, P, 4], BF16, bufs=5, name="p", align_bytes=64)
+            for g in range(2):
+                pl, ob = banks[g]
+                if i in DVE_PLANES:
+                    nc.vector.tensor_copy(out=p[:, g, :, :], in_=pl[:].rearrange("p t m -> p m t"))
+                else:
+                    nc.scalar.copy(p[:, g, :, :], pl[:].rearrange("p t m -> p m t"))
+                nc.scalar.copy(o[:, g, :, :], ob[:].rearrange("m t p -> m p t"))
+            nc.sync.dma_start(out=out_0[i * P : (i + 1) * P, :], in_=o[:].rearrange("m g p t -> m (g p t)"))
+            p_sb[i] = p
+
+        def quantize_planes(i):
+            c, h = divmod(i, 2)
+            if h == 0:
+                p_codes[c] = work.tile([P, 2, 2 * P], U32, name="pc", align_bytes=64)
+            for g in range(2):
+                nc.vector.quantize_mx(
+                    out=p_codes[c][:, g, h * P : (h + 1) * P].bitcast(X4),
+                    scales=pls[:, g, i * P : (i + 1) * P],
+                    in_=p_sb[i][:, g, :, :].rearrange("p m t -> p (m t)"),
+                )
+            if h == 1:
+                nc.sync.dma_start(
+                    out=out_1[:, :, 256 * c : 256 * (c + 1), :].rearrange("g p m t -> p g (m t)").bitcast(I32),
+                    in_=p_codes[c][:].bitcast(I32),
+                )
+            if i % 8 == 7:
+                cols = slice((i - 7) * P, (i + 1) * P)
+                for quad in range(4):
+                    nc.sync.dma_start(
+                        out=out_2[:, 4 * quad : 4 * quad + 4, cols].rearrange("g r m -> r g m").bitcast(I32),
+                        in_=pls[32 * quad : 32 * quad + 4, :, cols].bitcast(I32),
+                    )
+
+        words = wk_raw[:].rearrange("p g t d -> p (g t d)").bitcast(F32)
+        wg = keep.tile([P, E, 4], BF16, name="wg", align_bytes=64)
+        wbanks = []
+
+        def wk_transposes():
+            for b in range(4):
+                bank = ps_out.tile([P, 4, P], F32, name="ob")
+                for s in range(4):
+                    base = (2 * b + s // 2) * 256
+                    nc.tensor.transpose(bank[:, s, :], words[:, base + s % 2 : base + 256 : 2], ident[:])
+                wbanks.append(bank)
+
+        def wk_copy(b, copy):
+            dst = (
+                wg[:, 256 * b : 256 * (b + 1), :]
+                .rearrange("p c k -> p (c k)")
+                .bitcast(F32)
+                .rearrange("p (a c w) -> p a c w", a=2, w=2)
+            )
+            copy(dst, wbanks[b][:].rearrange("p (a w) c -> p a c w", a=2))
+
+        def wk_quantize(g):
+            cols = slice(512 * g, 512 * (g + 1))
+            nc.vector.quantize_mx(
+                out=wkc[:, cols].bitcast(X4), scales=wks[:, cols], in_=wg[:, cols, :].rearrange("p c k -> p (c k)")
+            )
+
+        ds_interleave(0)
+        gbank = ps_tr.tile([P, 4, P], F32, name="tr")
+        nc.tensor.matmul(gbank[:].rearrange("p t m -> p (t m)"), ones[:], g_row[:], start=True, stop=True)
+        nc.scalar.copy(gam[:], gbank[:].rearrange("p t m -> p (t m)"))
+        u_square(0)
+        u_square(1)
+        ds_quantize(0)
+        u_stats(0)
+        mx1(0)
+        mx1(1)
+        wk_transposes()
+
+
+        LAG = {'p2': 0, 'tr': 1, 'mx1': -1, 'evl': 1, 'p1': 0, 'cu': 0, 'mx2': 2, 'ev': 2, 'qpl': 3, 'qdz': 1}
+        ORDER = ['p2', 'ds', 'tr', 'mx1', 'wk', 'p1', 'evl', 'qpl', 'sq', 'mx2', 'qdz', 'cu', 'dsq', 'ev']
+        FN = dict(p2=p2, tr=transposes, mx1=mx1, evl=times_l, p1=p1, cu=cu_make, mx2=mx2, ev=evacuate, qpl=quantize_planes, qdz=quantize_dz)
+        for s in range(0, TILES + LAG["qpl"]):
+            for name in ORDER:
+                if name in LAG:
+                    i = s - LAG[name]
+                    if 0 <= i < TILES and not (name == "mx1" and i < 2):
+                        FN[name](i)
+                elif name == "wk":
+                    if s == WK0:
+                        wk_copy(0, nc.vector.tensor_copy)
+                        wk_copy(1, nc.scalar.copy)
+                    if s == WK0 + 1:
+                        wk_copy(2, nc.vector.tensor_copy)
+                        wk_copy(3, nc.scalar.copy)
+                        wk_quantize(0)
+                    if s == WK0 + 2:
+                        wk_quantize(1)
+                elif name == "ds":
+                    for unit in DSI.get(s, []):
+                        ds_interleave(unit)
+                elif name == "dsq":
+                    unit = (s + DSL) // 2
+                    if 1 <= unit < M // UNIT and (s + DSL) % 2 == 1:
+                        ds_quantize(unit)
+                elif name == "sq":
+                    for i in SQ.get(s, []):
+                        u_square(i)
+                    if s in ST:
+                        u_stats(ST[s])

@@ -17,19 +17,12 @@ ACT = mybir.ActivationFunctionType
 
 P = 128
 EPS = 1e-6
-Q_DVE = 320
-CUB = 4
-ILV = {0: 'v', 1: 'a', (6, 1): 'v', (3, 1): 'v', (5, 1): 'a', (7, 1): 'a', (4, 1): 'a', (0, 1): 'v', (6, 0): 'v', (2, 1): 'a', (3, 0): 'v', (0, 0): 'v', (2, 0): 'v', (1, 0): 'v', (1, 1): 'a', (4, 0): 'v', (5, 0): 'v'}
-DVE_PLANES = [3, 7, 13, 14, 15]
-DSL = 3
-WK0 = 0
-DSI = {0: [1], 1: [], 3: [], 5: [], 7: [5], 9: [6], 11: [7], 4: [3], 2: [2], 10: [], 8: [], 6: [4]}
-SQ = {0: [3, 2], 1: [4, 5], 2: [6, 7, 8], 3: [10, 9], 4: [], 5: [11], 6: [12], 7: [], 8: [], 9: [13], 10: [15, 14]}
-ST = {6: 3, 10: 4, 1: 1, 2: 2}
-GROUPS = [(0, 2), (2, 2), (4, 4), (8, 4), (12, 4)]
 TILES = M // P
-UNIT = 256
-CHUNKS = [(0, 256), (256, 256), (512, 512), (1024, 512), (1536, 512)]
+UNIT = 2 * P
+UNITS = M // UNIT
+DS_CHUNKS = [(0, 256), (256, 256), (512, 512), (1024, 1024)]
+STAT_GROUPS = [(0, 2), (2, 2), (4, 2), (6, 2), (8, 4), (12, 4)]
+Q_VECTOR = 384
 
 
 def tile_ia3scaledqknormkeybackwardtoinput_x1_kernel(tc, ds, q, u, gamma, l, wk, out_0, out_1, out_2):
@@ -37,24 +30,23 @@ def tile_ia3scaledqknormkeybackwardtoinput_x1_kernel(tc, ds, q, u, gamma, l, wk,
     with ExitStack() as ctx:
         keep = ctx.enter_context(tc.tile_pool(name="keep", bufs=1))
         work = ctx.enter_context(tc.tile_pool(name="work", bufs=3))
-        ps_dk = ctx.enter_context(tc.psum_pool(name="ps_dk", bufs=2))
-        ps_tr = ctx.enter_context(tc.psum_pool(name="ps_tr", bufs=2))
-        ps_out = ctx.enter_context(tc.psum_pool(name="ps_out", bufs=4))
+        psum = ctx.enter_context(tc.psum_pool(name="psum", bufs=2))
         ctx.enter_context(tc.manual_schedule())
 
         q_raw = [keep.tile([P, 4, D], BF16, name="q_raw%d" % g) for g in range(2)]
-        ds_raw = [keep.tile([P, 2, 4, w], BF16, name="ds_raw%d" % c) for c, (a, w) in enumerate(CHUNKS)]
-        u_raw = [keep.tile([P, 2, D], BF16, name="u_raw%d" % c) for c in range(TILES // 2)]
-        wk_raw = keep.tile([P, 2, 4, D], BF16, name="wk_raw")
-        g_row = keep.tile([P, D], BF16, name="g_row")
-        ones = keep.tile([P, P], BF16, name="ones")
+        ds_raw = [keep.tile([P, 2, 4, w], BF16, name="ds_raw%d" % c) for c, (a, w) in enumerate(DS_CHUNKS)]
+        u_raw = [keep.tile([P, 2, D], BF16, name="u_raw%d" % c) for c in range(UNITS)]
+        wk_raw = [keep.tile([P, 4 * D], BF16, name="wk_raw%d" % g) for g in range(2)]
         l_col = keep.tile([P, 4], BF16, name="l_col")
+        g_col = keep.tile([P, 4], BF16, name="g_col")
         ident = keep.tile([P, P], F32, name="ident")
         warm = keep.tile([P, 1], F32, name="warm")
-        eps = keep.tile([P, 1], F32, name="eps")
+
+        def load_q(g):
+            nc.sync.dma_start(out=q_raw[g][:], in_=q[512 * g : 512 * (g + 1), :].rearrange("(p j) d -> p j d", j=4))
 
         def load_ds(c):
-            a, w = CHUNKS[c]
+            a, w = DS_CHUNKS[c]
             for g in range(2):
                 nc.sync.dma_start(
                     out=ds_raw[c][:, g, :, :],
@@ -62,40 +54,33 @@ def tile_ia3scaledqknormkeybackwardtoinput_x1_kernel(tc, ds, q, u, gamma, l, wk,
                 )
 
         def load_u(c):
+            nc.sync.dma_start(out=u_raw[c][:], in_=u[UNIT * c : UNIT * (c + 1), :].rearrange("(i p) d -> p i d", i=2))
+
+        def load_wk(g):
             nc.sync.dma_start(
-                out=u_raw[c][:], in_=u[256 * c : 256 * (c + 1), :].rearrange("(i p) d -> p i d", i=2)
+                out=wk_raw[g][:], in_=wk[512 * g : 512 * (g + 1), :].rearrange("(p t) d -> p (t d)", t=4)
             )
 
-        nc.vector.memset(g_row[:], 0.0)
-        nc.vector.memset(ones[:], 1.0)
         nc.vector.memset(warm[:], 1.0)
-        nc.vector.tensor_scalar(eps[:], warm[:], 0.0, D * EPS, ALU.mult, ALU.add)
+        nc.scalar.dma_start(out=g_col[:], in_=gamma.rearrange("(p t) -> p t", t=4))
+        nc.scalar.dma_start(out=l_col[:], in_=l.rearrange("(p t) -> p t", t=4))
         nc.scalar.activation(warm[:], warm[:], ACT.Sqrt)
         make_identity(nc, ident[:])
-        nc.scalar.dma_start(out=l_col[:], in_=l.rearrange("(p t) -> p t", t=4))
-        nc.scalar.dma_start(out=g_row[0:1, :], in_=gamma.rearrange("(o d) -> o d", o=1))
-
-        def load_q(g):
-            nc.sync.dma_start(
-                out=q_raw[g][:], in_=q[512 * g : 512 * (g + 1), :].rearrange("(p j) d -> p j d", j=4)
-            )
 
         load_q(0)
         load_q(1)
-        load_ds(0)
         load_u(0)
-        nc.sync.dma_start(out=wk_raw[:], in_=wk.rearrange("(g p t) d -> p g t d", g=2, t=4))
+        load_ds(0)
+        load_wk(0)
+        load_wk(1)
         load_ds(1)
         load_u(1)
         load_ds(2)
         load_u(2)
         load_u(3)
         load_ds(3)
-        load_u(4)
-        load_u(5)
-        load_ds(4)
-        load_u(6)
-        load_u(7)
+        for c in range(4, UNITS):
+            load_u(c)
 
         def spread(x):
             return x.rearrange("p (c i) t -> p c t i", i=4)
@@ -103,217 +88,98 @@ def tile_ia3scaledqknormkeybackwardtoinput_x1_kernel(tc, ds, q, u, gamma, l, wk,
         def gather(x):
             return x.rearrange("p t (c i) -> p c t i", i=4)
 
-        ssq = [keep.tile([P, w], F32, name="ssq%d" % c) for c, (a, w) in enumerate(GROUPS)]
-        zz = [keep.tile([P, w], F32, name="zz%d" % c) for c, (a, w) in enumerate(GROUPS)]
-        ir = [keep.tile([P, w], F32, name="ir%d" % c) for c, (a, w) in enumerate(GROUPS)]
-        k2 = [keep.tile([P, w], F32, name="k2%d" % c) for c, (a, w) in enumerate(GROUPS)]
+        ssq = [keep.tile([P, w], F32, name="ssq%d" % c) for c, (a, w) in enumerate(STAT_GROUPS)]
+        root = [keep.tile([P, w], F32, name="root%d" % c) for c, (a, w) in enumerate(STAT_GROUPS)]
+        rinv = [keep.tile([P, w], F32, name="rinv%d" % c) for c, (a, w) in enumerate(STAT_GROUPS)]
+        nrr = [keep.tile([P, w], F32, name="nrr%d" % c) for c, (a, w) in enumerate(STAT_GROUPS)]
+        group_of = [c for c, (a, w) in enumerate(STAT_GROUPS) for i in range(w)]
 
         def column(x, i):
-            c = [n for n, (a, w) in enumerate(GROUPS) if a <= i < a + w][0]
-            return x[c][:, i - GROUPS[c][0] : i - GROUPS[c][0] + 1]
+            j = i - STAT_GROUPS[group_of[i]][0]
+            return x[group_of[i]][:, j : j + 1]
 
-        def u_square(i):
-            c, h = divmod(i, 2)
+        def u_rows(i):
+            return u_raw[i // 2][:, i % 2, :]
+
+        def square(i):
             sq = work.tile([P, D], BF16, name="sq")
-            nc.scalar.activation(sq[:], u_raw[c][:, h, :], ACT.Square, accum_out=column(ssq, i))
+            nc.scalar.activation(sq[:], u_rows(i), ACT.Square, accum_out=column(ssq, i))
 
-        def u_stats(c):
-            nc.scalar.activation(zz[c][:], ssq[c][:], ACT.Sqrt, bias=eps[:])
-            nc.vector.reciprocal(ir[c][:], zz[c][:])
-            nc.vector.scalar_tensor_tensor(k2[c][:], ir[c][:], -1.0, ir[c][:], ALU.mult, ALU.mult)
+        def take_root(c):
+            nc.scalar.activation(root[c][:], ssq[c][:], ACT.Sqrt, bias=D * EPS)
+
+        def invert(c):
+            nc.vector.reciprocal(rinv[c][:], root[c][:])
+
+        def minus_square(c):
+            nc.vector.scalar_tensor_tensor(nrr[c][:], rinv[c][:], -1.0, rinv[c][:], ALU.mult, ALU.mult)
 
         qg = [keep.tile([P, D, 4], BF16, name="qg%d" % g, align_bytes=64) for g in range(2)]
         qc = keep.tile([P, 2, D], U32, name="qc", align_bytes=64)
         qs = keep.tile([P, 2, D], U8, name="qs", align_bytes=64)
-        for g in range(2):
-            nc.vector.tensor_copy(out=spread(qg[g][:, 0:Q_DVE, :]), in_=gather(q_raw[g][:, :, 0:Q_DVE]))
-            nc.scalar.copy(spread(qg[g][:, Q_DVE:D, :]), gather(q_raw[g][:, :, Q_DVE:D]))
-        for g in range(2):
+
+        def q_interleave(g):
+            nc.vector.tensor_copy(out=spread(qg[g][:, 0:Q_VECTOR, :]), in_=gather(q_raw[g][:, :, 0:Q_VECTOR]))
+            nc.scalar.copy(spread(qg[g][:, Q_VECTOR:D, :]), gather(q_raw[g][:, :, Q_VECTOR:D]))
+
+        def q_quantize(g):
             nc.vector.quantize_mx(
                 out=qc[:, g, :].bitcast(X4), scales=qs[:, g, :], in_=qg[g][:].rearrange("p c t -> p (c t)")
             )
 
-        dsc = [keep.tile([P, 2, UNIT], U32, name="dsc%d" % k, align_bytes=64) for k in range(M // UNIT)]
-        dss = [keep.tile([P, 2, UNIT], U8, name="dss%d" % k, align_bytes=64) for k in range(M // UNIT)]
-        grouped = {}
+        dsg, dsc, dss = {}, {}, {}
 
-        def ds_interleave(k):
-            c = [i for i, (a, w) in enumerate(CHUNKS) if a <= k * UNIT < a + w][0]
-            off = k * UNIT - CHUNKS[c][0]
-            g0 = work.tile([P, UNIT, 4], BF16, bufs=4, name="g0", align_bytes=64)
-            g1 = work.tile([P, UNIT, 4], BF16, bufs=4, name="g1", align_bytes=64)
-            for g, t in ((0, g0), (1, g1)):
-                src = gather(ds_raw[c][:, g, :, off : off + UNIT])
-                eng = ILV.get((k, g), ILV[g])
-                if eng == "v":
-                    nc.vector.tensor_copy(out=spread(t[:]), in_=src)
-                elif eng == "a":
-                    nc.scalar.copy(spread(t[:]), src)
-                else:
-                    nc.gpsimd.tensor_scalar(spread(t[:]), src, 1.0, 1.0, ALU.mult, ALU.mult)
-            grouped[k] = (g0, g1)
+        def ds_interleave(i, copy, passes=slice(0, 2)):
+            c = [n for n, (a, w) in enumerate(DS_CHUNKS) if a <= i * P < a + w][0]
+            off = i * P - DS_CHUNKS[c][0]
+            if passes.start == 0:
+                dsg[i] = work.tile([P, 2, P, 4], BF16, name="dsg", align_bytes=64)
+            copy(
+                dsg[i][:, passes, :, :].rearrange("p g (c i) t -> p g c t i", i=4),
+                ds_raw[c][:, passes, :, off : off + P].rearrange("p g t (c i) -> p g c t i", i=4),
+            )
 
-        def ds_quantize(k):
-            for g in range(2):
-                nc.vector.quantize_mx(
-                    out=dsc[k][:, g, :].bitcast(X4),
-                    scales=dss[k][:, g, :],
-                    in_=grouped[k][g][:].rearrange("p c t -> p (c t)"),
-                )
+        def ds_quantize(i):
+            dsc[i] = work.tile([P, 2, P], U32, name="dsc", align_bytes=64)
+            dss[i] = work.tile([P, 2, P], U8, name="dss", align_bytes=64)
+            nc.vector.quantize_mx(
+                out=dsc[i][:].rearrange("p g c -> p (g c)").bitcast(X4),
+                scales=dss[i][:].rearrange("p g c -> p (g c)"),
+                in_=dsg[i][:].rearrange("p g c t -> p (g c t)"),
+            )
 
-        dk, gr, cu, coef, tr, dzg, dzc, dzs = {}, {}, {}, {}, {}, {}, {}, {}
-        gam = keep.tile([P, D], F32, name="gam")
+        gam = keep.tile([P, 4, P], F32, name="gam")
+
+        def spread_gamma():
+            bank = psum.tile([P, 2, P], F32, name="tr")
+            words = g_col[:].bitcast(F32)
+            for w in range(2):
+                nc.tensor.transpose(bank[:, w, :], words[:, w : w + 1].to_broadcast([P, P]), ident[:])
+            nc.scalar.copy(
+                gam[:].rearrange("x (w e) p -> x w e p", e=2),
+                bank[:].bitcast(BF16).rearrange("x w (p e) -> x w e p", e=2),
+            )
+
+        wg = keep.tile([P, E, 4], BF16, name="wg", align_bytes=64)
         wkc = keep.tile([P, E], U32, name="wkc", align_bytes=64)
         wks = keep.tile([P, E], U8, name="wks", align_bytes=64)
-        pls = keep.tile([P, 2, M], U8, name="pls", align_bytes=64)
 
-        def mx1(i):
-            k, h = divmod(i, 2)
-            bank = ps_dk.tile([P, D], F32, name="dk")
-            for g in range(2):
-                nc.tensor.matmul_mx(
-                    out=bank[:],
-                    lhsT=dsc[k][:, g, h * P : (h + 1) * P].bitcast(X4),
-                    lhsT_scale=dss[k][:, g, h * P : (h + 1) * P],
-                    rhs=qc[:, g, :].bitcast(X4),
-                    rhs_scale=qs[:, g, :],
-                    start=(g == 0),
-                    stop=(g == 1),
-                )
-            dk[i] = bank
+        wb = {}
 
-        def p2(i):
-            t = work.tile([P, D], F32, bufs=6, name="gr")
-            nc.vector.scalar_tensor_tensor(t[:], dk[i][:], column(ir, i), gam[:], ALU.mult, ALU.mult)
-            gr[i] = t
+        def wk_turn(g):
+            words = wk_raw[g][:].bitcast(F32)
+            for b, tag in enumerate(("ob", "pb")):
+                bank = psum.tile([P, 2, 2, P], F32, bufs=2 + b, name=tag)
+                for a in range(2):
+                    base = (2 * b + a) * 256
+                    for w in range(2):
+                        nc.tensor.transpose(bank[:, a, w, :], words[:, base + w : base + 256 : 2], ident[:])
+                wb[g, b] = bank
 
-        def p1(i):
-            c, h = divmod(i, 2)
-            junk = work.tile([P, D], BF16, bufs=3, name="junk")
-            ncoef = work.tile([P, 1], F32, bufs=6, name="ncoef")
-            nc.vector.scalar_tensor_tensor(
-                junk[:], gr[i][:], column(k2, i), u_raw[c][:, h, :], ALU.mult, ALU.mult, accum_out=ncoef[:]
-            )
-            coef[i] = ncoef
-
-        def cu_make(i):
-            c, h = divmod(i, 2)
-            t = work.tile([P, 4, P], F32, bufs=CUB, name="cu")
-            src = u_raw[c][:, h, :].rearrange("m (p t) -> m t p", t=4)
-            nc.scalar.activation(t[:], src, ACT.Copy, scale=coef[i][:])
-            cu[i] = t
-
-        def transposes(i):
-            bank = ps_tr.tile([P, 4, P], F32, name="tr")
-            for t in range(4):
-                nc.tensor.matmul(bank[:, t, :], gr[i][:, t:D:4], ident[:], start=True, stop=False, is_transpose=True)
-                nc.tensor.matmul(bank[:, t, :], cu[i][:, t, :], ident[:], start=False, stop=True, is_transpose=True)
-            tr[i] = bank
-
-        def times_l(i):
-            t = work.tile([P, P, 4], BF16, bufs=5, name="dzg", align_bytes=64)
-            nc.vector.tensor_tensor(
-                t[:],
-                tr[i][:].rearrange("p t m -> p m t"),
-                l_col[:].unsqueeze(1).to_broadcast([P, P, 4]),
-                ALU.mult,
-            )
-            dzg[i] = t
-
-        def quantize_dz(i):
-            c = work.tile([P, P], U32, bufs=6, name="dzc", align_bytes=64)
-            s = work.tile([P, P], U8, bufs=6, name="dzs", align_bytes=64)
-            nc.vector.quantize_mx(out=c[:].bitcast(X4), scales=s[:], in_=dzg[i][:].rearrange("p m t -> p (m t)"))
-            dzc[i], dzs[i] = c, s
-
-        ob_banks, p_sb, p_codes = {}, {}, {}
-
-        def mx2(i):
-            banks = []
-            for g in range(2):
-                pl = ps_out.tile([P, 4, P], F32, name="ob")
-                for t in range(4):
-                    cols = slice(g * 512 + t * P, g * 512 + (t + 1) * P)
-                    nc.tensor.matmul_mx(
-                        out=pl[:, t, :],
-                        lhsT=wkc[:, cols].bitcast(X4),
-                        lhsT_scale=wks[:, cols],
-                        rhs=dzc[i][:].bitcast(X4),
-                        rhs_scale=dzs[i][:],
-                        start=True,
-                        stop=True,
-                    )
-                ob = ps_out.tile([P, 4, P], F32, name="ob")
-                cols = slice(g * 512, (g + 1) * 512)
-                nc.tensor.matmul_mx(
-                    out=ob[:].rearrange("p t m -> p (t m)"),
-                    lhsT=dzc[i][:].bitcast(X4),
-                    lhsT_scale=dzs[i][:],
-                    rhs=wkc[:, cols].bitcast(X4),
-                    rhs_scale=wks[:, cols],
-                    start=True,
-                    stop=True,
-                )
-                banks.append((pl, ob))
-            ob_banks[i] = banks
-
-        def evacuate(i):
-            banks = ob_banks[i]
-            o = work.tile([P, 2, P, 4], F32, name="o")
-            p = work.tile([P, 2, P, 4], BF16, bufs=5, name="p", align_bytes=64)
-            for g in range(2):
-                pl, ob = banks[g]
-                if i in DVE_PLANES:
-                    nc.vector.tensor_copy(out=p[:, g, :, :], in_=pl[:].rearrange("p t m -> p m t"))
-                else:
-                    nc.scalar.copy(p[:, g, :, :], pl[:].rearrange("p t m -> p m t"))
-                nc.scalar.copy(o[:, g, :, :], ob[:].rearrange("m t p -> m p t"))
-            nc.sync.dma_start(out=out_0[i * P : (i + 1) * P, :], in_=o[:].rearrange("m g p t -> m (g p t)"))
-            p_sb[i] = p
-
-        def quantize_planes(i):
-            c, h = divmod(i, 2)
-            if h == 0:
-                p_codes[c] = work.tile([P, 2, 2 * P], U32, name="pc", align_bytes=64)
-            for g in range(2):
-                nc.vector.quantize_mx(
-                    out=p_codes[c][:, g, h * P : (h + 1) * P].bitcast(X4),
-                    scales=pls[:, g, i * P : (i + 1) * P],
-                    in_=p_sb[i][:, g, :, :].rearrange("p m t -> p (m t)"),
-                )
-            if h == 1:
-                nc.sync.dma_start(
-                    out=out_1[:, :, 256 * c : 256 * (c + 1), :].rearrange("g p m t -> p g (m t)").bitcast(I32),
-                    in_=p_codes[c][:].bitcast(I32),
-                )
-            if i % 8 == 7:
-                cols = slice((i - 7) * P, (i + 1) * P)
-                for quad in range(4):
-                    nc.sync.dma_start(
-                        out=out_2[:, 4 * quad : 4 * quad + 4, cols].rearrange("g r m -> r g m").bitcast(I32),
-                        in_=pls[32 * quad : 32 * quad + 4, :, cols].bitcast(I32),
-                    )
-
-        words = wk_raw[:].rearrange("p g t d -> p (g t d)").bitcast(F32)
-        wg = keep.tile([P, E, 4], BF16, name="wg", align_bytes=64)
-        wbanks = []
-
-        def wk_transposes():
-            for b in range(4):
-                bank = ps_out.tile([P, 4, P], F32, name="ob")
-                for s in range(4):
-                    base = (2 * b + s // 2) * 256
-                    nc.tensor.transpose(bank[:, s, :], words[:, base + s % 2 : base + 256 : 2], ident[:])
-                wbanks.append(bank)
-
-        def wk_copy(b, copy):
-            dst = (
-                wg[:, 256 * b : 256 * (b + 1), :]
-                .rearrange("p c k -> p (c k)")
-                .bitcast(F32)
-                .rearrange("p (a c w) -> p a c w", a=2, w=2)
-            )
-            copy(dst, wbanks[b][:].rearrange("p (a w) c -> p a c w", a=2))
+        def wk_out(g, b):
+            cols = slice(512 * g + 256 * b, 512 * g + 256 * (b + 1))
+            dst = wg[:, cols, :].rearrange("p c k -> p (c k)").bitcast(F32)
+            nc.scalar.copy(dst.rearrange("p (a c w) -> p a c w", a=2, w=2), wb[g, b][:].rearrange("p a w c -> p a c w"))
 
         def wk_quantize(g):
             cols = slice(512 * g, 512 * (g + 1))
@@ -321,47 +187,249 @@ def tile_ia3scaledqknormkeybackwardtoinput_x1_kernel(tc, ds, q, u, gamma, l, wk,
                 out=wkc[:, cols].bitcast(X4), scales=wks[:, cols], in_=wg[:, cols, :].rearrange("p c k -> p (c k)")
             )
 
-        ds_interleave(0)
-        gbank = ps_tr.tile([P, 4, P], F32, name="tr")
-        nc.tensor.matmul(gbank[:].rearrange("p t m -> p (t m)"), ones[:], g_row[:], start=True, stop=True)
-        nc.scalar.copy(gam[:], gbank[:].rearrange("p t m -> p (t m)"))
-        u_square(0)
-        u_square(1)
+        dk, gr, cu, coef, tr, dzg, ob, rows, pb, pg, pc = {}, {}, {}, {}, {}, {}, {}, {}, {}, {}, {}
+        dzc = [keep.tile([P, P], U32, name="dzc%d" % i, align_bytes=64) for i in range(TILES)]
+        dzs = [keep.tile([P, P], U8, name="dzs%d" % i, align_bytes=64) for i in range(TILES)]
+        filled = []
+        pls = keep.tile([P, 2, M], U8, name="pls", align_bytes=64)
+
+        def first_product(i):
+            dk[i] = psum.tile([P, D], F32, bufs=1, name="dk")
+            for g in range(2):
+                nc.tensor.matmul_mx(
+                    out=dk[i][:],
+                    lhsT=dsc[i][:, g, :].bitcast(X4),
+                    lhsT_scale=dss[i][:, g, :],
+                    rhs=qc[:, g, :].bitcast(X4),
+                    rhs_scale=qs[:, g, :],
+                    start=(g == 0),
+                    stop=(g == 1),
+                )
+
+        def scale_dk(i):
+            gr[i] = work.tile([P, 4, P], F32, name="gr")
+            nc.vector.scalar_tensor_tensor(
+                gr[i][:], dk[i][:].rearrange("m (p t) -> m t p", t=4), column(rinv, i), gam[:], ALU.mult, ALU.mult
+            )
+
+        def reduce_rows(i):
+            prod = work.tile([P, 4, P], BF16, name="prod")
+            coef[i] = work.tile([P, 1], F32, name="coef")
+            nc.vector.scalar_tensor_tensor(
+                prod[:],
+                gr[i][:],
+                column(nrr, i),
+                u_rows(i).rearrange("m (p t) -> m t p", t=4),
+                ALU.mult,
+                ALU.mult,
+                accum_out=coef[i][:],
+            )
+
+        def scale_u(i):
+            cu[i] = work.tile([P, 4, P], F32, name="cu")
+            nc.scalar.activation(cu[i][:], u_rows(i).rearrange("m (p t) -> m t p", t=4), ACT.Copy, scale=coef[i][:])
+
+        def turn(i):
+            tr[i] = psum.tile([P, 4, P], F32, name="tr")
+            for t in range(4):
+                nc.tensor.matmul(tr[i][:, t, :], gr[i][:, t, :], ident[:], start=True, stop=False, is_transpose=True)
+                nc.tensor.matmul(tr[i][:, t, :], cu[i][:, t, :], ident[:], start=False, stop=True, is_transpose=True)
+
+        def times_l(i):
+            dzg[i] = work.tile([P, P, 4], BF16, name="dzg", align_bytes=64)
+            nc.vector.tensor_tensor(
+                dzg[i][:],
+                tr[i][:].rearrange("p t m -> p m t"),
+                l_col[:].unsqueeze(1).to_broadcast([P, P, 4]),
+                ALU.mult,
+            )
+
+        def dz_quantize(i):
+            nc.vector.quantize_mx(
+                out=dzc[i][:].bitcast(X4), scales=dzs[i][:], in_=dzg[i][:].rearrange("p m t -> p (m t)")
+            )
+
+        def rows_product(i):
+            for g in range(2):
+                cols = slice(g * 512, (g + 1) * 512)
+                ob[i, g] = psum.tile([P, 4, P], F32, name="ob")
+                nc.tensor.matmul_mx(
+                    out=ob[i, g][:].rearrange("m t p -> m (t p)"),
+                    lhsT=dzc[i][:].bitcast(X4),
+                    lhsT_scale=dzs[i][:],
+                    rhs=wkc[:, cols].bitcast(X4),
+                    rhs_scale=wks[:, cols],
+                    start=True,
+                    stop=True,
+                )
+
+        def rows_out(i, g, copy):
+            if g == 0:
+                rows[i] = work.tile([P, 2, P, 4], F32, bufs=4, name="rows")
+            copy(rows[i][:, g, :, :], ob[i, g][:].rearrange("m t p -> m p t"))
+            if g == 1:
+                nc.sync.dma_start(out=out_0[i * P : (i + 1) * P, :], in_=rows[i][:].rearrange("m g p t -> m (g p t)"))
+
+        def planes_product(j):
+            i, g = divmod(j, 2)
+            pb[j] = psum.tile([P, 4, P], F32, bufs=3, name="pb")
+            for t in range(4):
+                cols = slice(g * 512 + t * P, g * 512 + (t + 1) * P)
+                nc.tensor.matmul_mx(
+                    out=pb[j][:, t, :],
+                    lhsT=wkc[:, cols].bitcast(X4),
+                    lhsT_scale=wks[:, cols],
+                    rhs=dzc[i][:].bitcast(X4),
+                    rhs_scale=dzs[i][:],
+                    start=True,
+                    stop=True,
+                )
+
+        def planes_out(j, copy):
+            i, g = divmod(j, 2)
+            k, h = divmod(i, 2)
+            if h == 0:
+                pg[k, g] = work.tile([P, UNIT, 4], BF16, bufs=4, name="pg", align_bytes=64)
+            copy(pg[k, g][:, h * P : (h + 1) * P, :], pb[j][:].rearrange("p t m -> p m t"))
+            if h == 1:
+                filled.append((k, g))
+
+        def planes_quantize(k, g):
+            if g == 0:
+                pc[k] = work.tile([P, 2, UNIT], U32, name="pc", align_bytes=64)
+            nc.vector.quantize_mx(
+                out=pc[k][:, g, :].bitcast(X4),
+                scales=pls[:, g, k * UNIT : (k + 1) * UNIT],
+                in_=pg[k, g][:].rearrange("p m t -> p (m t)"),
+            )
+            if g == 1:
+                nc.sync.dma_start(
+                    out=out_1[:, :, UNIT * k : UNIT * (k + 1), :].rearrange("g p m t -> p g (m t)").bitcast(I32),
+                    in_=pc[k][:].bitcast(I32),
+                )
+            if g == 1 and k % 4 == 3:
+                cols = slice((k - 3) * UNIT, (k + 1) * UNIT)
+                for quad in range(4):
+                    nc.sync.dma_start(
+                        out=out_2[:, 4 * quad : 4 * quad + 4, cols].rearrange("g r m -> r g m").bitcast(I32),
+                        in_=pls[32 * quad : 32 * quad + 4, :, cols].bitcast(I32),
+                    )
+
+        on_vector, on_scalar = nc.vector.tensor_copy, nc.scalar.copy
+
+        def quantize_filled(upto):
+            for k, g in filled[:upto]:
+                planes_quantize(k, g)
+            filled[:upto] = []
+
+        q_interleave(0)
+        spread_gamma()
+        q_interleave(1)
+        q_quantize(0)
+        square(0)
+        square(1)
+        q_quantize(1)
+        ds_interleave(0, on_vector, slice(0, 1))
+        take_root(0)
+        ds_interleave(0, on_vector, slice(1, 2))
+        invert(0)
         ds_quantize(0)
-        u_stats(0)
-        mx1(0)
-        mx1(1)
-        wk_transposes()
+        minus_square(0)
+        ds_interleave(1, on_scalar)
+        first_product(0)
+        scale_dk(0)
+        ds_quantize(1)
+        wk_turn(0)
+        first_product(1)
+        wk_out(0, 0)
+        wk_out(0, 1)
+        reduce_rows(0)
+        scale_u(0)
+        wk_turn(1)
+        turn(0)
+        scale_dk(1)
+        wk_quantize(0)
+        wk_out(1, 0)
+        wk_out(1, 1)
+        reduce_rows(1)
+        ds_interleave(2, on_vector)
+        scale_u(1)
+        square(2)
+        times_l(0)
+        ds_quantize(2)
+        first_product(2)
+        turn(1)
+        square(3)
+        wk_quantize(1)
+        take_root(1)
+        dz_quantize(0)
+        ds_interleave(3, on_vector)
+        invert(1)
+        ds_quantize(3)
+        minus_square(1)
 
+        squares = {2: [4, 5], 3: [6, 7], 4: [8, 9]}
+        for s in range(5, 11):
+            squares[s] = [s + 5]
+        last_square = {sum(STAT_GROUPS[c]) - 1: c for c in range(len(STAT_GROUPS))}
+        half = 0
+        for s in range(2, TILES):
+            count = 0 if s < 5 else 2 if s in squares else 3
+            halves = list(range(half, half + count))
+            half += count
+            fresh = [last_square[i] for i in squares.get(s - 1, []) if i in last_square]
+            ready = len(filled)
+            rows_product(s - 2)
+            scale_dk(s)
+            for j in halves:
+                planes_product(j)
+            if s + 1 < TILES:
+                first_product(s + 1)
+            if s + 2 < TILES:
+                ds_interleave(s + 2, on_vector)
+            else:
+                times_l(s - 1)
+            rows_out(s - 2, 0, on_scalar)
+            for c in fresh:
+                take_root(c)
+            rows_out(s - 2, 1, on_scalar)
+            reduce_rows(s)
+            scale_u(s)
+            turn(s)
+            if s + 2 < TILES:
+                times_l(s - 1)
+                for c in fresh:
+                    invert(c)
+                ds_quantize(s + 2)
+                for c in fresh:
+                    minus_square(c)
+            else:
+                planes_out(halves.pop(0), on_vector)
+            quantize_filled(ready)
+            dz_quantize(s - 1)
+            for j in halves:
+                planes_out(j, on_scalar)
+            for i in squares.get(s, []):
+                square(i)
 
-        LAG = {'p2': 0, 'tr': 1, 'mx1': -1, 'evl': 1, 'p1': 0, 'cu': 0, 'mx2': 2, 'ev': 2, 'qpl': 3, 'qdz': 1}
-        ORDER = ['p2', 'ds', 'tr', 'mx1', 'wk', 'p1', 'evl', 'qpl', 'sq', 'mx2', 'qdz', 'cu', 'dsq', 'ev']
-        FN = dict(p2=p2, tr=transposes, mx1=mx1, evl=times_l, p1=p1, cu=cu_make, mx2=mx2, ev=evacuate, qpl=quantize_planes, qdz=quantize_dz)
-        for s in range(0, TILES + LAG["qpl"]):
-            for name in ORDER:
-                if name in LAG:
-                    i = s - LAG[name]
-                    if 0 <= i < TILES and not (name == "mx1" and i < 2):
-                        FN[name](i)
-                elif name == "wk":
-                    if s == WK0:
-                        wk_copy(0, nc.vector.tensor_copy)
-                        wk_copy(1, nc.scalar.copy)
-                    if s == WK0 + 1:
-                        wk_copy(2, nc.vector.tensor_copy)
-                        wk_copy(3, nc.scalar.copy)
-                        wk_quantize(0)
-                    if s == WK0 + 2:
-                        wk_quantize(1)
-                elif name == "ds":
-                    for unit in DSI.get(s, []):
-                        ds_interleave(unit)
-                elif name == "dsq":
-                    unit = (s + DSL) // 2
-                    if 1 <= unit < M // UNIT and (s + DSL) % 2 == 1:
-                        ds_quantize(unit)
-                elif name == "sq":
-                    for i in SQ.get(s, []):
-                        u_square(i)
-                    if s in ST:
-                        u_stats(ST[s])
+        last = TILES - 1
+        rows_product(last - 1)
+        for j in range(half, half + 3):
+            planes_product(j)
+        quantize_filled(2)
+        times_l(last)
+        rows_out(last - 1, 0, on_scalar)
+        planes_out(half, on_vector)
+        dz_quantize(last)
+        rows_out(last - 1, 1, on_scalar)
+        planes_out(half + 1, on_vector)
+        planes_out(half + 2, on_scalar)
+        quantize_filled(2)
+        rows_product(last)
+        planes_product(half + 3)
+        planes_product(half + 4)
+        rows_out(last, 0, on_scalar)
+        rows_out(last, 1, on_vector)
+        planes_out(half + 3, on_scalar)
+        planes_out(half + 4, on_vector)
+        quantize_filled(2)

@@ -22,7 +22,11 @@ UNIT = 2 * P
 UNITS = M // UNIT
 DS_CHUNKS = [(0, 256), (256, 256), (512, 512), (1024, 1024)]
 STAT_GROUPS = [(0, 2), (2, 2), (4, 2), (6, 2), (8, 4), (12, 4)]
-Q_VECTOR = 384
+Q_VECTOR = 96
+DS_VECTOR = 208
+DS_GROUPS = [(0, 1), (1, 1)] + [(a, 2) for a in range(2, TILES, 2)]
+SCALE_STORES = {2: 0, 4: 12}
+PLANE_GROUPS = [(0, 4), (4, 4), (8, 4), (12, 2), (14, 2)]
 
 
 def tile_ia3scaledqknormkeybackwardtoinput_x1_kernel(tc, ds, q, u, gamma, l, wk, out_0, out_1, out_2):
@@ -78,15 +82,11 @@ def tile_ia3scaledqknormkeybackwardtoinput_x1_kernel(tc, ds, q, u, gamma, l, wk,
         load_ds(2)
         load_u(2)
         load_u(3)
+        load_u(4)
+        load_u(5)
         load_ds(3)
-        for c in range(4, UNITS):
-            load_u(c)
-
-        def spread(x):
-            return x.rearrange("p (c i) t -> p c t i", i=4)
-
-        def gather(x):
-            return x.rearrange("p t (c i) -> p c t i", i=4)
+        load_u(6)
+        load_u(7)
 
         ssq = [keep.tile([P, w], F32, name="ssq%d" % c) for c, (a, w) in enumerate(STAT_GROUPS)]
         root = [keep.tile([P, w], F32, name="root%d" % c) for c, (a, w) in enumerate(STAT_GROUPS)]
@@ -119,8 +119,10 @@ def tile_ia3scaledqknormkeybackwardtoinput_x1_kernel(tc, ds, q, u, gamma, l, wk,
         qs = keep.tile([P, 2, D], U8, name="qs", align_bytes=64)
 
         def q_interleave(g):
-            nc.vector.tensor_copy(out=spread(qg[g][:, 0:Q_VECTOR, :]), in_=gather(q_raw[g][:, :, 0:Q_VECTOR]))
-            nc.scalar.copy(spread(qg[g][:, Q_VECTOR:D, :]), gather(q_raw[g][:, :, Q_VECTOR:D]))
+            dst = qg[g][:].rearrange("p (t c) j -> p t c j", t=4)
+            src = q_raw[g][:].rearrange("p j (c t) -> p t c j", t=4)
+            nc.vector.tensor_copy(out=dst[:, :, 0:Q_VECTOR, :], in_=src[:, :, 0:Q_VECTOR, :])
+            nc.scalar.copy(dst[:, :, Q_VECTOR:P, :], src[:, :, Q_VECTOR:P, :])
 
         def q_quantize(g):
             nc.vector.quantize_mx(
@@ -129,23 +131,28 @@ def tile_ia3scaledqknormkeybackwardtoinput_x1_kernel(tc, ds, q, u, gamma, l, wk,
 
         dsg, dsc, dss = {}, {}, {}
 
-        def ds_interleave(i, copy, passes=slice(0, 2)):
-            c = [n for n, (a, w) in enumerate(DS_CHUNKS) if a <= i * P < a + w][0]
-            off = i * P - DS_CHUNKS[c][0]
-            if passes.start == 0:
-                dsg[i] = work.tile([P, 2, P, 4], BF16, name="dsg", align_bytes=64)
+        ds_group_of = [k for k, (a, w) in enumerate(DS_GROUPS) for i in range(w)]
+
+        def ds_interleave(k, copy, passes=slice(0, 2), part=None):
+            first, width = DS_GROUPS[k][0] * P, DS_GROUPS[k][1] * P
+            c = [n for n, (a, w) in enumerate(DS_CHUNKS) if a <= first < a + w][0]
+            off = first - DS_CHUNKS[c][0]
+            lo, hi = part or (0, width)
+            if k not in dsg:
+                dsg[k] = work.tile([P, 2, width, 4], BF16, name="dsg", align_bytes=64)
             copy(
-                dsg[i][:, passes, :, :].rearrange("p g (c i) t -> p g c t i", i=4),
-                ds_raw[c][:, passes, :, off : off + P].rearrange("p g t (c i) -> p g c t i", i=4),
+                dsg[k][:, passes, lo:hi, :].rearrange("p g (c i) t -> p g c t i", i=4),
+                ds_raw[c][:, passes, :, off + lo : off + hi].rearrange("p g t (c i) -> p g c t i", i=4),
             )
 
-        def ds_quantize(i):
-            dsc[i] = work.tile([P, 2, P], U32, name="dsc", align_bytes=64)
-            dss[i] = work.tile([P, 2, P], U8, name="dss", align_bytes=64)
+        def ds_quantize(k):
+            width = DS_GROUPS[k][1] * P
+            dsc[k] = work.tile([P, 2, width], U32, name="dsc", align_bytes=64)
+            dss[k] = work.tile([P, 2, width], U8, name="dss", align_bytes=64)
             nc.vector.quantize_mx(
-                out=dsc[i][:].rearrange("p g c -> p (g c)").bitcast(X4),
-                scales=dss[i][:].rearrange("p g c -> p (g c)"),
-                in_=dsg[i][:].rearrange("p g c t -> p (g c t)"),
+                out=dsc[k][:].rearrange("p g c -> p (g c)").bitcast(X4),
+                scales=dss[k][:].rearrange("p g c -> p (g c)"),
+                in_=dsg[k][:].rearrange("p g c t -> p (g c t)"),
             )
 
         gam = keep.tile([P, 4, P], F32, name="gam")
@@ -187,19 +194,21 @@ def tile_ia3scaledqknormkeybackwardtoinput_x1_kernel(tc, ds, q, u, gamma, l, wk,
                 out=wkc[:, cols].bitcast(X4), scales=wks[:, cols], in_=wg[:, cols, :].rearrange("p c k -> p (c k)")
             )
 
-        dk, gr, cu, coef, tr, dzg, ob, rows, pb, pg, pc = {}, {}, {}, {}, {}, {}, {}, {}, {}, {}, {}
+        dk, gr, cu, coef, tr, dzg, ob, rows, pb, pg = {}, {}, {}, {}, {}, {}, {}, {}, {}, {}
         dzc = [keep.tile([P, P], U32, name="dzc%d" % i, align_bytes=64) for i in range(TILES)]
         dzs = [keep.tile([P, P], U8, name="dzs%d" % i, align_bytes=64) for i in range(TILES)]
         filled = []
         pls = keep.tile([P, 2, M], U8, name="pls", align_bytes=64)
 
         def first_product(i):
+            k = ds_group_of[i]
+            cols = slice((i - DS_GROUPS[k][0]) * P, (i - DS_GROUPS[k][0] + 1) * P)
             dk[i] = psum.tile([P, D], F32, bufs=1, name="dk")
             for g in range(2):
                 nc.tensor.matmul_mx(
                     out=dk[i][:],
-                    lhsT=dsc[i][:, g, :].bitcast(X4),
-                    lhsT_scale=dss[i][:, g, :],
+                    lhsT=dsc[k][:, g, cols].bitcast(X4),
+                    lhsT_scale=dss[k][:, g, cols],
                     rhs=qc[:, g, :].bitcast(X4),
                     rhs_scale=qs[:, g, :],
                     start=(g == 0),
@@ -209,7 +218,7 @@ def tile_ia3scaledqknormkeybackwardtoinput_x1_kernel(tc, ds, q, u, gamma, l, wk,
         def scale_dk(i):
             gr[i] = work.tile([P, 4, P], F32, name="gr")
             nc.vector.scalar_tensor_tensor(
-                gr[i][:], dk[i][:].rearrange("m (p t) -> m t p", t=4), column(rinv, i), gam[:], ALU.mult, ALU.mult
+                gr[i][:], dk[i][:].rearrange("m (t p) -> m t p", t=4), column(rinv, i), gam[:], ALU.mult, ALU.mult
             )
 
         def reduce_rows(i):
@@ -225,9 +234,10 @@ def tile_ia3scaledqknormkeybackwardtoinput_x1_kernel(tc, ds, q, u, gamma, l, wk,
                 accum_out=coef[i][:],
             )
 
-        def scale_u(i):
+        def scale_u(i, engine):
             cu[i] = work.tile([P, 4, P], F32, name="cu")
-            nc.scalar.activation(cu[i][:], u_rows(i).rearrange("m (p t) -> m t p", t=4), ACT.Copy, scale=coef[i][:])
+            src = u_rows(i).rearrange("m (p t) -> m t p", t=4)
+            engine.tensor_scalar(cu[i][:], src, coef[i][:], 1.0, ALU.mult, ALU.mult)
 
         def turn(i):
             tr[i] = psum.tile([P, 4, P], F32, name="tr")
@@ -285,30 +295,30 @@ def tile_ia3scaledqknormkeybackwardtoinput_x1_kernel(tc, ds, q, u, gamma, l, wk,
                     stop=True,
                 )
 
+        plane_group_of = [k for k, (a, w) in enumerate(PLANE_GROUPS) for i in range(w)]
+
         def planes_out(j, copy):
             i, g = divmod(j, 2)
-            k, h = divmod(i, 2)
-            if h == 0:
-                pg[k, g] = work.tile([P, UNIT, 4], BF16, bufs=4, name="pg", align_bytes=64)
-            copy(pg[k, g][:, h * P : (h + 1) * P, :], pb[j][:].rearrange("p t m -> p m t"))
-            if h == 1:
+            k = plane_group_of[i]
+            a, w = PLANE_GROUPS[k]
+            if i == a:
+                pg[k, g] = work.tile([P, w * P, 4], BF16, bufs=6, name="pg", align_bytes=64)
+            copy(pg[k, g][:, (i - a) * P : (i - a + 1) * P, :], pb[j][:].rearrange("p t m -> p m t"))
+            if i == a + w - 1:
                 filled.append((k, g))
 
         def planes_quantize(k, g):
-            if g == 0:
-                pc[k] = work.tile([P, 2, UNIT], U32, name="pc", align_bytes=64)
+            a, w = PLANE_GROUPS[k]
+            cols = slice(a * P, (a + w) * P)
+            codes = work.tile([P, w * P], U32, bufs=4, name="pc", align_bytes=64)
             nc.vector.quantize_mx(
-                out=pc[k][:, g, :].bitcast(X4),
-                scales=pls[:, g, k * UNIT : (k + 1) * UNIT],
-                in_=pg[k, g][:].rearrange("p m t -> p (m t)"),
+                out=codes[:].bitcast(X4), scales=pls[:, g, cols], in_=pg[k, g][:].rearrange("p m t -> p (m t)")
             )
-            if g == 1:
-                nc.sync.dma_start(
-                    out=out_1[:, :, UNIT * k : UNIT * (k + 1), :].rearrange("g p m t -> p g (m t)").bitcast(I32),
-                    in_=pc[k][:].bitcast(I32),
-                )
-            if g == 1 and k % 4 == 3:
-                cols = slice((k - 3) * UNIT, (k + 1) * UNIT)
+            nc.sync.dma_start(
+                out=out_1[g, :, cols, :].rearrange("p m t -> p (m t)").bitcast(I32), in_=codes[:].bitcast(I32)
+            )
+            if g == 1 and k in SCALE_STORES:
+                cols = slice(SCALE_STORES[k] * P, (a + w) * P)
                 for quad in range(4):
                     nc.sync.dma_start(
                         out=out_2[:, 4 * quad : 4 * quad + 4, cols].rearrange("g r m -> r g m").bitcast(I32),
@@ -344,92 +354,100 @@ def tile_ia3scaledqknormkeybackwardtoinput_x1_kernel(tc, ds, q, u, gamma, l, wk,
         wk_out(0, 0)
         wk_out(0, 1)
         reduce_rows(0)
-        scale_u(0)
+        scale_u(0, nc.gpsimd)
+        scale_dk(1)
         wk_turn(1)
         turn(0)
-        scale_dk(1)
-        wk_quantize(0)
         wk_out(1, 0)
         wk_out(1, 1)
-        reduce_rows(1)
-        ds_interleave(2, on_vector)
-        scale_u(1)
+        wk_quantize(0)
+        ds_interleave(2, on_vector, part=(0, DS_VECTOR))
+        ds_interleave(2, on_scalar, part=(DS_VECTOR, UNIT))
         square(2)
+        square(3)
+        reduce_rows(1)
+        scale_u(1, nc.gpsimd)
         times_l(0)
+        take_root(1)
         ds_quantize(2)
         first_product(2)
         turn(1)
-        square(3)
-        wk_quantize(1)
-        take_root(1)
-        dz_quantize(0)
-        ds_interleave(3, on_vector)
         invert(1)
-        ds_quantize(3)
+        wk_quantize(1)
         minus_square(1)
+        dz_quantize(0)
+        scale_dk(2)
+        first_product(3)
+        rows_product(0)
+        ds_interleave(3, on_vector, part=(0, DS_VECTOR))
+        ds_interleave(3, on_scalar, part=(DS_VECTOR, UNIT))
+        square(4)
+        square(5)
+        rows_out(0, 0, on_scalar)
+        take_root(2)
+        rows_out(0, 1, on_scalar)
 
-        squares = {2: [4, 5], 3: [6, 7], 4: [8, 9]}
-        for s in range(5, 11):
-            squares[s] = [s + 5]
+        squares = {2: [6, 7, 8], 3: [9, 10, 11]}
+        for s in range(4, 8):
+            squares[s] = [s + 8]
         last_square = {sum(STAT_GROUPS[c]) - 1: c for c in range(len(STAT_GROUPS))}
+        last = TILES - 1
         half = 0
+        rooted = {a - 2: [c] for c, (a, w) in enumerate(STAT_GROUPS)}
+        ready = {}
         for s in range(2, TILES):
-            count = 0 if s < 5 else 2 if s in squares else 3
-            halves = list(range(half, half + count))
-            half += count
-            fresh = [last_square[i] for i in squares.get(s - 1, []) if i in last_square]
-            ready = len(filled)
-            rows_product(s - 2)
-            scale_dk(s)
+            count = 0 if s < 4 else 2 if s in squares else 3
+            halves = list(range(half, min(half + count, 2 * s)))
+            half += len(halves)
+            reduce_rows(s)
+            if s < last:
+                scale_u(s, nc.gpsimd)
+                times_l(s - 1)
+                scale_dk(s + 1)
+            else:
+                times_l(s - 1)
+                scale_u(s, nc.vector)
+            turn(s)
+            dz_quantize(s - 1)
+            for c in rooted.get(s, []):
+                invert(c)
+            if s % 2 == 0 and s + 2 < TILES:
+                ds_quantize(ds_group_of[s + 2])
+            for c in rooted.get(s, []):
+                minus_square(c)
+            if s % 2 == 1 and s + 3 < TILES:
+                ds_interleave(ds_group_of[s + 3], on_vector, part=(0, DS_VECTOR))
+                ds_interleave(ds_group_of[s + 3], on_scalar, part=(DS_VECTOR, UNIT))
+            if ready.get(s - 2, 0) > 0:
+                quantize_filled(1)
+                for earlier in ready:
+                    ready[earlier] -= 1
+            if s + 2 < TILES:
+                first_product(s + 2)
+            rows_product(s - 1)
             for j in halves:
                 planes_product(j)
-            if s + 1 < TILES:
-                first_product(s + 1)
-            if s + 2 < TILES:
-                ds_interleave(s + 2, on_vector)
-            else:
-                times_l(s - 1)
-            rows_out(s - 2, 0, on_scalar)
-            for c in fresh:
-                take_root(c)
-            rows_out(s - 2, 1, on_scalar)
-            reduce_rows(s)
-            scale_u(s)
-            turn(s)
-            if s + 2 < TILES:
-                times_l(s - 1)
-                for c in fresh:
-                    invert(c)
-                ds_quantize(s + 2)
-                for c in fresh:
-                    minus_square(c)
-            else:
-                planes_out(halves.pop(0), on_vector)
-            quantize_filled(ready)
-            dz_quantize(s - 1)
-            for j in halves:
-                planes_out(j, on_scalar)
             for i in squares.get(s, []):
                 square(i)
+            rows_out(s - 1, 0, on_scalar)
+            for i in squares.get(s, []):
+                if i in last_square:
+                    take_root(last_square[i])
+            rows_out(s - 1, 1, on_scalar)
+            for j in halves:
+                planes_out(j, on_scalar)
+            ready[s] = len(filled)
 
-        last = TILES - 1
-        rows_product(last - 1)
-        for j in range(half, half + 3):
-            planes_product(j)
-        quantize_filled(2)
+        quantize_filled(1)
         times_l(last)
-        rows_out(last - 1, 0, on_scalar)
-        planes_out(half, on_vector)
+        quantize_filled(1)
         dz_quantize(last)
-        rows_out(last - 1, 1, on_scalar)
-        planes_out(half + 1, on_vector)
-        planes_out(half + 2, on_scalar)
-        quantize_filled(2)
         rows_product(last)
-        planes_product(half + 3)
-        planes_product(half + 4)
+        for j in range(half, 2 * TILES):
+            planes_product(j)
+        quantize_filled(4)
         rows_out(last, 0, on_scalar)
         rows_out(last, 1, on_vector)
-        planes_out(half + 3, on_scalar)
-        planes_out(half + 4, on_vector)
-        quantize_filled(2)
+        for j in range(half, 2 * TILES):
+            planes_out(j, on_scalar if j % 2 == 0 else on_vector)
+        quantize_filled(4)

@@ -23,10 +23,11 @@ UNITS = M // UNIT
 DS_CHUNKS = [(0, 256), (256, 256), (512, 512), (1024, 1024)]
 STAT_GROUPS = [(0, 2), (2, 2), (4, 2), (6, 2), (8, 4), (12, 4)]
 Q_VECTOR = 96
-DS_VECTOR = 208
-DS_GROUPS = [(0, 1), (1, 1)] + [(a, 2) for a in range(2, TILES, 2)]
-SCALE_STORES = {2: 0, 4: 12}
-PLANE_GROUPS = [(0, 4), (4, 4), (8, 4), (12, 2), (14, 2)]
+CATCH = 2
+G0 = 3
+WAIT = 2
+SCALE_STORES = {1: 0, 4: 8}
+PLANE_GROUPS = [(0, 4), (4, 4), (8, 4), (12, 3), (15, 1)]
 
 
 def tile_ia3scaledqknormkeybackwardtoinput_x1_kernel(tc, ds, q, u, gamma, l, wk, out_0, out_1, out_2):
@@ -44,6 +45,7 @@ def tile_ia3scaledqknormkeybackwardtoinput_x1_kernel(tc, ds, q, u, gamma, l, wk,
         l_col = keep.tile([P, 4], BF16, name="l_col")
         g_col = keep.tile([P, 4], BF16, name="g_col")
         ident = keep.tile([P, P], F32, name="ident")
+        ident_bf = keep.tile([P, P], BF16, name="ident_bf")
         warm = keep.tile([P, 1], F32, name="warm")
 
         def load_q(g):
@@ -68,17 +70,18 @@ def tile_ia3scaledqknormkeybackwardtoinput_x1_kernel(tc, ds, q, u, gamma, l, wk,
         nc.vector.memset(warm[:], 1.0)
         nc.scalar.dma_start(out=g_col[:], in_=gamma.rearrange("(p t) -> p t", t=4))
         nc.scalar.dma_start(out=l_col[:], in_=l.rearrange("(p t) -> p t", t=4))
-        nc.scalar.activation(warm[:], warm[:], ACT.Sqrt)
+        nc.scalar.activation(warm[:], warm[:], ACT.Abs_reciprocal_sqrt)
         make_identity(nc, ident[:])
+        make_identity(nc, ident_bf[:])
 
         load_q(0)
         load_q(1)
         load_u(0)
         load_ds(0)
-        load_wk(0)
-        load_wk(1)
         load_ds(1)
         load_u(1)
+        load_wk(0)
+        load_wk(1)
         load_ds(2)
         load_u(2)
         load_u(3)
@@ -89,9 +92,8 @@ def tile_ia3scaledqknormkeybackwardtoinput_x1_kernel(tc, ds, q, u, gamma, l, wk,
         load_u(7)
 
         ssq = [keep.tile([P, w], F32, name="ssq%d" % c) for c, (a, w) in enumerate(STAT_GROUPS)]
-        root = [keep.tile([P, w], F32, name="root%d" % c) for c, (a, w) in enumerate(STAT_GROUPS)]
         rinv = [keep.tile([P, w], F32, name="rinv%d" % c) for c, (a, w) in enumerate(STAT_GROUPS)]
-        nrr = [keep.tile([P, w], F32, name="nrr%d" % c) for c, (a, w) in enumerate(STAT_GROUPS)]
+        rr = [keep.tile([P, w], F32, name="rr%d" % c) for c, (a, w) in enumerate(STAT_GROUPS)]
         group_of = [c for c, (a, w) in enumerate(STAT_GROUPS) for i in range(w)]
 
         def column(x, i):
@@ -106,13 +108,10 @@ def tile_ia3scaledqknormkeybackwardtoinput_x1_kernel(tc, ds, q, u, gamma, l, wk,
             nc.scalar.activation(sq[:], u_rows(i), ACT.Square, accum_out=column(ssq, i))
 
         def take_root(c):
-            nc.scalar.activation(root[c][:], ssq[c][:], ACT.Sqrt, bias=D * EPS)
+            nc.scalar.activation(rinv[c][:], ssq[c][:], ACT.Abs_reciprocal_sqrt, bias=D * EPS)
 
-        def invert(c):
-            nc.vector.reciprocal(rinv[c][:], root[c][:])
-
-        def minus_square(c):
-            nc.vector.scalar_tensor_tensor(nrr[c][:], rinv[c][:], -1.0, rinv[c][:], ALU.mult, ALU.mult)
+        def square_root_again(c):
+            nc.scalar.activation(rr[c][:], rinv[c][:], ACT.Square)
 
         qg = [keep.tile([P, D, 4], BF16, name="qg%d" % g, align_bytes=64) for g in range(2)]
         qc = keep.tile([P, 2, D], U32, name="qc", align_bytes=64)
@@ -131,34 +130,33 @@ def tile_ia3scaledqknormkeybackwardtoinput_x1_kernel(tc, ds, q, u, gamma, l, wk,
 
         dsg, dsc, dss = {}, {}, {}
 
-        ds_group_of = [k for k, (a, w) in enumerate(DS_GROUPS) for i in range(w)]
-
-        def ds_interleave(k, copy, passes=slice(0, 2), part=None):
-            first, width = DS_GROUPS[k][0] * P, DS_GROUPS[k][1] * P
-            c = [n for n, (a, w) in enumerate(DS_CHUNKS) if a <= first < a + w][0]
-            off = first - DS_CHUNKS[c][0]
-            lo, hi = part or (0, width)
-            if k not in dsg:
-                dsg[k] = work.tile([P, 2, width, 4], BF16, name="dsg", align_bytes=64)
+        def ds_interleave(i, g, copy):
+            c = [n for n, (a, w) in enumerate(DS_CHUNKS) if a <= i * P < a + w][0]
+            off = i * P - DS_CHUNKS[c][0]
+            if i not in dsg:
+                dsg[i] = work.tile([P, 2, P, 4], BF16, bufs=2, name="dsg", align_bytes=64)
+            run = 1 if copy == on_gpsimd else 4
             copy(
-                dsg[k][:, passes, lo:hi, :].rearrange("p g (c i) t -> p g c t i", i=4),
-                ds_raw[c][:, passes, :, off + lo : off + hi].rearrange("p g t (c i) -> p g c t i", i=4),
+                dsg[i][:, g, :, :].rearrange("p (c i) t -> p c t i", i=run),
+                ds_raw[c][:, g, :, off : off + P].rearrange("p t (c i) -> p c t i", i=run),
             )
 
-        def ds_quantize(k):
-            width = DS_GROUPS[k][1] * P
-            dsc[k] = work.tile([P, 2, width], U32, name="dsc", align_bytes=64)
-            dss[k] = work.tile([P, 2, width], U8, name="dss", align_bytes=64)
+        def ds_quantize(i):
+            dsc[i] = work.tile([P, 2, P], U32, name="dsc", align_bytes=64)
+            dss[i] = work.tile([P, 2, P], U8, name="dss", align_bytes=64)
             nc.vector.quantize_mx(
-                out=dsc[k][:].rearrange("p g c -> p (g c)").bitcast(X4),
-                scales=dss[k][:].rearrange("p g c -> p (g c)"),
-                in_=dsg[k][:].rearrange("p g c t -> p (g c t)"),
+                out=dsc[i][:].rearrange("p g c -> p (g c)").bitcast(X4),
+                scales=dss[i][:].rearrange("p g c -> p (g c)"),
+                in_=dsg[i][:].rearrange("p g c t -> p (g c t)"),
             )
+
+        def on_gpsimd(dst, src):
+            nc.gpsimd.tensor_scalar(dst, src, 1.0, 1.0, ALU.mult, ALU.mult)
 
         gam = keep.tile([P, 4, P], F32, name="gam")
 
         def spread_gamma():
-            bank = psum.tile([P, 2, P], F32, name="tr")
+            bank = psum.tile([P, 2, P], F32, bufs=1, name="tr")
             words = g_col[:].bitcast(F32)
             for w in range(2):
                 nc.tensor.transpose(bank[:, w, :], words[:, w : w + 1].to_broadcast([P, P]), ident[:])
@@ -197,23 +195,26 @@ def tile_ia3scaledqknormkeybackwardtoinput_x1_kernel(tc, ds, q, u, gamma, l, wk,
         dk, gr, cu, coef, tr, dzg, ob, rows, pb, pg = {}, {}, {}, {}, {}, {}, {}, {}, {}, {}
         dzc = [keep.tile([P, P], U32, name="dzc%d" % i, align_bytes=64) for i in range(TILES)]
         dzs = [keep.tile([P, P], U8, name="dzs%d" % i, align_bytes=64) for i in range(TILES)]
-        filled = []
+        filled, pc, ub = [], {}, {}
         pls = keep.tile([P, 2, M], U8, name="pls", align_bytes=64)
 
         def first_product(i):
-            k = ds_group_of[i]
-            cols = slice((i - DS_GROUPS[k][0]) * P, (i - DS_GROUPS[k][0] + 1) * P)
             dk[i] = psum.tile([P, D], F32, bufs=1, name="dk")
             for g in range(2):
                 nc.tensor.matmul_mx(
                     out=dk[i][:],
-                    lhsT=dsc[k][:, g, cols].bitcast(X4),
-                    lhsT_scale=dss[k][:, g, cols],
+                    lhsT=dsc[i][:, g, :].bitcast(X4),
+                    lhsT_scale=dss[i][:, g, :],
                     rhs=qc[:, g, :].bitcast(X4),
                     rhs_scale=qs[:, g, :],
                     start=(g == 0),
                     stop=(g == 1),
                 )
+
+        def u_to_psum(i):
+            ub[i] = psum.tile([P, 4, P], F32, bufs=1, name="ub")
+            src = u_rows(i).rearrange("m (p t) -> m t p", t=4)
+            nc.tensor.matmul(ub[i][:], ident_bf[:], src, start=True, stop=True)
 
         def scale_dk(i):
             gr[i] = work.tile([P, 4, P], F32, name="gr")
@@ -227,8 +228,8 @@ def tile_ia3scaledqknormkeybackwardtoinput_x1_kernel(tc, ds, q, u, gamma, l, wk,
             nc.vector.scalar_tensor_tensor(
                 prod[:],
                 gr[i][:],
-                column(nrr, i),
-                u_rows(i).rearrange("m (p t) -> m t p", t=4),
+                column(rr, i),
+                ub[i][:],
                 ALU.mult,
                 ALU.mult,
                 accum_out=coef[i][:],
@@ -237,10 +238,10 @@ def tile_ia3scaledqknormkeybackwardtoinput_x1_kernel(tc, ds, q, u, gamma, l, wk,
         def scale_u(i, engine):
             cu[i] = work.tile([P, 4, P], F32, name="cu")
             src = u_rows(i).rearrange("m (p t) -> m t p", t=4)
-            engine.tensor_scalar(cu[i][:], src, coef[i][:], 1.0, ALU.mult, ALU.mult)
+            engine.tensor_scalar(cu[i][:], src, coef[i][:], -1.0, ALU.mult, ALU.mult)
 
         def turn(i):
-            tr[i] = psum.tile([P, 4, P], F32, name="tr")
+            tr[i] = psum.tile([P, 4, P], F32, bufs=1, name="tr")
             for t in range(4):
                 nc.tensor.matmul(tr[i][:, t, :], gr[i][:, t, :], ident[:], start=True, stop=False, is_transpose=True)
                 nc.tensor.matmul(tr[i][:, t, :], cu[i][:, t, :], ident[:], start=False, stop=True, is_transpose=True)
@@ -277,7 +278,12 @@ def tile_ia3scaledqknormkeybackwardtoinput_x1_kernel(tc, ds, q, u, gamma, l, wk,
             if g == 0:
                 rows[i] = work.tile([P, 2, P, 4], F32, bufs=4, name="rows")
             copy(rows[i][:, g, :, :], ob[i, g][:].rearrange("m t p -> m p t"))
-            if g == 1:
+            if i == TILES - 1:
+                nc.sync.dma_start(
+                    out=out_0[i * P : (i + 1) * P, 512 * g : 512 * (g + 1)],
+                    in_=rows[i][:, g, :, :].rearrange("m p t -> m (p t)"),
+                )
+            elif g == 1:
                 nc.sync.dma_start(out=out_0[i * P : (i + 1) * P, :], in_=rows[i][:].rearrange("m g p t -> m (g p t)"))
 
         def planes_product(j):
@@ -310,13 +316,15 @@ def tile_ia3scaledqknormkeybackwardtoinput_x1_kernel(tc, ds, q, u, gamma, l, wk,
         def planes_quantize(k, g):
             a, w = PLANE_GROUPS[k]
             cols = slice(a * P, (a + w) * P)
-            codes = work.tile([P, w * P], U32, bufs=4, name="pc", align_bytes=64)
+            if g == 0:
+                pc[k] = work.tile([P, 2, w * P], U32, name="pc", align_bytes=64)
             nc.vector.quantize_mx(
-                out=codes[:].bitcast(X4), scales=pls[:, g, cols], in_=pg[k, g][:].rearrange("p m t -> p (m t)")
+                out=pc[k][:, g, :].bitcast(X4), scales=pls[:, g, cols], in_=pg[k, g][:].rearrange("p m t -> p (m t)")
             )
-            nc.sync.dma_start(
-                out=out_1[g, :, cols, :].rearrange("p m t -> p (m t)").bitcast(I32), in_=codes[:].bitcast(I32)
-            )
+            if g == 1:
+                nc.sync.dma_start(
+                    out=out_1[:, :, cols, :].rearrange("g p m t -> p g (m t)").bitcast(I32), in_=pc[k][:].bitcast(I32)
+                )
             if g == 1 and k in SCALE_STORES:
                 cols = slice(SCALE_STORES[k] * P, (a + w) * P)
                 for quad in range(4):
@@ -335,119 +343,133 @@ def tile_ia3scaledqknormkeybackwardtoinput_x1_kernel(tc, ds, q, u, gamma, l, wk,
         q_interleave(0)
         spread_gamma()
         q_interleave(1)
+        u_to_psum(0)
         q_quantize(0)
         square(0)
         square(1)
         q_quantize(1)
-        ds_interleave(0, on_vector, slice(0, 1))
+        ds_interleave(0, 0, on_vector)
         take_root(0)
-        ds_interleave(0, on_vector, slice(1, 2))
-        invert(0)
+        ds_interleave(0, 1, on_vector)
         ds_quantize(0)
-        minus_square(0)
-        ds_interleave(1, on_scalar)
+        ds_interleave(1, 0, on_scalar)
+        square_root_again(0)
+        ds_interleave(1, 1, on_scalar)
         first_product(0)
+        ds_interleave(2, 0, on_scalar)
+        ds_interleave(2, 1, on_scalar)
         scale_dk(0)
         ds_quantize(1)
-        wk_turn(0)
         first_product(1)
-        wk_out(0, 0)
-        wk_out(0, 1)
+        wk_turn(0)
+        square(2)
+        square(3)
         reduce_rows(0)
         scale_u(0, nc.gpsimd)
         scale_dk(1)
-        wk_turn(1)
+        u_to_psum(1)
         turn(0)
-        wk_out(1, 0)
-        wk_out(1, 1)
-        wk_quantize(0)
-        ds_interleave(2, on_vector, part=(0, DS_VECTOR))
-        ds_interleave(2, on_scalar, part=(DS_VECTOR, UNIT))
-        square(2)
-        square(3)
+        ds_interleave(3, 0, on_vector)
+        ds_interleave(3, 1, on_scalar)
+        take_root(1)
+        wk_out(0, 0)
+        square_root_again(1)
+        wk_out(0, 1)
+        ds_quantize(2)
+        first_product(2)
+        wk_turn(1)
         reduce_rows(1)
         scale_u(1, nc.gpsimd)
         times_l(0)
-        take_root(1)
-        ds_quantize(2)
-        first_product(2)
-        turn(1)
-        invert(1)
-        wk_quantize(1)
-        minus_square(1)
-        dz_quantize(0)
         scale_dk(2)
+        u_to_psum(2)
+        turn(1)
+        wk_out(1, 0)
+        wk_out(1, 1)
+        dz_quantize(0)
+        ds_quantize(3)
+        ds_interleave(4, 0, on_vector)
+        wk_quantize(0)
+        wk_quantize(1)
         first_product(3)
         rows_product(0)
-        ds_interleave(3, on_vector, part=(0, DS_VECTOR))
-        ds_interleave(3, on_scalar, part=(DS_VECTOR, UNIT))
+        ds_interleave(4, 1, on_scalar)
         square(4)
         square(5)
         rows_out(0, 0, on_scalar)
         take_root(2)
         rows_out(0, 1, on_scalar)
+        square_root_again(2)
 
-        squares = {2: [6, 7, 8], 3: [9, 10, 11]}
-        for s in range(4, 8):
-            squares[s] = [s + 8]
+        squares = {2: [6, 7], 3: [8, 9]}
+        for s in range(4, 10):
+            squares[s] = [s + 6]
         last_square = {sum(STAT_GROUPS[c]) - 1: c for c in range(len(STAT_GROUPS))}
         last = TILES - 1
         half = 0
-        rooted = {a - 2: [c] for c, (a, w) in enumerate(STAT_GROUPS)}
         ready = {}
-        for s in range(2, TILES):
-            count = 0 if s < 4 else 2 if s in squares else 3
+        for s in range(2, last):
+            count = 0 if s < CATCH else 3 - len(squares.get(s, []))
             halves = list(range(half, min(half + count, 2 * s)))
             half += len(halves)
+            if G0 <= s < TILES - 3:
+                ds_interleave(s + 3, 1, on_gpsimd)
             reduce_rows(s)
-            if s < last:
-                scale_u(s, nc.gpsimd)
-                times_l(s - 1)
-                scale_dk(s + 1)
-            else:
-                times_l(s - 1)
-                scale_u(s, nc.vector)
+            scale_u(s, nc.gpsimd)
+            times_l(s - 1)
+            scale_dk(s + 1)
+            u_to_psum(s + 1)
             turn(s)
             dz_quantize(s - 1)
-            for c in rooted.get(s, []):
-                invert(c)
-            if s % 2 == 0 and s + 2 < TILES:
-                ds_quantize(ds_group_of[s + 2])
-            for c in rooted.get(s, []):
-                minus_square(c)
-            if s % 2 == 1 and s + 3 < TILES:
-                ds_interleave(ds_group_of[s + 3], on_vector, part=(0, DS_VECTOR))
-                ds_interleave(ds_group_of[s + 3], on_scalar, part=(DS_VECTOR, UNIT))
-            if ready.get(s - 2, 0) > 0:
+            if s < G0:
+                ds_interleave(s + 3, 1, on_scalar)
+            if s + 3 < TILES:
+                ds_interleave(s + 3, 0, on_vector)
+            if ready.get(s - WAIT, 0) > 0:
                 quantize_filled(1)
                 for earlier in ready:
                     ready[earlier] -= 1
             if s + 2 < TILES:
-                first_product(s + 2)
+                ds_quantize(s + 2)
             rows_product(s - 1)
+            if s + 2 < TILES:
+                first_product(s + 2)
             for j in halves:
                 planes_product(j)
             for i in squares.get(s, []):
                 square(i)
+            rooted = [last_square[i] for i in squares.get(s, []) if i in last_square]
             rows_out(s - 1, 0, on_scalar)
-            for i in squares.get(s, []):
-                if i in last_square:
-                    take_root(last_square[i])
+            for c in rooted:
+                take_root(c)
             rows_out(s - 1, 1, on_scalar)
+            for c in rooted:
+                square_root_again(c)
             for j in halves:
                 planes_out(j, on_scalar)
             ready[s] = len(filled)
 
+        reduce_rows(last)
+        times_l(last - 1)
+        scale_u(last, nc.vector)
+        turn(last)
+        dz_quantize(last - 1)
+        rows_product(last - 1)
+        for j in range(half, 2 * last):
+            planes_product(j)
         quantize_filled(1)
         times_l(last)
-        quantize_filled(1)
+        rows_out(last - 1, 0, on_scalar)
+        rows_out(last - 1, 1, on_vector)
         dz_quantize(last)
+        for j in range(half, 2 * last):
+            planes_out(j, on_vector if j == 2 * last - 1 else on_scalar)
         rows_product(last)
-        for j in range(half, 2 * TILES):
-            planes_product(j)
-        quantize_filled(4)
+        planes_product(2 * last)
+        planes_product(2 * last + 1)
+        quantize_filled(len(filled))
         rows_out(last, 0, on_scalar)
-        rows_out(last, 1, on_vector)
-        for j in range(half, 2 * TILES):
-            planes_out(j, on_scalar if j % 2 == 0 else on_vector)
-        quantize_filled(4)
+        planes_out(2 * last, on_scalar)
+        planes_out(2 * last + 1, on_vector)
+        rows_out(last, 1, on_scalar)
+        quantize_filled(len(filled))

@@ -19,15 +19,19 @@ P = 128
 EPS = 1e-6
 TILES = M // P
 UNIT = 2 * P
-UNITS = M // UNIT
 DS_CHUNKS = [(0, 256), (256, 256), (512, 512), (1024, 1024)]
-STAT_GROUPS = [(0, 2), (2, 2), (4, 2), (6, 2), (8, 4), (12, 4)]
+U_CHUNKS = [(0, 2), (2, 2), (4, 4), (8, 8)]
+STAT_GROUPS = [(a, 2) for a in range(0, TILES, 2)]
+DS_GROUPS = [(0, 1), (1, 1)] + [(a, 2) for a in range(2, TILES, 2)]
 Q_VECTOR = 96
-CATCH = 2
-G0 = 3
+DS_VECTOR = 224
 WAIT = 2
-SCALE_STORES = {1: 0, 4: 8}
-PLANE_GROUPS = [(0, 4), (4, 4), (8, 4), (12, 3), (15, 1)]
+STOPQ = 15
+E1 = 1
+E2 = 1
+D3 = 64
+SCALE_STORES = {1: 0, 4: 7}
+PLANE_GROUPS = [(0, 3), (3, 4), (7, 4), (11, 3), (14, 2)]
 
 
 def tile_ia3scaledqknormkeybackwardtoinput_x1_kernel(tc, ds, q, u, gamma, l, wk, out_0, out_1, out_2):
@@ -38,14 +42,16 @@ def tile_ia3scaledqknormkeybackwardtoinput_x1_kernel(tc, ds, q, u, gamma, l, wk,
         psum = ctx.enter_context(tc.psum_pool(name="psum", bufs=2))
         ctx.enter_context(tc.manual_schedule())
 
-        q_raw = [keep.tile([P, 4, D], BF16, name="q_raw%d" % g) for g in range(2)]
+        def wide(shape, dtype):
+            return work.tile(shape, dtype, bufs=TILES, name="wide", align_bytes=64)
+
+        q_raw = [wide([P, 4, D], BF16) for g in range(2)]
         ds_raw = [keep.tile([P, 2, 4, w], BF16, name="ds_raw%d" % c) for c, (a, w) in enumerate(DS_CHUNKS)]
-        u_raw = [keep.tile([P, 2, D], BF16, name="u_raw%d" % c) for c in range(UNITS)]
-        wk_raw = [keep.tile([P, 4 * D], BF16, name="wk_raw%d" % g) for g in range(2)]
+        u_raw = [keep.tile([P, w, D], BF16, name="u_raw%d" % c) for c, (a, w) in enumerate(U_CHUNKS)]
+        wk_raw = [wide([P, 4 * D], BF16) for g in range(2)]
         l_col = keep.tile([P, 4], BF16, name="l_col")
         g_col = keep.tile([P, 4], BF16, name="g_col")
         ident = keep.tile([P, P], F32, name="ident")
-        ident_bf = keep.tile([P, P], BF16, name="ident_bf")
         warm = keep.tile([P, 1], F32, name="warm")
 
         def load_q(g):
@@ -60,7 +66,8 @@ def tile_ia3scaledqknormkeybackwardtoinput_x1_kernel(tc, ds, q, u, gamma, l, wk,
                 )
 
         def load_u(c):
-            nc.sync.dma_start(out=u_raw[c][:], in_=u[UNIT * c : UNIT * (c + 1), :].rearrange("(i p) d -> p i d", i=2))
+            a, w = U_CHUNKS[c]
+            nc.sync.dma_start(out=u_raw[c][:], in_=u[a * P : (a + w) * P, :].rearrange("(i p) d -> p i d", i=w))
 
         def load_wk(g):
             nc.sync.dma_start(
@@ -72,7 +79,6 @@ def tile_ia3scaledqknormkeybackwardtoinput_x1_kernel(tc, ds, q, u, gamma, l, wk,
         nc.scalar.dma_start(out=l_col[:], in_=l.rearrange("(p t) -> p t", t=4))
         nc.scalar.activation(warm[:], warm[:], ACT.Abs_reciprocal_sqrt)
         make_identity(nc, ident[:])
-        make_identity(nc, ident_bf[:])
 
         load_q(0)
         load_q(1)
@@ -84,12 +90,8 @@ def tile_ia3scaledqknormkeybackwardtoinput_x1_kernel(tc, ds, q, u, gamma, l, wk,
         load_wk(1)
         load_ds(2)
         load_u(2)
-        load_u(3)
-        load_u(4)
-        load_u(5)
         load_ds(3)
-        load_u(6)
-        load_u(7)
+        load_u(3)
 
         ssq = [keep.tile([P, w], F32, name="ssq%d" % c) for c, (a, w) in enumerate(STAT_GROUPS)]
         rinv = [keep.tile([P, w], F32, name="rinv%d" % c) for c, (a, w) in enumerate(STAT_GROUPS)]
@@ -101,10 +103,11 @@ def tile_ia3scaledqknormkeybackwardtoinput_x1_kernel(tc, ds, q, u, gamma, l, wk,
             return x[group_of[i]][:, j : j + 1]
 
         def u_rows(i):
-            return u_raw[i // 2][:, i % 2, :]
+            c = [n for n, (a, w) in enumerate(U_CHUNKS) if a <= i < a + w][0]
+            return u_raw[c][:, i - U_CHUNKS[c][0], :]
 
         def square(i):
-            sq = work.tile([P, D], BF16, name="sq")
+            sq = work.tile([P, D], BF16, bufs=1, name="sq")
             nc.scalar.activation(sq[:], u_rows(i), ACT.Square, accum_out=column(ssq, i))
 
         def take_root(c):
@@ -113,7 +116,7 @@ def tile_ia3scaledqknormkeybackwardtoinput_x1_kernel(tc, ds, q, u, gamma, l, wk,
         def square_root_again(c):
             nc.scalar.activation(rr[c][:], rinv[c][:], ACT.Square)
 
-        qg = [keep.tile([P, D, 4], BF16, name="qg%d" % g, align_bytes=64) for g in range(2)]
+        qg = [wide([P, D, 4], BF16) for g in range(2)]
         qc = keep.tile([P, 2, D], U32, name="qc", align_bytes=64)
         qs = keep.tile([P, 2, D], U8, name="qs", align_bytes=64)
 
@@ -130,33 +133,34 @@ def tile_ia3scaledqknormkeybackwardtoinput_x1_kernel(tc, ds, q, u, gamma, l, wk,
 
         dsg, dsc, dss = {}, {}, {}
 
-        def ds_interleave(i, g, copy):
-            c = [n for n, (a, w) in enumerate(DS_CHUNKS) if a <= i * P < a + w][0]
-            off = i * P - DS_CHUNKS[c][0]
-            if i not in dsg:
-                dsg[i] = work.tile([P, 2, P, 4], BF16, bufs=2, name="dsg", align_bytes=64)
-            run = 1 if copy == on_gpsimd else 4
+        ds_group_of = [k for k, (a, w) in enumerate(DS_GROUPS) for i in range(w)]
+
+        def ds_interleave(k, copy, passes=slice(0, 2), part=None):
+            first, width = DS_GROUPS[k][0] * P, DS_GROUPS[k][1] * P
+            c = [n for n, (a, w) in enumerate(DS_CHUNKS) if a <= first < a + w][0]
+            off = first - DS_CHUNKS[c][0]
+            lo, hi = part or (0, width)
+            if k not in dsg:
+                dsg[k] = work.tile([P, 2, width, 4], BF16, name="dsg", align_bytes=64)
             copy(
-                dsg[i][:, g, :, :].rearrange("p (c i) t -> p c t i", i=run),
-                ds_raw[c][:, g, :, off : off + P].rearrange("p t (c i) -> p c t i", i=run),
+                dsg[k][:, passes, lo:hi, :].rearrange("p g (c i) t -> p g c t i", i=4),
+                ds_raw[c][:, passes, :, off + lo : off + hi].rearrange("p g t (c i) -> p g c t i", i=4),
             )
 
-        def ds_quantize(i):
-            dsc[i] = work.tile([P, 2, P], U32, name="dsc", align_bytes=64)
-            dss[i] = work.tile([P, 2, P], U8, name="dss", align_bytes=64)
+        def ds_quantize(k):
+            width = DS_GROUPS[k][1] * P
+            dsc[k] = work.tile([P, 2, width], U32, name="dsc", align_bytes=64)
+            dss[k] = work.tile([P, 2, width], U8, name="dss", align_bytes=64)
             nc.vector.quantize_mx(
-                out=dsc[i][:].rearrange("p g c -> p (g c)").bitcast(X4),
-                scales=dss[i][:].rearrange("p g c -> p (g c)"),
-                in_=dsg[i][:].rearrange("p g c t -> p (g c t)"),
+                out=dsc[k][:].rearrange("p g c -> p (g c)").bitcast(X4),
+                scales=dss[k][:].rearrange("p g c -> p (g c)"),
+                in_=dsg[k][:].rearrange("p g c t -> p (g c t)"),
             )
-
-        def on_gpsimd(dst, src):
-            nc.gpsimd.tensor_scalar(dst, src, 1.0, 1.0, ALU.mult, ALU.mult)
 
         gam = keep.tile([P, 4, P], F32, name="gam")
 
         def spread_gamma():
-            bank = psum.tile([P, 2, P], F32, bufs=1, name="tr")
+            bank = psum.tile([P, 2, P], F32, name="tr")
             words = g_col[:].bitcast(F32)
             for w in range(2):
                 nc.tensor.transpose(bank[:, w, :], words[:, w : w + 1].to_broadcast([P, P]), ident[:])
@@ -165,7 +169,7 @@ def tile_ia3scaledqknormkeybackwardtoinput_x1_kernel(tc, ds, q, u, gamma, l, wk,
                 bank[:].bitcast(BF16).rearrange("x w (p e) -> x w e p", e=2),
             )
 
-        wg = keep.tile([P, E, 4], BF16, name="wg", align_bytes=64)
+        wg = [wide([P, 512, 4], BF16) for g in range(2)]
         wkc = keep.tile([P, E], U32, name="wkc", align_bytes=64)
         wks = keep.tile([P, E], U8, name="wks", align_bytes=64)
 
@@ -182,39 +186,35 @@ def tile_ia3scaledqknormkeybackwardtoinput_x1_kernel(tc, ds, q, u, gamma, l, wk,
                 wb[g, b] = bank
 
         def wk_out(g, b):
-            cols = slice(512 * g + 256 * b, 512 * g + 256 * (b + 1))
-            dst = wg[:, cols, :].rearrange("p c k -> p (c k)").bitcast(F32)
+            dst = wg[g][:, 256 * b : 256 * (b + 1), :].rearrange("p c k -> p (c k)").bitcast(F32)
             nc.scalar.copy(dst.rearrange("p (a c w) -> p a c w", a=2, w=2), wb[g, b][:].rearrange("p a w c -> p a c w"))
 
         def wk_quantize(g):
             cols = slice(512 * g, 512 * (g + 1))
             nc.vector.quantize_mx(
-                out=wkc[:, cols].bitcast(X4), scales=wks[:, cols], in_=wg[:, cols, :].rearrange("p c k -> p (c k)")
+                out=wkc[:, cols].bitcast(X4), scales=wks[:, cols], in_=wg[g][:].rearrange("p c k -> p (c k)")
             )
 
         dk, gr, cu, coef, tr, dzg, ob, rows, pb, pg = {}, {}, {}, {}, {}, {}, {}, {}, {}, {}
         dzc = [keep.tile([P, P], U32, name="dzc%d" % i, align_bytes=64) for i in range(TILES)]
         dzs = [keep.tile([P, P], U8, name="dzs%d" % i, align_bytes=64) for i in range(TILES)]
-        filled, pc, ub = [], {}, {}
+        filled, pc, done = [], {}, set()
         pls = keep.tile([P, 2, M], U8, name="pls", align_bytes=64)
 
         def first_product(i):
+            k = ds_group_of[i]
+            cols = slice((i - DS_GROUPS[k][0]) * P, (i - DS_GROUPS[k][0] + 1) * P)
             dk[i] = psum.tile([P, D], F32, bufs=1, name="dk")
             for g in range(2):
                 nc.tensor.matmul_mx(
                     out=dk[i][:],
-                    lhsT=dsc[i][:, g, :].bitcast(X4),
-                    lhsT_scale=dss[i][:, g, :],
+                    lhsT=dsc[k][:, g, cols].bitcast(X4),
+                    lhsT_scale=dss[k][:, g, cols],
                     rhs=qc[:, g, :].bitcast(X4),
                     rhs_scale=qs[:, g, :],
                     start=(g == 0),
                     stop=(g == 1),
                 )
-
-        def u_to_psum(i):
-            ub[i] = psum.tile([P, 4, P], F32, bufs=1, name="ub")
-            src = u_rows(i).rearrange("m (p t) -> m t p", t=4)
-            nc.tensor.matmul(ub[i][:], ident_bf[:], src, start=True, stop=True)
 
         def scale_dk(i):
             gr[i] = work.tile([P, 4, P], F32, name="gr")
@@ -223,13 +223,13 @@ def tile_ia3scaledqknormkeybackwardtoinput_x1_kernel(tc, ds, q, u, gamma, l, wk,
             )
 
         def reduce_rows(i):
-            prod = work.tile([P, 4, P], BF16, name="prod")
-            coef[i] = work.tile([P, 1], F32, name="coef")
+            prod = work.tile([P, 4, P], BF16, bufs=1, name="prod")
+            coef[i] = work.tile([P, 1], F32, bufs=TILES, name="coef")
             nc.vector.scalar_tensor_tensor(
                 prod[:],
                 gr[i][:],
                 column(rr, i),
-                ub[i][:],
+                u_rows(i).rearrange("m (p t) -> m t p", t=4),
                 ALU.mult,
                 ALU.mult,
                 accum_out=coef[i][:],
@@ -241,7 +241,7 @@ def tile_ia3scaledqknormkeybackwardtoinput_x1_kernel(tc, ds, q, u, gamma, l, wk,
             engine.tensor_scalar(cu[i][:], src, coef[i][:], -1.0, ALU.mult, ALU.mult)
 
         def turn(i):
-            tr[i] = psum.tile([P, 4, P], F32, bufs=1, name="tr")
+            tr[i] = psum.tile([P, 4, P], F32, name="tr")
             for t in range(4):
                 nc.tensor.matmul(tr[i][:, t, :], gr[i][:, t, :], ident[:], start=True, stop=False, is_transpose=True)
                 nc.tensor.matmul(tr[i][:, t, :], cu[i][:, t, :], ident[:], start=False, stop=True, is_transpose=True)
@@ -275,15 +275,15 @@ def tile_ia3scaledqknormkeybackwardtoinput_x1_kernel(tc, ds, q, u, gamma, l, wk,
                 )
 
         def rows_out(i, g, copy):
-            if g == 0:
-                rows[i] = work.tile([P, 2, P, 4], F32, bufs=4, name="rows")
+            if i not in rows:
+                rows[i] = wide([P, 2, P, 4], F32)
             copy(rows[i][:, g, :, :], ob[i, g][:].rearrange("m t p -> m p t"))
-            if i == TILES - 1:
+            if i >= TILES - 2:
                 nc.sync.dma_start(
                     out=out_0[i * P : (i + 1) * P, 512 * g : 512 * (g + 1)],
                     in_=rows[i][:, g, :, :].rearrange("m p t -> m (p t)"),
                 )
-            elif g == 1:
+            elif g == 0:
                 nc.sync.dma_start(out=out_0[i * P : (i + 1) * P, :], in_=rows[i][:].rearrange("m g p t -> m (g p t)"))
 
         def planes_product(j):
@@ -316,16 +316,17 @@ def tile_ia3scaledqknormkeybackwardtoinput_x1_kernel(tc, ds, q, u, gamma, l, wk,
         def planes_quantize(k, g):
             a, w = PLANE_GROUPS[k]
             cols = slice(a * P, (a + w) * P)
-            if g == 0:
-                pc[k] = work.tile([P, 2, w * P], U32, name="pc", align_bytes=64)
+            if k not in pc:
+                pc[k] = work.tile([P, 2, w * P], U32, bufs=len(PLANE_GROUPS), name="pc", align_bytes=64)
             nc.vector.quantize_mx(
                 out=pc[k][:, g, :].bitcast(X4), scales=pls[:, g, cols], in_=pg[k, g][:].rearrange("p m t -> p (m t)")
             )
-            if g == 1:
+            done.add((k, g))
+            if (k, 1 - g) in done:
                 nc.sync.dma_start(
                     out=out_1[:, :, cols, :].rearrange("g p m t -> p g (m t)").bitcast(I32), in_=pc[k][:].bitcast(I32)
                 )
-            if g == 1 and k in SCALE_STORES:
+            if (k, 1 - g) in done and k in SCALE_STORES:
                 cols = slice(SCALE_STORES[k] * P, (a + w) * P)
                 for quad in range(4):
                     nc.sync.dma_start(
@@ -343,21 +344,19 @@ def tile_ia3scaledqknormkeybackwardtoinput_x1_kernel(tc, ds, q, u, gamma, l, wk,
         q_interleave(0)
         spread_gamma()
         q_interleave(1)
-        u_to_psum(0)
         q_quantize(0)
         square(0)
         square(1)
         q_quantize(1)
-        ds_interleave(0, 0, on_vector)
+        ds_interleave(0, on_vector, slice(0, 1))
         take_root(0)
-        ds_interleave(0, 1, on_vector)
+        ds_interleave(0, on_vector, slice(1, 2))
         ds_quantize(0)
-        ds_interleave(1, 0, on_scalar)
+        ds_interleave(1, on_scalar, slice(0, 1))
         square_root_again(0)
-        ds_interleave(1, 1, on_scalar)
+        ds_interleave(1, on_scalar, slice(1, 2))
         first_product(0)
-        ds_interleave(2, 0, on_scalar)
-        ds_interleave(2, 1, on_scalar)
+        ds_interleave(2, on_scalar)
         scale_dk(0)
         ds_quantize(1)
         first_product(1)
@@ -367,109 +366,109 @@ def tile_ia3scaledqknormkeybackwardtoinput_x1_kernel(tc, ds, q, u, gamma, l, wk,
         reduce_rows(0)
         scale_u(0, nc.gpsimd)
         scale_dk(1)
-        u_to_psum(1)
         turn(0)
-        ds_interleave(3, 0, on_vector)
-        ds_interleave(3, 1, on_scalar)
-        take_root(1)
         wk_out(0, 0)
-        square_root_again(1)
+        take_root(1)
         wk_out(0, 1)
+        square_root_again(1)
         ds_quantize(2)
         first_product(2)
         wk_turn(1)
         reduce_rows(1)
         scale_u(1, nc.gpsimd)
-        times_l(0)
         scale_dk(2)
-        u_to_psum(2)
+        times_l(0)
         turn(1)
+        first_product(3)
         wk_out(1, 0)
         wk_out(1, 1)
-        dz_quantize(0)
-        ds_quantize(3)
-        ds_interleave(4, 0, on_vector)
         wk_quantize(0)
+        dz_quantize(0)
+        ds_interleave(3, on_vector, part=(0, D3))
+        ds_interleave(3, on_scalar, part=(D3, UNIT))
         wk_quantize(1)
-        first_product(3)
         rows_product(0)
-        ds_interleave(4, 1, on_scalar)
+        planes_product(0)
+        planes_product(1)
         square(4)
         square(5)
-        rows_out(0, 0, on_scalar)
-        take_root(2)
         rows_out(0, 1, on_scalar)
+        take_root(2)
+        rows_out(0, 0, on_scalar)
         square_root_again(2)
+        planes_out(1, on_scalar)
+        planes_out(0, on_scalar)
 
-        squares = {2: [6, 7], 3: [8, 9]}
-        for s in range(4, 10):
-            squares[s] = [s + 6]
+        squares = {s: [s + 4] for s in range(2, 4)}
+        squares.update({s: [s + 4] for s in range(4, TILES - 4)})
         last_square = {sum(STAT_GROUPS[c]) - 1: c for c in range(len(STAT_GROUPS))}
         last = TILES - 1
-        half = 0
         ready = {}
         for s in range(2, last):
-            count = 0 if s < CATCH else 3 - len(squares.get(s, []))
-            halves = list(range(half, min(half + count, 2 * s)))
-            half += len(halves)
-            if G0 <= s < TILES - 3:
-                ds_interleave(s + 3, 1, on_gpsimd)
             reduce_rows(s)
             scale_u(s, nc.gpsimd)
-            times_l(s - 1)
             scale_dk(s + 1)
-            u_to_psum(s + 1)
+            if 2 < s < TILES - 2:
+                first_product(s + 2)
+            times_l(s - 1)
             turn(s)
-            dz_quantize(s - 1)
-            if s < G0:
-                ds_interleave(s + 3, 1, on_scalar)
-            if s + 3 < TILES:
-                ds_interleave(s + 3, 0, on_vector)
-            if ready.get(s - WAIT, 0) > 0:
+            if s == 2:
+                ds_quantize(ds_group_of[s + 2])
+                first_product(s + 2)
+            if s % 2 == 1 and s + 3 < TILES:
+                ds_quantize(ds_group_of[s + 3])
+            if s % 2 == 0 and s + 4 < TILES:
+                ds_interleave(ds_group_of[s + 4], on_vector, part=(0, DS_VECTOR))
+                if DS_VECTOR < UNIT:
+                    ds_interleave(ds_group_of[s + 4], on_scalar, part=(DS_VECTOR, UNIT))
+            early = s + 4 >= TILES and s % 2 == 0 or s + 3 >= TILES
+            if not early:
+                dz_quantize(s - 1)
+            if ready.get(s - WAIT, 0) > 0 and (s % 2 == 1 or s + 4 >= TILES) and s < STOPQ:
                 quantize_filled(1)
                 for earlier in ready:
                     ready[earlier] -= 1
-            if s + 2 < TILES:
-                ds_quantize(s + 2)
+            if early:
+                dz_quantize(s - 1)
             rows_product(s - 1)
-            if s + 2 < TILES:
-                first_product(s + 2)
-            for j in halves:
-                planes_product(j)
+            planes_product(2 * s - 2)
+            planes_product(2 * s - 1)
             for i in squares.get(s, []):
                 square(i)
             rooted = [last_square[i] for i in squares.get(s, []) if i in last_square]
-            rows_out(s - 1, 0, on_scalar)
-            for c in rooted:
-                take_root(c)
             rows_out(s - 1, 1, on_scalar)
             for c in rooted:
+                take_root(c)
+            rows_out(s - 1, 0, on_scalar)
+            for c in rooted:
                 square_root_again(c)
-            for j in halves:
-                planes_out(j, on_scalar)
+            planes_out(2 * s - 1, on_scalar)
+            if s < last - 1:
+                planes_out(2 * s - 2, on_scalar)
             ready[s] = len(filled)
 
         reduce_rows(last)
-        times_l(last - 1)
         scale_u(last, nc.vector)
+        times_l(last - 1)
         turn(last)
+        planes_out(2 * last - 4, on_vector)
         dz_quantize(last - 1)
         rows_product(last - 1)
-        for j in range(half, 2 * last):
-            planes_product(j)
-        quantize_filled(1)
+        planes_product(2 * last - 2)
+        planes_product(2 * last - 1)
         times_l(last)
+        quantize_filled(E1)
         rows_out(last - 1, 0, on_scalar)
-        rows_out(last - 1, 1, on_vector)
+        rows_out(last - 1, 1, on_scalar)
         dz_quantize(last)
-        for j in range(half, 2 * last):
-            planes_out(j, on_vector if j == 2 * last - 1 else on_scalar)
+        planes_out(2 * last - 2, on_vector)
         rows_product(last)
+        planes_out(2 * last - 1, on_vector)
         planes_product(2 * last)
         planes_product(2 * last + 1)
         quantize_filled(len(filled))
         rows_out(last, 0, on_scalar)
-        planes_out(2 * last, on_scalar)
-        planes_out(2 * last + 1, on_vector)
         rows_out(last, 1, on_scalar)
+        planes_out(2 * last, on_vector)
+        planes_out(2 * last + 1, on_scalar)
         quantize_filled(len(filled))

@@ -26,6 +26,11 @@ DS_GROUPS = [(0, 1), (1, 1)] + [(a, 2) for a in range(2, TILES, 2)]
 Q_VECTOR = 96
 DS_VECTOR = 224
 WAIT = 2
+DS_LATE = 224
+SPLIT = 16
+PRO = 1
+TWO = 0
+CATCH = 12
 STOPQ = 15
 E1 = 1
 E2 = 1
@@ -57,9 +62,9 @@ def tile_ia3scaledqknormkeybackwardtoinput_x1_kernel(tc, ds, q, u, gamma, l, wk,
         def load_q(g):
             nc.sync.dma_start(out=q_raw[g][:], in_=q[512 * g : 512 * (g + 1), :].rearrange("(p j) d -> p j d", j=4))
 
-        def load_ds(c):
+        def load_ds(c, passes=(0, 1)):
             a, w = DS_CHUNKS[c]
-            for g in range(2):
+            for g in passes:
                 nc.sync.dma_start(
                     out=ds_raw[c][:, g, :, :],
                     in_=ds[512 * g : 512 * (g + 1), a : a + w].rearrange("(p j) m -> p j m", j=4),
@@ -81,9 +86,10 @@ def tile_ia3scaledqknormkeybackwardtoinput_x1_kernel(tc, ds, q, u, gamma, l, wk,
         make_identity(nc, ident[:])
 
         load_q(0)
+        load_ds(0, (0,))
         load_q(1)
+        load_ds(0, (1,))
         load_u(0)
-        load_ds(0)
         load_ds(1)
         load_u(1)
         load_wk(0)
@@ -147,14 +153,15 @@ def tile_ia3scaledqknormkeybackwardtoinput_x1_kernel(tc, ds, q, u, gamma, l, wk,
                 ds_raw[c][:, passes, :, off + lo : off + hi].rearrange("p g t (c i) -> p g c t i", i=4),
             )
 
-        def ds_quantize(k):
+        def ds_quantize(k, passes=slice(0, 2)):
             width = DS_GROUPS[k][1] * P
-            dsc[k] = work.tile([P, 2, width], U32, name="dsc", align_bytes=64)
-            dss[k] = work.tile([P, 2, width], U8, name="dss", align_bytes=64)
+            if k not in dsc:
+                dsc[k] = work.tile([P, 2, width], U32, name="dsc", align_bytes=64)
+                dss[k] = work.tile([P, 2, width], U8, name="dss", align_bytes=64)
             nc.vector.quantize_mx(
-                out=dsc[k][:].rearrange("p g c -> p (g c)").bitcast(X4),
-                scales=dss[k][:].rearrange("p g c -> p (g c)"),
-                in_=dsg[k][:].rearrange("p g c t -> p (g c t)"),
+                out=dsc[k][:, passes, :].rearrange("p g c -> p (g c)").bitcast(X4),
+                scales=dss[k][:, passes, :].rearrange("p g c -> p (g c)"),
+                in_=dsg[k][:, passes, :, :].rearrange("p g c t -> p (g c t)"),
             )
 
         gam = keep.tile([P, 4, P], F32, name="gam")
@@ -198,7 +205,7 @@ def tile_ia3scaledqknormkeybackwardtoinput_x1_kernel(tc, ds, q, u, gamma, l, wk,
         dk, gr, cu, coef, tr, dzg, ob, rows, pb, pg = {}, {}, {}, {}, {}, {}, {}, {}, {}, {}
         dzc = [keep.tile([P, P], U32, name="dzc%d" % i, align_bytes=64) for i in range(TILES)]
         dzs = [keep.tile([P, P], U8, name="dzs%d" % i, align_bytes=64) for i in range(TILES)]
-        filled, pc, done = [], {}, set()
+        filled, pc, done, stored = [], {}, set(), set()
         pls = keep.tile([P, 2, M], U8, name="pls", align_bytes=64)
 
         def first_product(i):
@@ -278,12 +285,13 @@ def tile_ia3scaledqknormkeybackwardtoinput_x1_kernel(tc, ds, q, u, gamma, l, wk,
             if i not in rows:
                 rows[i] = wide([P, 2, P, 4], F32)
             copy(rows[i][:, g, :, :], ob[i, g][:].rearrange("m t p -> m p t"))
-            if i >= TILES - 2:
+            stored.add((i, g))
+            if i >= SPLIT:
                 nc.sync.dma_start(
                     out=out_0[i * P : (i + 1) * P, 512 * g : 512 * (g + 1)],
                     in_=rows[i][:, g, :, :].rearrange("m p t -> m (p t)"),
                 )
-            elif g == 0:
+            elif (i, 1 - g) in stored:
                 nc.sync.dma_start(out=out_0[i * P : (i + 1) * P, :], in_=rows[i][:].rearrange("m g p t -> m (g p t)"))
 
         def planes_product(j):
@@ -342,30 +350,30 @@ def tile_ia3scaledqknormkeybackwardtoinput_x1_kernel(tc, ds, q, u, gamma, l, wk,
             filled[:upto] = []
 
         q_interleave(0)
+        ds_interleave(0, on_scalar, slice(0, 1))
+        q_quantize(0)
         spread_gamma()
         q_interleave(1)
-        q_quantize(0)
+        ds_interleave(1, on_scalar, slice(0, 1))
+        ds_interleave(0, on_vector, slice(1, 2))
+        q_quantize(1)
         square(0)
         square(1)
-        q_quantize(1)
-        ds_interleave(0, on_vector, slice(0, 1))
-        take_root(0)
-        ds_interleave(0, on_vector, slice(1, 2))
         ds_quantize(0)
-        ds_interleave(1, on_scalar, slice(0, 1))
-        square_root_again(0)
-        ds_interleave(1, on_scalar, slice(1, 2))
+        take_root(0)
         first_product(0)
+        ds_interleave(1, on_vector, slice(1, 2))
+        square_root_again(0)
         ds_interleave(2, on_scalar)
-        scale_dk(0)
         ds_quantize(1)
+        scale_dk(0)
         first_product(1)
-        wk_turn(0)
         square(2)
         square(3)
+        wk_turn(0)
         reduce_rows(0)
-        scale_u(0, nc.gpsimd)
         scale_dk(1)
+        scale_u(0, nc.vector)
         turn(0)
         wk_out(0, 0)
         take_root(1)
@@ -376,8 +384,8 @@ def tile_ia3scaledqknormkeybackwardtoinput_x1_kernel(tc, ds, q, u, gamma, l, wk,
         wk_turn(1)
         reduce_rows(1)
         scale_u(1, nc.gpsimd)
-        scale_dk(2)
         times_l(0)
+        scale_dk(2)
         turn(1)
         first_product(3)
         wk_out(1, 0)
@@ -388,19 +396,20 @@ def tile_ia3scaledqknormkeybackwardtoinput_x1_kernel(tc, ds, q, u, gamma, l, wk,
         ds_interleave(3, on_scalar, part=(D3, UNIT))
         wk_quantize(1)
         rows_product(0)
-        planes_product(0)
-        planes_product(1)
+        for j in range(2 * PRO):
+            planes_product(j)
         square(4)
         square(5)
         rows_out(0, 1, on_scalar)
         take_root(2)
         rows_out(0, 0, on_scalar)
         square_root_again(2)
-        planes_out(1, on_scalar)
-        planes_out(0, on_scalar)
+        for j in reversed(range(2 * PRO)):
+            planes_out(j, on_scalar)
 
-        squares = {s: [s + 4] for s in range(2, 4)}
-        squares.update({s: [s + 4] for s in range(4, TILES - 4)})
+        squares = {2 + s: [6 + 2 * s, 7 + 2 * s] for s in range(TWO)}
+        squares.update({s: [s + 4 + TWO] for s in range(2 + TWO, TILES - 4 - TWO)})
+        half = 2 * PRO
         last_square = {sum(STAT_GROUPS[c]) - 1: c for c in range(len(STAT_GROUPS))}
         last = TILES - 1
         ready = {}
@@ -418,9 +427,10 @@ def tile_ia3scaledqknormkeybackwardtoinput_x1_kernel(tc, ds, q, u, gamma, l, wk,
             if s % 2 == 1 and s + 3 < TILES:
                 ds_quantize(ds_group_of[s + 3])
             if s % 2 == 0 and s + 4 < TILES:
-                ds_interleave(ds_group_of[s + 4], on_vector, part=(0, DS_VECTOR))
-                if DS_VECTOR < UNIT:
-                    ds_interleave(ds_group_of[s + 4], on_scalar, part=(DS_VECTOR, UNIT))
+                share = DS_VECTOR if s in squares else DS_LATE
+                ds_interleave(ds_group_of[s + 4], on_vector, part=(0, share))
+                if share < UNIT:
+                    ds_interleave(ds_group_of[s + 4], on_scalar, part=(share, UNIT))
             early = s + 4 >= TILES and s % 2 == 0 or s + 3 >= TILES
             if not early:
                 dz_quantize(s - 1)
@@ -431,8 +441,11 @@ def tile_ia3scaledqknormkeybackwardtoinput_x1_kernel(tc, ds, q, u, gamma, l, wk,
             if early:
                 dz_quantize(s - 1)
             rows_product(s - 1)
-            planes_product(2 * s - 2)
-            planes_product(2 * s - 1)
+            count = 3 - len(squares[s]) if s in squares else 3 if s >= CATCH else 2
+            halves = list(range(half, min(half + count, 2 * s)))
+            half += len(halves)
+            for j in halves:
+                planes_product(j)
             for i in squares.get(s, []):
                 square(i)
             rooted = [last_square[i] for i in squares.get(s, []) if i in last_square]
@@ -442,16 +455,19 @@ def tile_ia3scaledqknormkeybackwardtoinput_x1_kernel(tc, ds, q, u, gamma, l, wk,
             rows_out(s - 1, 0, on_scalar)
             for c in rooted:
                 square_root_again(c)
-            planes_out(2 * s - 1, on_scalar)
-            if s < last - 1:
-                planes_out(2 * s - 2, on_scalar)
+            order = halves[1::-1] + halves[2:]
+            if s == last - 1:
+                kept = order.pop()
+            for j in order:
+                planes_out(j, on_scalar)
             ready[s] = len(filled)
 
         reduce_rows(last)
         scale_u(last, nc.vector)
         times_l(last - 1)
         turn(last)
-        planes_out(2 * last - 4, on_vector)
+        assert half == 2 * last - 2
+        planes_out(kept, on_vector)
         dz_quantize(last - 1)
         rows_product(last - 1)
         planes_product(2 * last - 2)

@@ -18,29 +18,27 @@ ACT = mybir.ActivationFunctionType
 P = 128
 EPS = 1e-6
 TILES = M // P
-UNIT = 2 * P
-DS_CHUNKS = [(0, 256), (256, 256), (512, 512), (1024, 1024)]
-U_CHUNKS = [(0, 2), (2, 2), (4, 4), (8, 8)]
-STAT_GROUPS = [(a, 2) for a in range(0, TILES, 2)]
-DS_GROUPS = [(0, 1), (1, 1)] + [(a, 2) for a in range(2, TILES, 2)]
-Q_VECTOR = 96
-DS_VECTOR = 224
-WAIT = 2
-DS_LATE = 224
-SPLIT = 16
-PRO = 1
-TWO = 0
-CATCH = 12
-STOPQ = 15
-E1 = 1
-E2 = 1
-D3 = 64
-SCALE_STORES = {1: 0, 4: 7}
+LAST = TILES - 1
+PAIR = 2 * P
+
+DS_LOADS = [(0, 256), (256, 256), (512, 512), (1024, 1024)]
+U_LOADS = [(0, 2), (2, 2), (4, 4), (8, 8)]
+GROUPS = [(0, 1), (1, 1)] + [(a, 2) for a in range(2, TILES, 2)]
 PLANE_GROUPS = [(0, 3), (3, 4), (7, 4), (11, 3), (14, 2)]
+SCALE_STORES = {2: 0, 4: 11}
+Q_VECTOR = (96, 80)
+DS_VECTOR_EARLY = 64
+DS_VECTOR = 224
+
+
+def place_in(groups, i):
+    k = [n for n, (a, w) in enumerate(groups) if a <= i < a + w][0]
+    return k, i - groups[k][0]
 
 
 def tile_ia3scaledqknormkeybackwardtoinput_x1_kernel(tc, ds, q, u, gamma, l, wk, out_0, out_1, out_2):
     nc = tc.nc
+    on_vector, on_scalar = nc.vector.tensor_copy, nc.scalar.copy
     with ExitStack() as ctx:
         keep = ctx.enter_context(tc.tile_pool(name="keep", bufs=1))
         work = ctx.enter_context(tc.tile_pool(name="work", bufs=3))
@@ -51,8 +49,8 @@ def tile_ia3scaledqknormkeybackwardtoinput_x1_kernel(tc, ds, q, u, gamma, l, wk,
             return work.tile(shape, dtype, bufs=TILES, name="wide", align_bytes=64)
 
         q_raw = [wide([P, 4, D], BF16) for g in range(2)]
-        ds_raw = [keep.tile([P, 2, 4, w], BF16, name="ds_raw%d" % c) for c, (a, w) in enumerate(DS_CHUNKS)]
-        u_raw = [keep.tile([P, w, D], BF16, name="u_raw%d" % c) for c, (a, w) in enumerate(U_CHUNKS)]
+        ds_raw = [keep.tile([P, 2, 4, w], BF16, name="ds_raw%d" % c) for c, (a, w) in enumerate(DS_LOADS)]
+        u_raw = [keep.tile([P, w, D], BF16, name="u_raw%d" % c) for c, (a, w) in enumerate(U_LOADS)]
         wk_raw = [wide([P, 4 * D], BF16) for g in range(2)]
         l_col = keep.tile([P, 4], BF16, name="l_col")
         g_col = keep.tile([P, 4], BF16, name="g_col")
@@ -63,7 +61,7 @@ def tile_ia3scaledqknormkeybackwardtoinput_x1_kernel(tc, ds, q, u, gamma, l, wk,
             nc.sync.dma_start(out=q_raw[g][:], in_=q[512 * g : 512 * (g + 1), :].rearrange("(p j) d -> p j d", j=4))
 
         def load_ds(c, passes=(0, 1)):
-            a, w = DS_CHUNKS[c]
+            a, w = DS_LOADS[c]
             for g in passes:
                 nc.sync.dma_start(
                     out=ds_raw[c][:, g, :, :],
@@ -71,7 +69,7 @@ def tile_ia3scaledqknormkeybackwardtoinput_x1_kernel(tc, ds, q, u, gamma, l, wk,
                 )
 
         def load_u(c):
-            a, w = U_CHUNKS[c]
+            a, w = U_LOADS[c]
             nc.sync.dma_start(out=u_raw[c][:], in_=u[a * P : (a + w) * P, :].rearrange("(i p) d -> p i d", i=w))
 
         def load_wk(g):
@@ -99,28 +97,30 @@ def tile_ia3scaledqknormkeybackwardtoinput_x1_kernel(tc, ds, q, u, gamma, l, wk,
         load_ds(3)
         load_u(3)
 
-        ssq = [keep.tile([P, w], F32, name="ssq%d" % c) for c, (a, w) in enumerate(STAT_GROUPS)]
-        rinv = [keep.tile([P, w], F32, name="rinv%d" % c) for c, (a, w) in enumerate(STAT_GROUPS)]
-        rr = [keep.tile([P, w], F32, name="rr%d" % c) for c, (a, w) in enumerate(STAT_GROUPS)]
-        group_of = [c for c, (a, w) in enumerate(STAT_GROUPS) for i in range(w)]
+        ssq = [keep.tile([P, w], F32, name="ssq%d" % c) for c, (a, w) in enumerate(GROUPS)]
+        r1 = [keep.tile([P, w], F32, name="r1_%d" % c) for c, (a, w) in enumerate(GROUPS)]
+        r2 = [keep.tile([P, w], F32, name="r2_%d" % c) for c, (a, w) in enumerate(GROUPS)]
 
         def column(x, i):
-            j = i - STAT_GROUPS[group_of[i]][0]
-            return x[group_of[i]][:, j : j + 1]
+            c, j = place_in(GROUPS, i)
+            return x[c][:, j : j + 1]
 
         def u_rows(i):
-            c = [n for n, (a, w) in enumerate(U_CHUNKS) if a <= i < a + w][0]
-            return u_raw[c][:, i - U_CHUNKS[c][0], :]
+            c, j = place_in(U_LOADS, i)
+            return u_raw[c][:, j, :]
 
-        def square(i):
-            sq = work.tile([P, D], BF16, bufs=1, name="sq")
-            nc.scalar.activation(sq[:], u_rows(i), ACT.Square, accum_out=column(ssq, i))
+        def u_slots(i):
+            return u_rows(i).rearrange("m (p t) -> m t p", t=4)
 
-        def take_root(c):
-            nc.scalar.activation(rinv[c][:], ssq[c][:], ACT.Abs_reciprocal_sqrt, bias=D * EPS)
+        def sum_squares(i):
+            squares = work.tile([P, D], BF16, bufs=1, name="squares")
+            nc.scalar.activation(squares[:], u_rows(i), ACT.Square, accum_out=column(ssq, i))
 
-        def square_root_again(c):
-            nc.scalar.activation(rr[c][:], rinv[c][:], ACT.Square)
+        def inverse_root(c):
+            nc.scalar.activation(r1[c][:], ssq[c][:], ACT.Abs_reciprocal_sqrt, bias=D * EPS)
+
+        def square_of_root(c):
+            nc.scalar.activation(r2[c][:], r1[c][:], ACT.Square)
 
         qg = [wide([P, D, 4], BF16) for g in range(2)]
         qc = keep.tile([P, 2, D], U32, name="qc", align_bytes=64)
@@ -129,49 +129,49 @@ def tile_ia3scaledqknormkeybackwardtoinput_x1_kernel(tc, ds, q, u, gamma, l, wk,
         def q_interleave(g):
             dst = qg[g][:].rearrange("p (t c) j -> p t c j", t=4)
             src = q_raw[g][:].rearrange("p j (c t) -> p t c j", t=4)
-            nc.vector.tensor_copy(out=dst[:, :, 0:Q_VECTOR, :], in_=src[:, :, 0:Q_VECTOR, :])
-            nc.scalar.copy(dst[:, :, Q_VECTOR:P, :], src[:, :, Q_VECTOR:P, :])
+            share = Q_VECTOR[g]
+            on_vector(dst[:, :, 0:share, :], src[:, :, 0:share, :])
+            on_scalar(dst[:, :, share:P, :], src[:, :, share:P, :])
 
         def q_quantize(g):
             nc.vector.quantize_mx(
-                out=qc[:, g, :].bitcast(X4), scales=qs[:, g, :], in_=qg[g][:].rearrange("p c t -> p (c t)")
+                out=qc[:, g, :].bitcast(X4), scales=qs[:, g, :], in_=qg[g][:].rearrange("p c j -> p (c j)")
             )
 
         dsg, dsc, dss = {}, {}, {}
+        pass0, pass1, both = slice(0, 1), slice(1, 2), slice(0, 2)
 
-        ds_group_of = [k for k, (a, w) in enumerate(DS_GROUPS) for i in range(w)]
-
-        def ds_interleave(k, copy, passes=slice(0, 2), part=None):
-            first, width = DS_GROUPS[k][0] * P, DS_GROUPS[k][1] * P
-            c = [n for n, (a, w) in enumerate(DS_CHUNKS) if a <= first < a + w][0]
-            off = first - DS_CHUNKS[c][0]
-            lo, hi = part or (0, width)
+        def ds_interleave(k, copy, passes, lo, hi):
+            c, off = place_in(DS_LOADS, GROUPS[k][0] * P)
             if k not in dsg:
-                dsg[k] = work.tile([P, 2, width, 4], BF16, name="dsg", align_bytes=64)
+                dsg[k] = work.tile([P, 2, GROUPS[k][1] * P, 4], BF16, name="dsg", align_bytes=64)
             copy(
-                dsg[k][:, passes, lo:hi, :].rearrange("p g (c i) t -> p g c t i", i=4),
-                ds_raw[c][:, passes, :, off + lo : off + hi].rearrange("p g t (c i) -> p g c t i", i=4),
+                dsg[k][:, passes, lo:hi, :].rearrange("p g (c i) j -> p g c j i", i=4),
+                ds_raw[c][:, passes, :, off + lo : off + hi].rearrange("p g j (c i) -> p g c j i", i=4),
             )
 
-        def ds_quantize(k, passes=slice(0, 2)):
-            width = DS_GROUPS[k][1] * P
+        def ds_interleave_shared(k, share):
+            ds_interleave(k, on_vector, both, 0, share)
+            ds_interleave(k, on_scalar, both, share, PAIR)
+
+        def ds_quantize(k, passes=both):
             if k not in dsc:
-                dsc[k] = work.tile([P, 2, width], U32, name="dsc", align_bytes=64)
-                dss[k] = work.tile([P, 2, width], U8, name="dss", align_bytes=64)
+                dsc[k] = work.tile([P, 2, GROUPS[k][1] * P], U32, name="dsc", align_bytes=64)
+                dss[k] = work.tile([P, 2, GROUPS[k][1] * P], U8, name="dss", align_bytes=64)
             nc.vector.quantize_mx(
                 out=dsc[k][:, passes, :].rearrange("p g c -> p (g c)").bitcast(X4),
                 scales=dss[k][:, passes, :].rearrange("p g c -> p (g c)"),
-                in_=dsg[k][:, passes, :, :].rearrange("p g c t -> p (g c t)"),
+                in_=dsg[k][:, passes, :, :].rearrange("p g c j -> p (g c j)"),
             )
 
         gam = keep.tile([P, 4, P], F32, name="gam")
 
         def spread_gamma():
-            bank = psum.tile([P, 2, P], F32, name="tr")
+            bank = psum.tile([P, 2, P], F32, name="turned")
             words = g_col[:].bitcast(F32)
             for w in range(2):
                 nc.tensor.transpose(bank[:, w, :], words[:, w : w + 1].to_broadcast([P, P]), ident[:])
-            nc.scalar.copy(
+            on_scalar(
                 gam[:].rearrange("x (w e) p -> x w e p", e=2),
                 bank[:].bitcast(BF16).rearrange("x w (p e) -> x w e p", e=2),
             )
@@ -179,22 +179,26 @@ def tile_ia3scaledqknormkeybackwardtoinput_x1_kernel(tc, ds, q, u, gamma, l, wk,
         wg = [wide([P, 512, 4], BF16) for g in range(2)]
         wkc = keep.tile([P, E], U32, name="wkc", align_bytes=64)
         wks = keep.tile([P, E], U8, name="wks", align_bytes=64)
-
         wb = {}
+
+        def rows_bank(shape):
+            return psum.tile(shape, F32, name="rows_bank")
+
+        def planes_bank(shape):
+            return psum.tile(shape, F32, bufs=3, name="planes_bank")
 
         def wk_turn(g):
             words = wk_raw[g][:].bitcast(F32)
-            for b, tag in enumerate(("ob", "pb")):
-                bank = psum.tile([P, 2, 2, P], F32, bufs=2 + b, name=tag)
+            for b, take in enumerate((rows_bank, planes_bank)):
+                wb[g, b] = take([P, 2, 2, P])
                 for a in range(2):
-                    base = (2 * b + a) * 256
+                    row = (2 * b + a) * 256
                     for w in range(2):
-                        nc.tensor.transpose(bank[:, a, w, :], words[:, base + w : base + 256 : 2], ident[:])
-                wb[g, b] = bank
+                        nc.tensor.transpose(wb[g, b][:, a, w, :], words[:, row + w : row + 256 : 2], ident[:])
 
         def wk_out(g, b):
             dst = wg[g][:, 256 * b : 256 * (b + 1), :].rearrange("p c k -> p (c k)").bitcast(F32)
-            nc.scalar.copy(dst.rearrange("p (a c w) -> p a c w", a=2, w=2), wb[g, b][:].rearrange("p a w c -> p a c w"))
+            on_scalar(dst.rearrange("p (a c w) -> p a c w", a=2, w=2), wb[g, b][:].rearrange("p a w c -> p a c w"))
 
         def wk_quantize(g):
             cols = slice(512 * g, 512 * (g + 1))
@@ -202,17 +206,18 @@ def tile_ia3scaledqknormkeybackwardtoinput_x1_kernel(tc, ds, q, u, gamma, l, wk,
                 out=wkc[:, cols].bitcast(X4), scales=wks[:, cols], in_=wg[g][:].rearrange("p c k -> p (c k)")
             )
 
-        dk, gr, cu, coef, tr, dzg, ob, rows, pb, pg = {}, {}, {}, {}, {}, {}, {}, {}, {}, {}
+        dk, big_g, minus_cu, coef, turned, dzg = {}, {}, {}, {}, {}, {}
+        row_sums, rows, plane_sums, plane_in, plane_codes = {}, {}, {}, {}, {}
         dzc = [keep.tile([P, P], U32, name="dzc%d" % i, align_bytes=64) for i in range(TILES)]
         dzs = [keep.tile([P, P], U8, name="dzs%d" % i, align_bytes=64) for i in range(TILES)]
-        filled, pc, done, stored = [], {}, set(), set()
-        pls = keep.tile([P, 2, M], U8, name="pls", align_bytes=64)
+        plane_scales = keep.tile([P, 2, M], U8, name="plane_scales", align_bytes=64)
 
-        def first_product(i):
-            k = ds_group_of[i]
-            cols = slice((i - DS_GROUPS[k][0]) * P, (i - DS_GROUPS[k][0] + 1) * P)
-            dk[i] = psum.tile([P, D], F32, bufs=1, name="dk")
-            for g in range(2):
+        def first_product(i, passes=(0, 1)):
+            k, j = place_in(GROUPS, i)
+            cols = slice(j * P, (j + 1) * P)
+            if i not in dk:
+                dk[i] = psum.tile([P, D], F32, bufs=1, name="dk")
+            for g in passes:
                 nc.tensor.matmul_mx(
                     out=dk[i][:],
                     lhsT=dsc[k][:, g, cols].bitcast(X4),
@@ -223,41 +228,41 @@ def tile_ia3scaledqknormkeybackwardtoinput_x1_kernel(tc, ds, q, u, gamma, l, wk,
                     stop=(g == 1),
                 )
 
-        def scale_dk(i):
-            gr[i] = work.tile([P, 4, P], F32, name="gr")
+        def make_g(i):
+            big_g[i] = work.tile([P, 4, P], F32, name="big_g")
             nc.vector.scalar_tensor_tensor(
-                gr[i][:], dk[i][:].rearrange("m (t p) -> m t p", t=4), column(rinv, i), gam[:], ALU.mult, ALU.mult
+                big_g[i][:], dk[i][:].rearrange("m (t p) -> m t p", t=4), column(r1, i), gam[:], ALU.mult, ALU.mult
             )
 
-        def reduce_rows(i):
-            prod = work.tile([P, 4, P], BF16, bufs=1, name="prod")
+        def make_c(i):
+            terms = work.tile([P, 4, P], BF16, bufs=1, name="terms")
             coef[i] = work.tile([P, 1], F32, bufs=TILES, name="coef")
             nc.vector.scalar_tensor_tensor(
-                prod[:],
-                gr[i][:],
-                column(rr, i),
-                u_rows(i).rearrange("m (p t) -> m t p", t=4),
-                ALU.mult,
-                ALU.mult,
-                accum_out=coef[i][:],
+                terms[:], big_g[i][:], column(r2, i), u_slots(i), ALU.mult, ALU.mult, accum_out=coef[i][:]
             )
 
-        def scale_u(i, engine):
-            cu[i] = work.tile([P, 4, P], F32, name="cu")
-            src = u_rows(i).rearrange("m (p t) -> m t p", t=4)
-            engine.tensor_scalar(cu[i][:], src, coef[i][:], -1.0, ALU.mult, ALU.mult)
+        def make_minus_cu(i, engine):
+            minus_cu[i] = work.tile([P, 4, P], F32, name="minus_cu")
+            engine.tensor_scalar(minus_cu[i][:], u_slots(i), coef[i][:], -1.0, ALU.mult, ALU.mult)
 
         def turn(i):
-            tr[i] = psum.tile([P, 4, P], F32, name="tr")
-            for t in range(4):
-                nc.tensor.matmul(tr[i][:, t, :], gr[i][:, t, :], ident[:], start=True, stop=False, is_transpose=True)
-                nc.tensor.matmul(tr[i][:, t, :], cu[i][:, t, :], ident[:], start=False, stop=True, is_transpose=True)
+            turned[i] = psum.tile([P, 4, P], F32, name="turned")
+            for n, x in enumerate((big_g[i], minus_cu[i])):
+                for t in range(4):
+                    nc.tensor.matmul(
+                        turned[i][:, t, :],
+                        x[:, t, :],
+                        ident[:],
+                        start=(n == 0 and t == 0),
+                        stop=(n == 1 and t == 3),
+                        is_transpose=True,
+                    )
 
         def times_l(i):
             dzg[i] = work.tile([P, P, 4], BF16, name="dzg", align_bytes=64)
             nc.vector.tensor_tensor(
                 dzg[i][:],
-                tr[i][:].rearrange("p t m -> p m t"),
+                turned[i][:].rearrange("p t m -> p m t"),
                 l_col[:].unsqueeze(1).to_broadcast([P, P, 4]),
                 ALU.mult,
             )
@@ -270,9 +275,9 @@ def tile_ia3scaledqknormkeybackwardtoinput_x1_kernel(tc, ds, q, u, gamma, l, wk,
         def rows_product(i):
             for g in range(2):
                 cols = slice(g * 512, (g + 1) * 512)
-                ob[i, g] = psum.tile([P, 4, P], F32, name="ob")
+                row_sums[i, g] = rows_bank([P, 4, P])
                 nc.tensor.matmul_mx(
-                    out=ob[i, g][:].rearrange("m t p -> m (t p)"),
+                    out=row_sums[i, g][:].rearrange("m t p -> m (t p)"),
                     lhsT=dzc[i][:].bitcast(X4),
                     lhsT_scale=dzs[i][:],
                     rhs=wkc[:, cols].bitcast(X4),
@@ -281,210 +286,200 @@ def tile_ia3scaledqknormkeybackwardtoinput_x1_kernel(tc, ds, q, u, gamma, l, wk,
                     stop=True,
                 )
 
-        def rows_out(i, g, copy):
+        def rows_out(i, g):
             if i not in rows:
                 rows[i] = wide([P, 2, P, 4], F32)
-            copy(rows[i][:, g, :, :], ob[i, g][:].rearrange("m t p -> m p t"))
-            stored.add((i, g))
-            if i >= SPLIT:
-                nc.sync.dma_start(
-                    out=out_0[i * P : (i + 1) * P, 512 * g : 512 * (g + 1)],
-                    in_=rows[i][:, g, :, :].rearrange("m p t -> m (p t)"),
+            on_scalar(rows[i][:, g, :, :], row_sums[i, g][:].rearrange("m t p -> m p t"))
+
+        def rows_store(i, halves=both):
+            nc.sync.dma_start(
+                out=out_0[i * P : (i + 1) * P, 512 * halves.start : 512 * halves.stop],
+                in_=rows[i][:, halves, :, :].rearrange("m g p t -> m (g p t)"),
+            )
+
+        def planes_product(i):
+            for g in range(2):
+                plane_sums[i, g] = planes_bank([P, 4, P])
+                for t in range(4):
+                    cols = slice(g * 512 + t * P, g * 512 + (t + 1) * P)
+                    nc.tensor.matmul_mx(
+                        out=plane_sums[i, g][:, t, :],
+                        lhsT=wkc[:, cols].bitcast(X4),
+                        lhsT_scale=wks[:, cols],
+                        rhs=dzc[i][:].bitcast(X4),
+                        rhs_scale=dzs[i][:],
+                        start=True,
+                        stop=True,
+                    )
+
+        def planes_out(i, g, copy):
+            k, j = place_in(PLANE_GROUPS, i)
+            if j == 0:
+                plane_in[k, g] = work.tile(
+                    [P, PLANE_GROUPS[k][1] * P, 4], BF16, bufs=6, name="plane_in", align_bytes=64
                 )
-            elif (i, 1 - g) in stored:
-                nc.sync.dma_start(out=out_0[i * P : (i + 1) * P, :], in_=rows[i][:].rearrange("m g p t -> m (g p t)"))
-
-        def planes_product(j):
-            i, g = divmod(j, 2)
-            pb[j] = psum.tile([P, 4, P], F32, bufs=3, name="pb")
-            for t in range(4):
-                cols = slice(g * 512 + t * P, g * 512 + (t + 1) * P)
-                nc.tensor.matmul_mx(
-                    out=pb[j][:, t, :],
-                    lhsT=wkc[:, cols].bitcast(X4),
-                    lhsT_scale=wks[:, cols],
-                    rhs=dzc[i][:].bitcast(X4),
-                    rhs_scale=dzs[i][:],
-                    start=True,
-                    stop=True,
-                )
-
-        plane_group_of = [k for k, (a, w) in enumerate(PLANE_GROUPS) for i in range(w)]
-
-        def planes_out(j, copy):
-            i, g = divmod(j, 2)
-            k = plane_group_of[i]
-            a, w = PLANE_GROUPS[k]
-            if i == a:
-                pg[k, g] = work.tile([P, w * P, 4], BF16, bufs=6, name="pg", align_bytes=64)
-            copy(pg[k, g][:, (i - a) * P : (i - a + 1) * P, :], pb[j][:].rearrange("p t m -> p m t"))
-            if i == a + w - 1:
-                filled.append((k, g))
+            copy(plane_in[k, g][:, j * P : (j + 1) * P, :], plane_sums[i, g][:].rearrange("p t m -> p m t"))
 
         def planes_quantize(k, g):
             a, w = PLANE_GROUPS[k]
-            cols = slice(a * P, (a + w) * P)
-            if k not in pc:
-                pc[k] = work.tile([P, 2, w * P], U32, bufs=len(PLANE_GROUPS), name="pc", align_bytes=64)
-            nc.vector.quantize_mx(
-                out=pc[k][:, g, :].bitcast(X4), scales=pls[:, g, cols], in_=pg[k, g][:].rearrange("p m t -> p (m t)")
-            )
-            done.add((k, g))
-            if (k, 1 - g) in done:
-                nc.sync.dma_start(
-                    out=out_1[:, :, cols, :].rearrange("g p m t -> p g (m t)").bitcast(I32), in_=pc[k][:].bitcast(I32)
+            if k not in plane_codes:
+                plane_codes[k] = work.tile(
+                    [P, 2, w * P], U32, bufs=len(PLANE_GROUPS), name="plane_codes", align_bytes=64
                 )
-            if (k, 1 - g) in done and k in SCALE_STORES:
+            nc.vector.quantize_mx(
+                out=plane_codes[k][:, g, :].bitcast(X4),
+                scales=plane_scales[:, g, a * P : (a + w) * P],
+                in_=plane_in[k, g][:].rearrange("p m t -> p (m t)"),
+            )
+
+        def planes_store(k):
+            a, w = PLANE_GROUPS[k]
+            nc.sync.dma_start(
+                out=out_1[:, :, a * P : (a + w) * P, :].rearrange("g p m t -> p g (m t)").bitcast(I32),
+                in_=plane_codes[k][:].bitcast(I32),
+            )
+            if k in SCALE_STORES:
                 cols = slice(SCALE_STORES[k] * P, (a + w) * P)
                 for quad in range(4):
                     nc.sync.dma_start(
                         out=out_2[:, 4 * quad : 4 * quad + 4, cols].rearrange("g r m -> r g m").bitcast(I32),
-                        in_=pls[32 * quad : 32 * quad + 4, :, cols].bitcast(I32),
+                        in_=plane_scales[32 * quad : 32 * quad + 4, :, cols].bitcast(I32),
                     )
 
-        on_vector, on_scalar = nc.vector.tensor_copy, nc.scalar.copy
-
-        def quantize_filled(upto):
-            for k, g in filled[:upto]:
-                planes_quantize(k, g)
-            filled[:upto] = []
-
         q_interleave(0)
-        ds_interleave(0, on_scalar, slice(0, 1))
+        ds_interleave(0, on_vector, pass0, 0, P)
         q_quantize(0)
         spread_gamma()
+        ds_interleave(1, on_scalar, pass0, 0, P)
         q_interleave(1)
-        ds_interleave(1, on_scalar, slice(0, 1))
-        ds_interleave(0, on_vector, slice(1, 2))
+        ds_quantize(0, pass0)
+        first_product(0, (0,))
+        ds_interleave(0, on_vector, pass1, 0, P)
         q_quantize(1)
-        square(0)
-        square(1)
-        ds_quantize(0)
-        take_root(0)
-        first_product(0)
-        ds_interleave(1, on_vector, slice(1, 2))
-        square_root_again(0)
-        ds_interleave(2, on_scalar)
+        sum_squares(0)
+        sum_squares(1)
+        ds_quantize(0, pass1)
+        inverse_root(0)
+        inverse_root(1)
+        first_product(0, (1,))
+        ds_interleave(1, on_vector, pass1, 0, P)
+        square_of_root(0)
+        square_of_root(1)
+        ds_interleave(2, on_vector, pass0, 0, DS_VECTOR_EARLY)
+        ds_interleave(2, on_scalar, both, DS_VECTOR_EARLY, PAIR)
         ds_quantize(1)
-        scale_dk(0)
+        make_g(0)
+        ds_interleave(2, on_vector, pass1, 0, DS_VECTOR_EARLY)
         first_product(1)
-        square(2)
-        square(3)
+
+        sum_squares(2)
+        sum_squares(3)
         wk_turn(0)
-        reduce_rows(0)
-        scale_dk(1)
-        scale_u(0, nc.vector)
+        make_c(0)
+        make_g(1)
+        make_minus_cu(0, nc.vector)
         turn(0)
         wk_out(0, 0)
-        take_root(1)
+        inverse_root(2)
         wk_out(0, 1)
-        square_root_again(1)
+        square_of_root(2)
         ds_quantize(2)
         first_product(2)
+
         wk_turn(1)
-        reduce_rows(1)
-        scale_u(1, nc.gpsimd)
+        make_c(1)
+        make_minus_cu(1, nc.gpsimd)
         times_l(0)
-        scale_dk(2)
+        make_g(2)
         turn(1)
         first_product(3)
         wk_out(1, 0)
         wk_out(1, 1)
         wk_quantize(0)
         dz_quantize(0)
-        ds_interleave(3, on_vector, part=(0, D3))
-        ds_interleave(3, on_scalar, part=(D3, UNIT))
+        ds_interleave_shared(3, DS_VECTOR_EARLY)
         wk_quantize(1)
         rows_product(0)
-        for j in range(2 * PRO):
-            planes_product(j)
-        square(4)
-        square(5)
-        rows_out(0, 1, on_scalar)
-        take_root(2)
-        rows_out(0, 0, on_scalar)
-        square_root_again(2)
-        for j in reversed(range(2 * PRO)):
-            planes_out(j, on_scalar)
+        planes_product(0)
+        sum_squares(4)
+        sum_squares(5)
+        rows_out(0, 1)
+        inverse_root(3)
+        rows_out(0, 0)
+        rows_store(0)
+        square_of_root(3)
+        planes_out(0, 1, on_scalar)
+        planes_out(0, 0, on_scalar)
 
-        squares = {2 + s: [6 + 2 * s, 7 + 2 * s] for s in range(TWO)}
-        squares.update({s: [s + 4 + TWO] for s in range(2 + TWO, TILES - 4 - TWO)})
-        half = 2 * PRO
-        last_square = {sum(STAT_GROUPS[c]) - 1: c for c in range(len(STAT_GROUPS))}
-        last = TILES - 1
-        ready = {}
-        for s in range(2, last):
-            reduce_rows(s)
-            scale_u(s, nc.gpsimd)
-            scale_dk(s + 1)
-            if 2 < s < TILES - 2:
+        waiting = [(k, g) for k in range(len(PLANE_GROUPS)) for g in (1, 0)]
+        for s in range(2, LAST):
+            make_c(s)
+            make_minus_cu(s, nc.gpsimd)
+            make_g(s + 1)
+            if 2 < s < LAST - 1:
                 first_product(s + 2)
             times_l(s - 1)
             turn(s)
             if s == 2:
-                ds_quantize(ds_group_of[s + 2])
-                first_product(s + 2)
+                ds_quantize(3)
+                first_product(4)
             if s % 2 == 1 and s + 3 < TILES:
-                ds_quantize(ds_group_of[s + 3])
+                ds_quantize(place_in(GROUPS, s + 3)[0])
             if s % 2 == 0 and s + 4 < TILES:
-                share = DS_VECTOR if s in squares else DS_LATE
-                ds_interleave(ds_group_of[s + 4], on_vector, part=(0, share))
-                if share < UNIT:
-                    ds_interleave(ds_group_of[s + 4], on_scalar, part=(share, UNIT))
-            early = s + 4 >= TILES and s % 2 == 0 or s + 3 >= TILES
-            if not early:
+                ds_interleave_shared(place_in(GROUPS, s + 4)[0], DS_VECTOR)
+            ds_work = s + 4 < TILES
+            if ds_work:
                 dz_quantize(s - 1)
-            if ready.get(s - WAIT, 0) > 0 and (s % 2 == 1 or s + 4 >= TILES) and s < STOPQ:
-                quantize_filled(1)
-                for earlier in ready:
-                    ready[earlier] -= 1
-            if early:
+            k, g = waiting[0]
+            if (s % 2 == 1 or not ds_work) and sum(PLANE_GROUPS[k]) + 2 <= s:
+                waiting.remove((k, g))
+                planes_quantize(k, g)
+                if g == 0:
+                    planes_store(k)
+            if not ds_work:
                 dz_quantize(s - 1)
             rows_product(s - 1)
-            count = 3 - len(squares[s]) if s in squares else 3 if s >= CATCH else 2
-            halves = list(range(half, min(half + count, 2 * s)))
-            half += len(halves)
-            for j in halves:
-                planes_product(j)
-            for i in squares.get(s, []):
-                square(i)
-            rooted = [last_square[i] for i in squares.get(s, []) if i in last_square]
-            rows_out(s - 1, 1, on_scalar)
-            for c in rooted:
-                take_root(c)
-            rows_out(s - 1, 0, on_scalar)
-            for c in rooted:
-                square_root_again(c)
-            order = halves[1::-1] + halves[2:]
-            if s == last - 1:
-                kept = order.pop()
-            for j in order:
-                planes_out(j, on_scalar)
-            ready[s] = len(filled)
+            planes_product(s - 1)
+            ahead = s + 4
+            group_done = ahead < TILES and ahead % 2 == 1
+            if ahead < TILES:
+                sum_squares(ahead)
+            rows_out(s - 1, 1)
+            if group_done:
+                inverse_root(place_in(GROUPS, ahead)[0])
+            rows_out(s - 1, 0)
+            rows_store(s - 1)
+            if group_done:
+                square_of_root(place_in(GROUPS, ahead)[0])
+            planes_out(s - 1, 1, on_scalar)
+            planes_out(s - 1, 0, on_scalar)
 
-        reduce_rows(last)
-        scale_u(last, nc.vector)
-        times_l(last - 1)
-        turn(last)
-        assert half == 2 * last - 2
-        planes_out(kept, on_vector)
-        dz_quantize(last - 1)
-        rows_product(last - 1)
-        planes_product(2 * last - 2)
-        planes_product(2 * last - 1)
-        times_l(last)
-        quantize_filled(E1)
-        rows_out(last - 1, 0, on_scalar)
-        rows_out(last - 1, 1, on_scalar)
-        dz_quantize(last)
-        planes_out(2 * last - 2, on_vector)
-        rows_product(last)
-        planes_out(2 * last - 1, on_vector)
-        planes_product(2 * last)
-        planes_product(2 * last + 1)
-        quantize_filled(len(filled))
-        rows_out(last, 0, on_scalar)
-        rows_out(last, 1, on_scalar)
-        planes_out(2 * last, on_vector)
-        planes_out(2 * last + 1, on_scalar)
-        quantize_filled(len(filled))
+        before, final = len(PLANE_GROUPS) - 2, len(PLANE_GROUPS) - 1
+        make_c(LAST)
+        make_minus_cu(LAST, nc.vector)
+        times_l(LAST - 1)
+        turn(LAST)
+        dz_quantize(LAST - 1)
+        rows_product(LAST - 1)
+        planes_product(LAST - 1)
+        times_l(LAST)
+        planes_quantize(before, 1)
+        rows_out(LAST - 1, 0)
+        rows_store(LAST - 1, pass0)
+        rows_out(LAST - 1, 1)
+        rows_store(LAST - 1, pass1)
+        dz_quantize(LAST)
+        planes_out(LAST - 1, 0, on_vector)
+        rows_product(LAST)
+        planes_out(LAST - 1, 1, on_vector)
+        planes_product(LAST)
+        planes_quantize(before, 0)
+        planes_store(before)
+        rows_out(LAST, 0)
+        rows_out(LAST, 1)
+        rows_store(LAST)
+        planes_out(LAST, 0, on_vector)
+        planes_out(LAST, 1, on_scalar)
+        planes_quantize(final, 0)
+        planes_quantize(final, 1)
+        planes_store(final)

@@ -21,11 +21,11 @@ TILES = M // P
 LAST = TILES - 1
 PAIR = 2 * P
 
-DS_LOADS = [(0, 256), (256, 256), (512, 512), (1024, 1024)]
-U_LOADS = [(0, 2), (2, 2), (4, 4), (8, 8)]
+DS_LOADS = [(0, 256), (256, 256), (512, 256), (768, 256), (1024, 1024)]
+U_LOADS = [(0, 2), (2, 2), (4, 2), (6, 2), (8, 8)]
 GROUPS = [(0, 1), (1, 1)] + [(a, 2) for a in range(2, TILES, 2)]
-PLANE_GROUPS = [(0, 3), (3, 4), (7, 4), (11, 3), (14, 2)]
-SCALE_STORES = {2: 0, 4: 11}
+PLANE_GROUPS = [(0, 3), (3, 4), (7, 3), (10, 2), (12, 2), (14, 2)]
+SCALE_STORES = {2: 0, 5: 10}
 Q_VECTOR = (96, 80)
 DS_VECTOR_EARLY = 64
 DS_VECTOR = 224
@@ -89,13 +89,12 @@ def tile_ia3scaledqknormkeybackwardtoinput_x1_kernel(tc, ds, q, u, gamma, l, wk,
         load_ds(0, (1,))
         load_u(0)
         load_ds(1)
-        load_u(1)
         load_wk(0)
+        load_u(1)
         load_wk(1)
-        load_ds(2)
-        load_u(2)
-        load_ds(3)
-        load_u(3)
+        for c in range(2, len(DS_LOADS)):
+            load_ds(c)
+            load_u(c)
 
         ssq = [keep.tile([P, w], F32, name="ssq%d" % c) for c, (a, w) in enumerate(GROUPS)]
         r1 = [keep.tile([P, w], F32, name="r1_%d" % c) for c, (a, w) in enumerate(GROUPS)]
@@ -127,11 +126,11 @@ def tile_ia3scaledqknormkeybackwardtoinput_x1_kernel(tc, ds, q, u, gamma, l, wk,
         qs = keep.tile([P, 2, D], U8, name="qs", align_bytes=64)
 
         def q_interleave(g):
-            dst = qg[g][:].rearrange("p (t c) j -> p t c j", t=4)
-            src = q_raw[g][:].rearrange("p j (c t) -> p t c j", t=4)
+            dst = qg[g][:].rearrange("p (t c) j -> p c j t", t=4)
+            src = q_raw[g][:].rearrange("p j (c t) -> p c j t", t=4)
             share = Q_VECTOR[g]
-            on_vector(dst[:, :, 0:share, :], src[:, :, 0:share, :])
-            on_scalar(dst[:, :, share:P, :], src[:, :, share:P, :])
+            on_vector(dst[:, 0:share, :, :], src[:, 0:share, :, :])
+            on_scalar(dst[:, share:P, :, :], src[:, share:P, :, :])
 
         def q_quantize(g):
             nc.vector.quantize_mx(
@@ -452,15 +451,19 @@ def tile_ia3scaledqknormkeybackwardtoinput_x1_kernel(tc, ds, q, u, gamma, l, wk,
             if group_done:
                 square_of_root(place_in(GROUPS, ahead)[0])
             planes_out(s - 1, 1, on_scalar)
-            planes_out(s - 1, 0, on_scalar)
+            if s < LAST - 1:
+                planes_out(s - 1, 0, on_scalar)
 
         before, final = len(PLANE_GROUPS) - 2, len(PLANE_GROUPS) - 1
         make_c(LAST)
         make_minus_cu(LAST, nc.vector)
         times_l(LAST - 1)
         turn(LAST)
+        planes_quantize(before - 1, 0)
+        planes_store(before - 1)
         dz_quantize(LAST - 1)
         rows_product(LAST - 1)
+        planes_out(LAST - 2, 0, on_vector)
         planes_product(LAST - 1)
         times_l(LAST)
         planes_quantize(before, 1)

@@ -21,14 +21,17 @@ TILES = M // P
 LAST = TILES - 1
 PAIR = 2 * P
 
-DS_LOADS = [(0, 256), (256, 256), (512, 256), (768, 256), (1024, 1024)]
+DS_LOADS = [(0, 256), (256, 256), (512, 256), (768, 256), (1024, 512), (1536, 512)]
 U_LOADS = [(0, 2), (2, 2), (4, 2), (6, 2), (8, 8)]
-GROUPS = [(0, 1), (1, 1)] + [(a, 2) for a in range(2, TILES, 2)]
+ROOT_GROUPS = [(0, 1), (1, 1), (2, 2), (4, 2), (6, 2), (8, 2), (10, 2), (12, 2), (14, 2)]
 PLANE_GROUPS = [(0, 3), (3, 4), (7, 3), (10, 2), (12, 2), (14, 2)]
 SCALE_STORES = {2: 0, 5: 10}
-Q_VECTOR = (96, 80)
+Q_VECTOR = (96, 64)
 DS_VECTOR_EARLY = 64
-DS_VECTOR = 224
+DS_VECTOR_EARLY2 = 96
+AHEAD = 4
+PLANE_LAG = 2
+DS_VECTOR = 216
 
 
 def place_in(groups, i):
@@ -92,16 +95,17 @@ def tile_ia3scaledqknormkeybackwardtoinput_x1_kernel(tc, ds, q, u, gamma, l, wk,
         load_wk(0)
         load_u(1)
         load_wk(1)
-        for c in range(2, len(DS_LOADS)):
+        for c in range(2, len(U_LOADS)):
             load_ds(c)
             load_u(c)
+        load_ds(5)
 
-        ssq = [keep.tile([P, w], F32, name="ssq%d" % c) for c, (a, w) in enumerate(GROUPS)]
-        r1 = [keep.tile([P, w], F32, name="r1_%d" % c) for c, (a, w) in enumerate(GROUPS)]
-        r2 = [keep.tile([P, w], F32, name="r2_%d" % c) for c, (a, w) in enumerate(GROUPS)]
+        ssq = [keep.tile([P, w], F32, name="ssq%d" % c) for c, (a, w) in enumerate(ROOT_GROUPS)]
+        r1 = [keep.tile([P, w], F32, name="r1_%d" % c) for c, (a, w) in enumerate(ROOT_GROUPS)]
+        r2 = [keep.tile([P, w], F32, name="r2_%d" % c) for c, (a, w) in enumerate(ROOT_GROUPS)]
 
         def column(x, i):
-            c, j = place_in(GROUPS, i)
+            c, j = place_in(ROOT_GROUPS, i)
             return x[c][:, j : j + 1]
 
         def u_rows(i):
@@ -112,7 +116,7 @@ def tile_ia3scaledqknormkeybackwardtoinput_x1_kernel(tc, ds, q, u, gamma, l, wk,
             return u_rows(i).rearrange("m (p t) -> m t p", t=4)
 
         def sum_squares(i):
-            squares = work.tile([P, D], BF16, bufs=1, name="squares")
+            squares = work.tile([P, D], BF16, bufs=4, name="squares")
             nc.scalar.activation(squares[:], u_rows(i), ACT.Square, accum_out=column(ssq, i))
 
         def inverse_root(c):
@@ -141,26 +145,22 @@ def tile_ia3scaledqknormkeybackwardtoinput_x1_kernel(tc, ds, q, u, gamma, l, wk,
         pass0, pass1, both = slice(0, 1), slice(1, 2), slice(0, 2)
 
         def ds_interleave(k, copy, passes, lo, hi):
-            c, off = place_in(DS_LOADS, GROUPS[k][0] * P)
+            c, off = place_in(DS_LOADS, k * PAIR)
             if k not in dsg:
-                dsg[k] = work.tile([P, 2, GROUPS[k][1] * P, 4], BF16, name="dsg", align_bytes=64)
+                dsg[k] = work.tile([P, 2, PAIR, 4], BF16, name="dsg", align_bytes=64)
             copy(
                 dsg[k][:, passes, lo:hi, :].rearrange("p g (c i) j -> p g c j i", i=4),
                 ds_raw[c][:, passes, :, off + lo : off + hi].rearrange("p g j (c i) -> p g c j i", i=4),
             )
 
-        def ds_interleave_shared(k, share):
-            ds_interleave(k, on_vector, both, 0, share)
-            ds_interleave(k, on_scalar, both, share, PAIR)
-
-        def ds_quantize(k, passes=both):
+        def ds_quantize(k, passes=both, keys=slice(0, PAIR)):
             if k not in dsc:
-                dsc[k] = work.tile([P, 2, GROUPS[k][1] * P], U32, name="dsc", align_bytes=64)
-                dss[k] = work.tile([P, 2, GROUPS[k][1] * P], U8, name="dss", align_bytes=64)
+                dsc[k] = work.tile([P, 2, PAIR], U32, name="dsc", align_bytes=64)
+                dss[k] = work.tile([P, 2, PAIR], U8, name="dss", align_bytes=64)
             nc.vector.quantize_mx(
-                out=dsc[k][:, passes, :].rearrange("p g c -> p (g c)").bitcast(X4),
-                scales=dss[k][:, passes, :].rearrange("p g c -> p (g c)"),
-                in_=dsg[k][:, passes, :, :].rearrange("p g c j -> p (g c j)"),
+                out=dsc[k][:, passes, keys].rearrange("p g c -> p (g c)").bitcast(X4),
+                scales=dss[k][:, passes, keys].rearrange("p g c -> p (g c)"),
+                in_=dsg[k][:, passes, keys, :].rearrange("p g c j -> p (g c j)"),
             )
 
         gam = keep.tile([P, 4, P], F32, name="gam")
@@ -211,11 +211,14 @@ def tile_ia3scaledqknormkeybackwardtoinput_x1_kernel(tc, ds, q, u, gamma, l, wk,
         dzs = [keep.tile([P, P], U8, name="dzs%d" % i, align_bytes=64) for i in range(TILES)]
         plane_scales = keep.tile([P, 2, M], U8, name="plane_scales", align_bytes=64)
 
-        def first_product(i, passes=(0, 1)):
-            k, j = place_in(GROUPS, i)
+        def dk_bank(shape):
+            return psum.tile(shape, F32, bufs=1, name="dk")
+
+        def first_product(i, passes=(0, 1), take=dk_bank):
+            k, j = divmod(i, 2)
             cols = slice(j * P, (j + 1) * P)
             if i not in dk:
-                dk[i] = psum.tile([P, D], F32, bufs=1, name="dk")
+                dk[i] = take([P, D])
             for g in passes:
                 nc.tensor.matmul_mx(
                     out=dk[i][:],
@@ -271,10 +274,13 @@ def tile_ia3scaledqknormkeybackwardtoinput_x1_kernel(tc, ds, q, u, gamma, l, wk,
                 out=dzc[i][:].bitcast(X4), scales=dzs[i][:], in_=dzg[i][:].rearrange("p m t -> p (m t)")
             )
 
-        def rows_product(i):
+        def turned_bank(shape):
+            return psum.tile(shape, F32, name="turned")
+
+        def rows_product(i, take=rows_bank):
             for g in range(2):
                 cols = slice(g * 512, (g + 1) * 512)
-                row_sums[i, g] = rows_bank([P, 4, P])
+                row_sums[i, g] = take([P, 4, P])
                 nc.tensor.matmul_mx(
                     out=row_sums[i, g][:].rearrange("m t p -> m (t p)"),
                     lhsT=dzc[i][:].bitcast(X4),
@@ -285,10 +291,10 @@ def tile_ia3scaledqknormkeybackwardtoinput_x1_kernel(tc, ds, q, u, gamma, l, wk,
                     stop=True,
                 )
 
-        def rows_out(i, g):
+        def rows_out(i, g, copy=on_scalar):
             if i not in rows:
                 rows[i] = wide([P, 2, P, 4], F32)
-            on_scalar(rows[i][:, g, :, :], row_sums[i, g][:].rearrange("m t p -> m p t"))
+            copy(rows[i][:, g, :, :], row_sums[i, g][:].rearrange("m t p -> m p t"))
 
         def rows_store(i, halves=both):
             nc.sync.dma_start(
@@ -296,9 +302,9 @@ def tile_ia3scaledqknormkeybackwardtoinput_x1_kernel(tc, ds, q, u, gamma, l, wk,
                 in_=rows[i][:, halves, :, :].rearrange("m g p t -> m (g p t)"),
             )
 
-        def planes_product(i):
-            for g in range(2):
-                plane_sums[i, g] = planes_bank([P, 4, P])
+        def planes_product(i, takes=(planes_bank, planes_bank)):
+            for g, take in enumerate(takes):
+                plane_sums[i, g] = take([P, 4, P])
                 for t in range(4):
                     cols = slice(g * 512 + t * P, g * 512 + (t + 1) * P)
                     nc.tensor.matmul_mx(
@@ -349,59 +355,62 @@ def tile_ia3scaledqknormkeybackwardtoinput_x1_kernel(tc, ds, q, u, gamma, l, wk,
         ds_interleave(0, on_vector, pass0, 0, P)
         q_quantize(0)
         spread_gamma()
-        ds_interleave(1, on_scalar, pass0, 0, P)
+        ds_interleave(0, on_scalar, pass0, P, PAIR)
         q_interleave(1)
         ds_quantize(0, pass0)
         first_product(0, (0,))
+        first_product(1, (0,), planes_bank)
         ds_interleave(0, on_vector, pass1, 0, P)
         q_quantize(1)
         sum_squares(0)
         sum_squares(1)
-        ds_quantize(0, pass1)
-        inverse_root(0)
-        inverse_root(1)
+        ds_quantize(0, pass1, slice(0, P))
         first_product(0, (1,))
-        ds_interleave(1, on_vector, pass1, 0, P)
+        inverse_root(0)
+        ds_interleave(0, on_vector, pass1, P, PAIR)
+        ds_interleave(1, on_vector, pass0, 0, DS_VECTOR_EARLY)
+        ds_quantize(0, pass1, slice(P, PAIR))
+        first_product(1, (1,))
+        ds_interleave(1, on_scalar, pass0, DS_VECTOR_EARLY, PAIR)
         square_of_root(0)
-        square_of_root(1)
-        ds_interleave(2, on_vector, pass0, 0, DS_VECTOR_EARLY)
-        ds_interleave(2, on_scalar, both, DS_VECTOR_EARLY, PAIR)
-        ds_quantize(1)
+        inverse_root(1)
         make_g(0)
-        ds_interleave(2, on_vector, pass1, 0, DS_VECTOR_EARLY)
-        first_product(1)
-
-        sum_squares(2)
-        sum_squares(3)
+        ds_interleave(1, on_vector, pass1, 0, DS_VECTOR_EARLY)
+        ds_interleave(1, on_scalar, pass1, DS_VECTOR_EARLY, PAIR)
+        square_of_root(1)
         wk_turn(0)
         make_c(0)
         make_g(1)
         make_minus_cu(0, nc.vector)
         turn(0)
+        ds_quantize(1)
+        first_product(2)
+        sum_squares(2)
+        sum_squares(3)
         wk_out(0, 0)
         inverse_root(2)
         wk_out(0, 1)
         square_of_root(2)
-        ds_quantize(2)
-        first_product(2)
-
-        wk_turn(1)
         make_c(1)
-        make_minus_cu(1, nc.gpsimd)
         times_l(0)
+        make_minus_cu(1, nc.vector)
+        wk_quantize(0)
         make_g(2)
+        wk_turn(1)
         turn(1)
         first_product(3)
+        ds_interleave(2, on_scalar, both, DS_VECTOR_EARLY2, PAIR)
         wk_out(1, 0)
         wk_out(1, 1)
-        wk_quantize(0)
+        ds_interleave(2, on_vector, both, 0, DS_VECTOR_EARLY2)
         dz_quantize(0)
-        ds_interleave_shared(3, DS_VECTOR_EARLY)
+        ds_quantize(2)
         wk_quantize(1)
         rows_product(0)
         planes_product(0)
         sum_squares(4)
         sum_squares(5)
+        ds_interleave(3, on_scalar, both, DS_VECTOR, PAIR)
         rows_out(0, 1)
         inverse_root(3)
         rows_out(0, 0)
@@ -411,78 +420,88 @@ def tile_ia3scaledqknormkeybackwardtoinput_x1_kernel(tc, ds, q, u, gamma, l, wk,
         planes_out(0, 0, on_scalar)
 
         waiting = [(k, g) for k in range(len(PLANE_GROUPS)) for g in (1, 0)]
+
+        def next_planes():
+            k, g = waiting[0]
+            waiting.remove((k, g))
+            planes_quantize(k, g)
+            if g == 0:
+                planes_store(k)
+
         for s in range(2, LAST):
             make_c(s)
             make_minus_cu(s, nc.gpsimd)
             make_g(s + 1)
-            if 2 < s < LAST - 1:
+            if s + 2 < TILES:
                 first_product(s + 2)
             times_l(s - 1)
             turn(s)
-            if s == 2:
-                ds_quantize(3)
-                first_product(4)
             if s % 2 == 1 and s + 3 < TILES:
-                ds_quantize(place_in(GROUPS, s + 3)[0])
+                ds_quantize((s + 3) // 2)
             if s % 2 == 0 and s + 4 < TILES:
-                ds_interleave_shared(place_in(GROUPS, s + 4)[0], DS_VECTOR)
+                ds_interleave((s + 4) // 2, on_vector, both, 0, DS_VECTOR)
             ds_work = s + 4 < TILES
             if ds_work:
                 dz_quantize(s - 1)
-            k, g = waiting[0]
-            if (s % 2 == 1 or not ds_work) and sum(PLANE_GROUPS[k]) + 2 <= s:
-                waiting.remove((k, g))
-                planes_quantize(k, g)
-                if g == 0:
-                    planes_store(k)
+            if (s % 2 == 1 or not ds_work) and sum(PLANE_GROUPS[waiting[0][0]]) + 2 <= s:
+                next_planes()
             if not ds_work:
                 dz_quantize(s - 1)
             rows_product(s - 1)
+            if s == LAST - 1:
+                break
             planes_product(s - 1)
-            ahead = s + 4
-            group_done = ahead < TILES and ahead % 2 == 1
+            ahead = s + AHEAD
+            group = place_in(ROOT_GROUPS, min(ahead, LAST))[0]
+            group_done = sum(ROOT_GROUPS[group]) == ahead + 1
             if ahead < TILES:
                 sum_squares(ahead)
+            if s % 2 == 1 and s + 5 < TILES:
+                ds_interleave((s + 5) // 2, on_scalar, both, DS_VECTOR, PAIR)
             rows_out(s - 1, 1)
             if group_done:
-                inverse_root(place_in(GROUPS, ahead)[0])
+                inverse_root(group)
             rows_out(s - 1, 0)
             rows_store(s - 1)
             if group_done:
-                square_of_root(place_in(GROUPS, ahead)[0])
+                square_of_root(group)
             planes_out(s - 1, 1, on_scalar)
-            if s < LAST - 1:
-                planes_out(s - 1, 0, on_scalar)
+            planes_out(s - 1, 0, on_scalar)
 
-        before, final = len(PLANE_GROUPS) - 2, len(PLANE_GROUPS) - 1
+        planes_product(LAST - 2, (planes_bank, dk_bank))
         make_c(LAST)
-        make_minus_cu(LAST, nc.vector)
         times_l(LAST - 1)
-        turn(LAST)
-        planes_quantize(before - 1, 0)
-        planes_store(before - 1)
+        make_minus_cu(LAST, nc.vector)
         dz_quantize(LAST - 1)
-        rows_product(LAST - 1)
+        turn(LAST)
+        next_planes()
+        rows_out(LAST - 2, 0)
+        rows_out(LAST - 2, 1)
+        rows_store(LAST - 2)
         planes_out(LAST - 2, 0, on_vector)
+        rows_product(LAST - 1)
+        planes_out(LAST - 2, 1, on_scalar)
         planes_product(LAST - 1)
         times_l(LAST)
-        planes_quantize(before, 1)
+        left = sorted(waiting)
+        planes_quantize(*left[0])
+        dz_quantize(LAST)
+        rows_product(LAST, turned_bank)
+        planes_product(LAST, (planes_bank, dk_bank))
         rows_out(LAST - 1, 0)
         rows_store(LAST - 1, pass0)
         rows_out(LAST - 1, 1)
         rows_store(LAST - 1, pass1)
-        dz_quantize(LAST)
+        planes_quantize(*left[1])
+        planes_store(left[0][0])
         planes_out(LAST - 1, 0, on_vector)
-        rows_product(LAST)
-        planes_out(LAST - 1, 1, on_vector)
-        planes_product(LAST)
-        planes_quantize(before, 0)
-        planes_store(before)
-        rows_out(LAST, 0)
+        rows_out(LAST, 0, on_vector)
+        rows_store(LAST, pass0)
+        planes_out(LAST - 1, 1, on_scalar)
         rows_out(LAST, 1)
-        rows_store(LAST)
+        rows_store(LAST, pass1)
         planes_out(LAST, 0, on_vector)
         planes_out(LAST, 1, on_scalar)
-        planes_quantize(final, 0)
-        planes_quantize(final, 1)
-        planes_store(final)
+        planes_quantize(*left[2])
+        planes_quantize(*left[3])
+        planes_store(left[2][0])

@@ -24,14 +24,11 @@ PAIR = 2 * P
 DS_LOADS = [(0, 256), (256, 256), (512, 256), (768, 256), (1024, 512), (1536, 512)]
 U_LOADS = [(0, 2), (2, 2), (4, 2), (6, 2), (8, 8)]
 ROOT_GROUPS = [(0, 1), (1, 1), (2, 2), (4, 2), (6, 2), (8, 2), (10, 2), (12, 2), (14, 2)]
-PLANE_GROUPS = [(0, 3), (3, 4), (7, 3), (10, 2), (12, 2), (14, 2)]
-SCALE_STORES = {2: 0, 5: 10}
+PLANE_GROUPS = [(0, 3), (3, 3), (6, 2), (8, 2), (10, 2), (12, 2), (14, 2)]
+SCALE_STORES = {3: 0, 6: 10}
 Q_VECTOR = (96, 64)
 DS_VECTOR_EARLY = 64
-DS_VECTOR_EARLY2 = 96
 AHEAD = 4
-PLANE_LAG = 2
-DS_VECTOR = 216
 
 
 def place_in(groups, i):
@@ -58,6 +55,7 @@ def tile_ia3scaledqknormkeybackwardtoinput_x1_kernel(tc, ds, q, u, gamma, l, wk,
         l_col = keep.tile([P, 4], BF16, name="l_col")
         g_col = keep.tile([P, 4], BF16, name="g_col")
         ident = keep.tile([P, P], F32, name="ident")
+        ident_bf = keep.tile([P, P], BF16, name="ident_bf")
         warm = keep.tile([P, 1], F32, name="warm")
 
         def load_q(g):
@@ -85,16 +83,17 @@ def tile_ia3scaledqknormkeybackwardtoinput_x1_kernel(tc, ds, q, u, gamma, l, wk,
         nc.scalar.dma_start(out=l_col[:], in_=l.rearrange("(p t) -> p t", t=4))
         nc.scalar.activation(warm[:], warm[:], ACT.Abs_reciprocal_sqrt)
         make_identity(nc, ident[:])
+        make_identity(nc, ident_bf[:])
 
         load_q(0)
         load_ds(0, (0,))
         load_q(1)
         load_ds(0, (1,))
         load_u(0)
-        load_ds(1)
         load_wk(0)
-        load_u(1)
+        load_ds(1)
         load_wk(1)
+        load_u(1)
         for c in range(2, len(U_LOADS)):
             load_ds(c)
             load_u(c)
@@ -142,12 +141,13 @@ def tile_ia3scaledqknormkeybackwardtoinput_x1_kernel(tc, ds, q, u, gamma, l, wk,
             )
 
         dsg, dsc, dss = {}, {}, {}
+        one, one_c, one_s, u_sums = {}, {}, {}, {}
         pass0, pass1, both = slice(0, 1), slice(1, 2), slice(0, 2)
 
         def ds_interleave(k, copy, passes, lo, hi):
             c, off = place_in(DS_LOADS, k * PAIR)
             if k not in dsg:
-                dsg[k] = work.tile([P, 2, PAIR, 4], BF16, name="dsg", align_bytes=64)
+                dsg[k] = work.tile([P, 2, PAIR, 4], BF16, bufs=2, name="dsg", align_bytes=64)
             copy(
                 dsg[k][:, passes, lo:hi, :].rearrange("p g (c i) j -> p g c j i", i=4),
                 ds_raw[c][:, passes, :, off + lo : off + hi].rearrange("p g j (c i) -> p g c j i", i=4),
@@ -163,10 +163,33 @@ def tile_ia3scaledqknormkeybackwardtoinput_x1_kernel(tc, ds, q, u, gamma, l, wk,
                 in_=dsg[k][:, passes, keys, :].rearrange("p g c j -> p (g c j)"),
             )
 
+        def tile_interleave(i, copy, lo=0, hi=P):
+            c, off = place_in(DS_LOADS, i * P)
+            if i not in one:
+                one[i] = work.tile([P, 2, P, 4], BF16, bufs=1, name="one", align_bytes=64)
+            copy(one[i][:, :, lo:hi, :], ds_raw[c][:, :, :, off + lo : off + hi])
+
+        def runs_of_four(copy):
+            return lambda dst, src: copy(
+                dst.rearrange("p g (c i) j -> p g c j i", i=4), src.rearrange("p g j (c i) -> p g c j i", i=4)
+            )
+
+        def on_gpsimd(dst, src):
+            nc.gpsimd.tensor_scalar(dst, src.rearrange("p g j m -> p g m j"), 1.0, 0.0, ALU.mult, ALU.add)
+
+        def tile_quantize(i):
+            one_c[i] = work.tile([P, 2, P], U32, name="one_c", align_bytes=64)
+            one_s[i] = work.tile([P, 2, P], U8, name="one_s", align_bytes=64)
+            nc.vector.quantize_mx(
+                out=one_c[i][:].rearrange("p g c -> p (g c)").bitcast(X4),
+                scales=one_s[i][:].rearrange("p g c -> p (g c)"),
+                in_=one[i][:].rearrange("p g c j -> p (g c j)"),
+            )
+
         gam = keep.tile([P, 4, P], F32, name="gam")
 
         def spread_gamma():
-            bank = psum.tile([P, 2, P], F32, name="turned")
+            bank = psum.tile([P, 2, P], F32, bufs=1, name="turned")
             words = g_col[:].bitcast(F32)
             for w in range(2):
                 nc.tensor.transpose(bank[:, w, :], words[:, w : w + 1].to_broadcast([P, P]), ident[:])
@@ -217,13 +240,14 @@ def tile_ia3scaledqknormkeybackwardtoinput_x1_kernel(tc, ds, q, u, gamma, l, wk,
         def first_product(i, passes=(0, 1), take=dk_bank):
             k, j = divmod(i, 2)
             cols = slice(j * P, (j + 1) * P)
+            codes, scales = (one_c[i][:], one_s[i][:]) if i in one_c else (dsc[k][:, :, cols], dss[k][:, :, cols])
             if i not in dk:
                 dk[i] = take([P, D])
             for g in passes:
                 nc.tensor.matmul_mx(
                     out=dk[i][:],
-                    lhsT=dsc[k][:, g, cols].bitcast(X4),
-                    lhsT_scale=dss[k][:, g, cols],
+                    lhsT=codes[:, g, :].bitcast(X4),
+                    lhsT_scale=scales[:, g, :],
                     rhs=qc[:, g, :].bitcast(X4),
                     rhs_scale=qs[:, g, :],
                     start=(g == 0),
@@ -236,11 +260,21 @@ def tile_ia3scaledqknormkeybackwardtoinput_x1_kernel(tc, ds, q, u, gamma, l, wk,
                 big_g[i][:], dk[i][:].rearrange("m (t p) -> m t p", t=4), column(r1, i), gam[:], ALU.mult, ALU.mult
             )
 
+        def u_to_psum(i):
+            u_sums[i] = psum.tile([P, D], F32, bufs=1, name="u_bank")
+            nc.tensor.matmul(u_sums[i][:], ident_bf[:], u_rows(i), start=True, stop=True)
+
         def make_c(i):
             terms = work.tile([P, 4, P], BF16, bufs=1, name="terms")
             coef[i] = work.tile([P, 1], F32, bufs=TILES, name="coef")
             nc.vector.scalar_tensor_tensor(
-                terms[:], big_g[i][:], column(r2, i), u_slots(i), ALU.mult, ALU.mult, accum_out=coef[i][:]
+                terms[:],
+                u_sums[i][:].rearrange("m (p t) -> m t p", t=4) if i in u_sums else u_slots(i),
+                column(r2, i),
+                big_g[i][:],
+                ALU.mult,
+                ALU.mult,
+                accum_out=coef[i][:],
             )
 
         def make_minus_cu(i, engine):
@@ -248,7 +282,7 @@ def tile_ia3scaledqknormkeybackwardtoinput_x1_kernel(tc, ds, q, u, gamma, l, wk,
             engine.tensor_scalar(minus_cu[i][:], u_slots(i), coef[i][:], -1.0, ALU.mult, ALU.mult)
 
         def turn(i):
-            turned[i] = psum.tile([P, 4, P], F32, name="turned")
+            turned[i] = psum.tile([P, 4, P], F32, bufs=1, name="turned")
             for n, x in enumerate((big_g[i], minus_cu[i])):
                 for t in range(4):
                     nc.tensor.matmul(
@@ -275,12 +309,15 @@ def tile_ia3scaledqknormkeybackwardtoinput_x1_kernel(tc, ds, q, u, gamma, l, wk,
             )
 
         def turned_bank(shape):
-            return psum.tile(shape, F32, name="turned")
+            return psum.tile(shape, F32, bufs=1, name="turned")
 
-        def rows_product(i, take=rows_bank):
-            for g in range(2):
+        def u_bank(shape):
+            return psum.tile(shape, F32, bufs=1, name="u_bank")
+
+        def rows_product(i, takes=(rows_bank, rows_bank), halves=(0, 1)):
+            for g in halves:
                 cols = slice(g * 512, (g + 1) * 512)
-                row_sums[i, g] = take([P, 4, P])
+                row_sums[i, g] = takes[g]([P, 4, P])
                 nc.tensor.matmul_mx(
                     out=row_sums[i, g][:].rearrange("m t p -> m (t p)"),
                     lhsT=dzc[i][:].bitcast(X4),
@@ -302,9 +339,9 @@ def tile_ia3scaledqknormkeybackwardtoinput_x1_kernel(tc, ds, q, u, gamma, l, wk,
                 in_=rows[i][:, halves, :, :].rearrange("m g p t -> m (g p t)"),
             )
 
-        def planes_product(i, takes=(planes_bank, planes_bank)):
-            for g, take in enumerate(takes):
-                plane_sums[i, g] = take([P, 4, P])
+        def planes_product(i, takes=(planes_bank, planes_bank), halves=(0, 1)):
+            for g in halves:
+                plane_sums[i, g] = takes[g]([P, 4, P])
                 for t in range(4):
                     cols = slice(g * 512 + t * P, g * 512 + (t + 1) * P)
                     nc.tensor.matmul_mx(
@@ -368,49 +405,49 @@ def tile_ia3scaledqknormkeybackwardtoinput_x1_kernel(tc, ds, q, u, gamma, l, wk,
         first_product(0, (1,))
         inverse_root(0)
         ds_interleave(0, on_vector, pass1, P, PAIR)
-        ds_interleave(1, on_vector, pass0, 0, DS_VECTOR_EARLY)
+        wk_turn(0)
         ds_quantize(0, pass1, slice(P, PAIR))
         first_product(1, (1,))
-        ds_interleave(1, on_scalar, pass0, DS_VECTOR_EARLY, PAIR)
-        square_of_root(0)
+        u_to_psum(1)
         inverse_root(1)
+        square_of_root(0)
         make_g(0)
-        ds_interleave(1, on_vector, pass1, 0, DS_VECTOR_EARLY)
-        ds_interleave(1, on_scalar, pass1, DS_VECTOR_EARLY, PAIR)
+        ds_interleave(1, on_scalar, pass0, DS_VECTOR_EARLY, PAIR)
         square_of_root(1)
-        wk_turn(0)
+        ds_interleave(1, on_vector, pass0, 0, DS_VECTOR_EARLY)
+        ds_interleave(1, on_scalar, pass1, DS_VECTOR_EARLY, PAIR)
         make_c(0)
         make_g(1)
         make_minus_cu(0, nc.vector)
+        ds_interleave(1, on_vector, pass1, 0, DS_VECTOR_EARLY)
+        wk_out(0, 0)
+        wk_out(0, 1)
         turn(0)
+        wk_turn(1)
+        make_c(1)
         ds_quantize(1)
         first_product(2)
         sum_squares(2)
         sum_squares(3)
-        wk_out(0, 0)
+        wk_out(1, 0)
         inverse_root(2)
-        wk_out(0, 1)
+        wk_out(1, 1)
         square_of_root(2)
-        make_c(1)
-        times_l(0)
         make_minus_cu(1, nc.vector)
         wk_quantize(0)
-        make_g(2)
-        wk_turn(1)
+        times_l(0)
+        u_to_psum(2)
         turn(1)
+        make_g(2)
         first_product(3)
-        ds_interleave(2, on_scalar, both, DS_VECTOR_EARLY2, PAIR)
-        wk_out(1, 0)
-        wk_out(1, 1)
-        ds_interleave(2, on_vector, both, 0, DS_VECTOR_EARLY2)
+        tile_interleave(4, runs_of_four(on_scalar))
         dz_quantize(0)
-        ds_quantize(2)
         wk_quantize(1)
+        tile_quantize(4)
         rows_product(0)
         planes_product(0)
         sum_squares(4)
         sum_squares(5)
-        ds_interleave(3, on_scalar, both, DS_VECTOR, PAIR)
         rows_out(0, 1)
         inverse_root(3)
         rows_out(0, 0)
@@ -429,24 +466,29 @@ def tile_ia3scaledqknormkeybackwardtoinput_x1_kernel(tc, ds, q, u, gamma, l, wk,
                 planes_store(k)
 
         for s in range(2, LAST):
+            ds_work = s + 3 < TILES
+            if ds_work:
+                tile_interleave(s + 3, on_gpsimd)
             make_c(s)
-            make_minus_cu(s, nc.gpsimd)
+            if not ds_work:
+                make_minus_cu(s, nc.gpsimd)
             make_g(s + 1)
+            times_l(s - 1)
             if s + 2 < TILES:
                 first_product(s + 2)
-            times_l(s - 1)
-            turn(s)
-            if s % 2 == 1 and s + 3 < TILES:
-                ds_quantize((s + 3) // 2)
-            if s % 2 == 0 and s + 4 < TILES:
-                ds_interleave((s + 4) // 2, on_vector, both, 0, DS_VECTOR)
-            ds_work = s + 4 < TILES
+            if s + 4 < TILES:
+                u_to_psum(s + 1)
+            ready = sum(PLANE_GROUPS[waiting[0][0]]) + 2 <= s
             if ds_work:
-                dz_quantize(s - 1)
-            if (s % 2 == 1 or not ds_work) and sum(PLANE_GROUPS[waiting[0][0]]) + 2 <= s:
+                make_minus_cu(s, nc.vector)
+            else:
                 next_planes()
-            if not ds_work:
-                dz_quantize(s - 1)
+            turn(s)
+            dz_quantize(s - 1)
+            if ds_work:
+                if ready:
+                    next_planes()
+                tile_quantize(s + 3)
             rows_product(s - 1)
             if s == LAST - 1:
                 break
@@ -456,8 +498,6 @@ def tile_ia3scaledqknormkeybackwardtoinput_x1_kernel(tc, ds, q, u, gamma, l, wk,
             group_done = sum(ROOT_GROUPS[group]) == ahead + 1
             if ahead < TILES:
                 sum_squares(ahead)
-            if s % 2 == 1 and s + 5 < TILES:
-                ds_interleave((s + 5) // 2, on_scalar, both, DS_VECTOR, PAIR)
             rows_out(s - 1, 1)
             if group_done:
                 inverse_root(group)
@@ -486,7 +526,7 @@ def tile_ia3scaledqknormkeybackwardtoinput_x1_kernel(tc, ds, q, u, gamma, l, wk,
         left = sorted(waiting)
         planes_quantize(*left[0])
         dz_quantize(LAST)
-        rows_product(LAST, turned_bank)
+        rows_product(LAST, (u_bank, turned_bank))
         planes_product(LAST, (planes_bank, dk_bank))
         rows_out(LAST - 1, 0)
         rows_store(LAST - 1, pass0)

@@ -484,11 +484,11 @@ def tile_ia3scaledqknormkeybackwardtoinput_x1_kernel(tc, ds, q, u, gamma, l, wk,
             else:
                 next_planes()
             turn(s)
-            dz_quantize(s - 1)
             if ds_work:
                 if ready:
                     next_planes()
                 tile_quantize(s + 3)
+            dz_quantize(s - 1)
             rows_product(s - 1)
             if s == LAST - 1:
                 break

@@ -24,8 +24,8 @@ PAIR = 2 * P
 DS_LOADS = [(0, 256), (256, 256), (512, 256), (768, 256), (1024, 512), (1536, 512)]
 U_LOADS = [(0, 2), (2, 2), (4, 2), (6, 2), (8, 8)]
 ROOT_GROUPS = [(0, 1), (1, 1), (2, 2), (4, 2), (6, 2), (8, 2), (10, 2), (12, 2), (14, 2)]
-PLANE_GROUPS = [(0, 3), (3, 3), (6, 2), (8, 2), (10, 2), (12, 2), (14, 2)]
-SCALE_STORES = {3: 0, 6: 10}
+PLANE_GROUPS = [(0, 3), (3, 4), (7, 3), (10, 2), (12, 2), (14, 2)]
+SCALE_STORES = {2: 0, 5: 10}
 Q_VECTOR = (96, 64)
 DS_VECTOR_EARLY = 64
 AHEAD = 4
@@ -84,6 +84,7 @@ def tile_ia3scaledqknormkeybackwardtoinput_x1_kernel(tc, ds, q, u, gamma, l, wk,
         nc.scalar.activation(warm[:], warm[:], ACT.Abs_reciprocal_sqrt)
         make_identity(nc, ident[:])
         make_identity(nc, ident_bf[:])
+        nc.gpsimd.tensor_scalar(ident_bf[:], ident_bf[:], -1.0, 0.0, ALU.mult, ALU.add)
 
         load_q(0)
         load_ds(0, (0,))
@@ -141,7 +142,8 @@ def tile_ia3scaledqknormkeybackwardtoinput_x1_kernel(tc, ds, q, u, gamma, l, wk,
             )
 
         dsg, dsc, dss = {}, {}, {}
-        one, one_c, one_s, u_sums = {}, {}, {}, {}
+        one_c, one_s, u_sums, dzc, dzs = {}, {}, {}, {}, {}
+        stage = keep.tile([P, 4 * D], BF16, name="stage", align_bytes=64)
         pass0, pass1, both = slice(0, 1), slice(1, 2), slice(0, 2)
 
         def ds_interleave(k, copy, passes, lo, hi):
@@ -165,9 +167,8 @@ def tile_ia3scaledqknormkeybackwardtoinput_x1_kernel(tc, ds, q, u, gamma, l, wk,
 
         def tile_interleave(i, copy, lo=0, hi=P):
             c, off = place_in(DS_LOADS, i * P)
-            if i not in one:
-                one[i] = work.tile([P, 2, P, 4], BF16, bufs=1, name="one", align_bytes=64)
-            copy(one[i][:, :, lo:hi, :], ds_raw[c][:, :, :, off + lo : off + hi])
+            dst = stage[:, D : 3 * D].rearrange("p (g m j) -> p g m j", g=2, j=4)
+            copy(dst[:, :, lo:hi, :], ds_raw[c][:, :, :, off + lo : off + hi])
 
         def runs_of_four(copy):
             return lambda dst, src: copy(
@@ -177,14 +178,15 @@ def tile_ia3scaledqknormkeybackwardtoinput_x1_kernel(tc, ds, q, u, gamma, l, wk,
         def on_gpsimd(dst, src):
             nc.gpsimd.tensor_scalar(dst, src.rearrange("p g j m -> p g m j"), 1.0, 0.0, ALU.mult, ALU.add)
 
-        def tile_quantize(i):
-            one_c[i] = work.tile([P, 2, P], U32, name="one_c", align_bytes=64)
-            one_s[i] = work.tile([P, 2, P], U8, name="one_s", align_bytes=64)
-            nc.vector.quantize_mx(
-                out=one_c[i][:].rearrange("p g c -> p (g c)").bitcast(X4),
-                scales=one_s[i][:].rearrange("p g c -> p (g c)"),
-                in_=one[i][:].rearrange("p g c j -> p (g c j)"),
-            )
+        def stage_quantize(s):
+            codes = work.tile([P, 3 * P], U32, name="stage_codes", align_bytes=64)
+            scales = work.tile([P, 3 * P], U8, name="stage_scales", align_bytes=64)
+            first = D * (s % 2)
+            nc.vector.quantize_mx(out=codes[:].bitcast(X4), scales=scales[:], in_=stage[:, first : first + 3 * D])
+            of_dz, of_ds = (slice(2 * P, 3 * P), slice(0, 2 * P)) if s % 2 else (slice(0, P), slice(P, 3 * P))
+            dzc[s - 1], dzs[s - 1] = codes[:, of_dz], scales[:, of_dz]
+            one_c[s + 3] = codes[:, of_ds].rearrange("p (g c) -> p g c", g=2)
+            one_s[s + 3] = scales[:, of_ds].rearrange("p (g c) -> p g c", g=2)
 
         gam = keep.tile([P, 4, P], F32, name="gam")
 
@@ -230,8 +232,6 @@ def tile_ia3scaledqknormkeybackwardtoinput_x1_kernel(tc, ds, q, u, gamma, l, wk,
 
         dk, big_g, minus_cu, coef, turned, dzg = {}, {}, {}, {}, {}, {}
         row_sums, rows, plane_sums, plane_in, plane_codes = {}, {}, {}, {}, {}
-        dzc = [keep.tile([P, P], U32, name="dzc%d" % i, align_bytes=64) for i in range(TILES)]
-        dzs = [keep.tile([P, P], U8, name="dzs%d" % i, align_bytes=64) for i in range(TILES)]
         plane_scales = keep.tile([P, 2, M], U8, name="plane_scales", align_bytes=64)
 
         def dk_bank(shape):
@@ -240,7 +240,7 @@ def tile_ia3scaledqknormkeybackwardtoinput_x1_kernel(tc, ds, q, u, gamma, l, wk,
         def first_product(i, passes=(0, 1), take=dk_bank):
             k, j = divmod(i, 2)
             cols = slice(j * P, (j + 1) * P)
-            codes, scales = (one_c[i][:], one_s[i][:]) if i in one_c else (dsc[k][:, :, cols], dss[k][:, :, cols])
+            codes, scales = (one_c[i], one_s[i]) if i in one_c else (dsc[k][:, :, cols], dss[k][:, :, cols])
             if i not in dk:
                 dk[i] = take([P, D])
             for g in passes:
@@ -270,7 +270,7 @@ def tile_ia3scaledqknormkeybackwardtoinput_x1_kernel(tc, ds, q, u, gamma, l, wk,
             nc.vector.scalar_tensor_tensor(
                 terms[:],
                 u_sums[i][:].rearrange("m (p t) -> m t p", t=4) if i in u_sums else u_slots(i),
-                column(r2, i),
+                column(r1 if i in u_sums else r2, i),
                 big_g[i][:],
                 ALU.mult,
                 ALU.mult,
@@ -279,7 +279,8 @@ def tile_ia3scaledqknormkeybackwardtoinput_x1_kernel(tc, ds, q, u, gamma, l, wk,
 
         def make_minus_cu(i, engine):
             minus_cu[i] = work.tile([P, 4, P], F32, name="minus_cu")
-            engine.tensor_scalar(minus_cu[i][:], u_slots(i), coef[i][:], -1.0, ALU.mult, ALU.mult)
+            factor = column(r1, i) if i in u_sums else -1.0
+            engine.tensor_scalar(minus_cu[i][:], u_slots(i), coef[i][:], factor, ALU.mult, ALU.mult)
 
         def turn(i):
             turned[i] = psum.tile([P, 4, P], F32, bufs=1, name="turned")
@@ -295,18 +296,22 @@ def tile_ia3scaledqknormkeybackwardtoinput_x1_kernel(tc, ds, q, u, gamma, l, wk,
                     )
 
         def times_l(i):
-            dzg[i] = work.tile([P, P, 4], BF16, name="dzg", align_bytes=64)
+            if i + 4 < TILES:
+                first = 3 * D * ((i + 1) % 2)
+                dzg[i] = stage[:, first : first + D].rearrange("p (m t) -> p m t", t=4)
+            else:
+                dzg[i] = work.tile([P, P, 4], BF16, name="dzg", align_bytes=64)[:]
             nc.vector.tensor_tensor(
-                dzg[i][:],
+                dzg[i],
                 turned[i][:].rearrange("p t m -> p m t"),
                 l_col[:].unsqueeze(1).to_broadcast([P, P, 4]),
                 ALU.mult,
             )
 
         def dz_quantize(i):
-            nc.vector.quantize_mx(
-                out=dzc[i][:].bitcast(X4), scales=dzs[i][:], in_=dzg[i][:].rearrange("p m t -> p (m t)")
-            )
+            dzc[i] = work.tile([P, P], U32, name="dz_codes", align_bytes=64)[:]
+            dzs[i] = work.tile([P, P], U8, name="dz_scales", align_bytes=64)[:]
+            nc.vector.quantize_mx(out=dzc[i].bitcast(X4), scales=dzs[i], in_=dzg[i].rearrange("p m t -> p (m t)"))
 
         def turned_bank(shape):
             return psum.tile(shape, F32, bufs=1, name="turned")
@@ -320,8 +325,8 @@ def tile_ia3scaledqknormkeybackwardtoinput_x1_kernel(tc, ds, q, u, gamma, l, wk,
                 row_sums[i, g] = takes[g]([P, 4, P])
                 nc.tensor.matmul_mx(
                     out=row_sums[i, g][:].rearrange("m t p -> m (t p)"),
-                    lhsT=dzc[i][:].bitcast(X4),
-                    lhsT_scale=dzs[i][:],
+                    lhsT=dzc[i].bitcast(X4),
+                    lhsT_scale=dzs[i],
                     rhs=wkc[:, cols].bitcast(X4),
                     rhs_scale=wks[:, cols],
                     start=True,
@@ -348,8 +353,8 @@ def tile_ia3scaledqknormkeybackwardtoinput_x1_kernel(tc, ds, q, u, gamma, l, wk,
                         out=plane_sums[i, g][:, t, :],
                         lhsT=wkc[:, cols].bitcast(X4),
                         lhsT_scale=wks[:, cols],
-                        rhs=dzc[i][:].bitcast(X4),
-                        rhs_scale=dzs[i][:],
+                        rhs=dzc[i].bitcast(X4),
+                        rhs_scale=dzs[i],
                         start=True,
                         stop=True,
                     )
@@ -413,7 +418,6 @@ def tile_ia3scaledqknormkeybackwardtoinput_x1_kernel(tc, ds, q, u, gamma, l, wk,
         square_of_root(0)
         make_g(0)
         ds_interleave(1, on_scalar, pass0, DS_VECTOR_EARLY, PAIR)
-        square_of_root(1)
         ds_interleave(1, on_vector, pass0, 0, DS_VECTOR_EARLY)
         ds_interleave(1, on_scalar, pass1, DS_VECTOR_EARLY, PAIR)
         make_c(0)
@@ -432,7 +436,6 @@ def tile_ia3scaledqknormkeybackwardtoinput_x1_kernel(tc, ds, q, u, gamma, l, wk,
         wk_out(1, 0)
         inverse_root(2)
         wk_out(1, 1)
-        square_of_root(2)
         make_minus_cu(1, nc.vector)
         wk_quantize(0)
         times_l(0)
@@ -441,9 +444,8 @@ def tile_ia3scaledqknormkeybackwardtoinput_x1_kernel(tc, ds, q, u, gamma, l, wk,
         make_g(2)
         first_product(3)
         tile_interleave(4, runs_of_four(on_scalar))
-        dz_quantize(0)
         wk_quantize(1)
-        tile_quantize(4)
+        stage_quantize(1)
         rows_product(0)
         planes_product(0)
         sum_squares(4)
@@ -452,7 +454,6 @@ def tile_ia3scaledqknormkeybackwardtoinput_x1_kernel(tc, ds, q, u, gamma, l, wk,
         inverse_root(3)
         rows_out(0, 0)
         rows_store(0)
-        square_of_root(3)
         planes_out(0, 1, on_scalar)
         planes_out(0, 0, on_scalar)
 
@@ -487,8 +488,9 @@ def tile_ia3scaledqknormkeybackwardtoinput_x1_kernel(tc, ds, q, u, gamma, l, wk,
             if ds_work:
                 if ready:
                     next_planes()
-                tile_quantize(s + 3)
-            dz_quantize(s - 1)
+                stage_quantize(s)
+            else:
+                dz_quantize(s - 1)
             rows_product(s - 1)
             if s == LAST - 1:
                 break
@@ -503,7 +505,7 @@ def tile_ia3scaledqknormkeybackwardtoinput_x1_kernel(tc, ds, q, u, gamma, l, wk,
                 inverse_root(group)
             rows_out(s - 1, 0)
             rows_store(s - 1)
-            if group_done:
+            if group_done and ahead > TILES - 4:
                 square_of_root(group)
             planes_out(s - 1, 1, on_scalar)
             planes_out(s - 1, 0, on_scalar)

@@ -21,8 +21,8 @@ TILES = M // P
 LAST = TILES - 1
 PAIR = 2 * P
 
-DS_LOADS = [(0, 256), (256, 256), (512, 256), (768, 256), (1024, 512), (1536, 512)]
-U_LOADS = [(0, 2), (2, 2), (4, 2), (6, 2), (8, 8)]
+DS_LOADS = [(0, 256), (256, 256), (512, 512), (1024, 512), (1536, 512)]
+U_LOADS = [(0, 2), (2, 2), (4, 4), (8, 8)]
 ROOT_GROUPS = [(0, 1), (1, 1), (2, 2), (4, 2), (6, 2), (8, 2), (10, 2), (12, 2), (14, 2)]
 PLANE_GROUPS = [(0, 3), (3, 4), (7, 3), (10, 2), (12, 2), (14, 2)]
 SCALE_STORES = {2: 0, 5: 10}
@@ -80,11 +80,9 @@ def tile_ia3scaledqknormkeybackwardtoinput_x1_kernel(tc, ds, q, u, gamma, l, wk,
 
         nc.vector.memset(warm[:], 1.0)
         nc.scalar.dma_start(out=g_col[:], in_=gamma.rearrange("(p t) -> p t", t=4))
-        nc.scalar.dma_start(out=l_col[:], in_=l.rearrange("(p t) -> p t", t=4))
         nc.scalar.activation(warm[:], warm[:], ACT.Abs_reciprocal_sqrt)
         make_identity(nc, ident[:])
         make_identity(nc, ident_bf[:])
-        nc.gpsimd.tensor_scalar(ident_bf[:], ident_bf[:], -1.0, 0.0, ALU.mult, ALU.add)
 
         load_q(0)
         load_ds(0, (0,))
@@ -94,11 +92,12 @@ def tile_ia3scaledqknormkeybackwardtoinput_x1_kernel(tc, ds, q, u, gamma, l, wk,
         load_wk(0)
         load_ds(1)
         load_wk(1)
+        nc.sync.dma_start(out=l_col[:], in_=l.rearrange("(p t) -> p t", t=4))
         load_u(1)
         for c in range(2, len(U_LOADS)):
             load_ds(c)
             load_u(c)
-        load_ds(5)
+        load_ds(4)
 
         ssq = [keep.tile([P, w], F32, name="ssq%d" % c) for c, (a, w) in enumerate(ROOT_GROUPS)]
         r1 = [keep.tile([P, w], F32, name="r1_%d" % c) for c, (a, w) in enumerate(ROOT_GROUPS)]
@@ -270,7 +269,7 @@ def tile_ia3scaledqknormkeybackwardtoinput_x1_kernel(tc, ds, q, u, gamma, l, wk,
             nc.vector.scalar_tensor_tensor(
                 terms[:],
                 u_sums[i][:].rearrange("m (p t) -> m t p", t=4) if i in u_sums else u_slots(i),
-                column(r1 if i in u_sums else r2, i),
+                column(r2, i),
                 big_g[i][:],
                 ALU.mult,
                 ALU.mult,
@@ -279,8 +278,7 @@ def tile_ia3scaledqknormkeybackwardtoinput_x1_kernel(tc, ds, q, u, gamma, l, wk,
 
         def make_minus_cu(i, engine):
             minus_cu[i] = work.tile([P, 4, P], F32, name="minus_cu")
-            factor = column(r1, i) if i in u_sums else -1.0
-            engine.tensor_scalar(minus_cu[i][:], u_slots(i), coef[i][:], factor, ALU.mult, ALU.mult)
+            engine.tensor_scalar(minus_cu[i][:], u_slots(i), coef[i][:], -1.0, ALU.mult, ALU.mult)
 
         def turn(i):
             turned[i] = psum.tile([P, 4, P], F32, bufs=1, name="turned")
@@ -418,6 +416,7 @@ def tile_ia3scaledqknormkeybackwardtoinput_x1_kernel(tc, ds, q, u, gamma, l, wk,
         square_of_root(0)
         make_g(0)
         ds_interleave(1, on_scalar, pass0, DS_VECTOR_EARLY, PAIR)
+        square_of_root(1)
         ds_interleave(1, on_vector, pass0, 0, DS_VECTOR_EARLY)
         ds_interleave(1, on_scalar, pass1, DS_VECTOR_EARLY, PAIR)
         make_c(0)
@@ -436,6 +435,7 @@ def tile_ia3scaledqknormkeybackwardtoinput_x1_kernel(tc, ds, q, u, gamma, l, wk,
         wk_out(1, 0)
         inverse_root(2)
         wk_out(1, 1)
+        square_of_root(2)
         make_minus_cu(1, nc.vector)
         wk_quantize(0)
         times_l(0)
@@ -454,6 +454,7 @@ def tile_ia3scaledqknormkeybackwardtoinput_x1_kernel(tc, ds, q, u, gamma, l, wk,
         inverse_root(3)
         rows_out(0, 0)
         rows_store(0)
+        square_of_root(3)
         planes_out(0, 1, on_scalar)
         planes_out(0, 0, on_scalar)
 
@@ -477,7 +478,7 @@ def tile_ia3scaledqknormkeybackwardtoinput_x1_kernel(tc, ds, q, u, gamma, l, wk,
             times_l(s - 1)
             if s + 2 < TILES:
                 first_product(s + 2)
-            if s + 4 < TILES:
+            if s + 4 < TILES and s % 2 == 1:
                 u_to_psum(s + 1)
             ready = sum(PLANE_GROUPS[waiting[0][0]]) + 2 <= s
             if ds_work:
@@ -505,7 +506,7 @@ def tile_ia3scaledqknormkeybackwardtoinput_x1_kernel(tc, ds, q, u, gamma, l, wk,
                 inverse_root(group)
             rows_out(s - 1, 0)
             rows_store(s - 1)
-            if group_done and ahead > TILES - 4:
+            if group_done:
                 square_of_root(group)
             planes_out(s - 1, 1, on_scalar)
             planes_out(s - 1, 0, on_scalar)

@@ -23,12 +23,14 @@ PAIR = 2 * P
 
 DS_LOADS = [(0, 256), (256, 256), (512, 512), (1024, 512), (1536, 512)]
 U_LOADS = [(0, 2), (2, 2), (4, 4), (8, 8)]
-ROOT_GROUPS = [(0, 1), (1, 1), (2, 2), (4, 2), (6, 2), (8, 2), (10, 2), (12, 2), (14, 2)]
+ROOT_GROUPS = [(0, 1), (1, 1)] + [(a, 2) for a in range(2, TILES, 2)]
 PLANE_GROUPS = [(0, 3), (3, 4), (7, 3), (10, 2), (12, 2), (14, 2)]
 SCALE_STORES = {2: 0, 5: 10}
 Q_VECTOR = (96, 64)
-DS_VECTOR_EARLY = 64
-AHEAD = 4
+DS_VECTOR = 64
+FIRST_SINGLE = 4
+SQUARES_AHEAD = 4
+CU_VECTOR = 96
 
 
 def place_in(groups, i):
@@ -48,6 +50,21 @@ def tile_ia3scaledqknormkeybackwardtoinput_x1_kernel(tc, ds, q, u, gamma, l, wk,
         def wide(shape, dtype):
             return work.tile(shape, dtype, bufs=TILES, name="wide", align_bytes=64)
 
+        def dk_bank(shape):
+            return psum.tile(shape, F32, bufs=1, name="dk")
+
+        def u_bank(shape):
+            return psum.tile(shape, F32, bufs=1, name="u_bank")
+
+        def turned_bank(shape):
+            return psum.tile(shape, F32, bufs=1, name="turned")
+
+        def rows_bank(shape):
+            return psum.tile(shape, F32, bufs=2, name="rows_bank")
+
+        def planes_bank(shape):
+            return psum.tile(shape, F32, bufs=3, name="planes_bank")
+
         q_raw = [wide([P, 4, D], BF16) for g in range(2)]
         ds_raw = [keep.tile([P, 2, 4, w], BF16, name="ds_raw%d" % c) for c, (a, w) in enumerate(DS_LOADS)]
         u_raw = [keep.tile([P, w, D], BF16, name="u_raw%d" % c) for c, (a, w) in enumerate(U_LOADS)]
@@ -55,7 +72,7 @@ def tile_ia3scaledqknormkeybackwardtoinput_x1_kernel(tc, ds, q, u, gamma, l, wk,
         l_col = keep.tile([P, 4], BF16, name="l_col")
         g_col = keep.tile([P, 4], BF16, name="g_col")
         ident = keep.tile([P, P], F32, name="ident")
-        ident_bf = keep.tile([P, P], BF16, name="ident_bf")
+        minus_one = keep.tile([P, P], BF16, name="minus_one")
         warm = keep.tile([P, 1], F32, name="warm")
 
         def load_q(g):
@@ -82,7 +99,8 @@ def tile_ia3scaledqknormkeybackwardtoinput_x1_kernel(tc, ds, q, u, gamma, l, wk,
         nc.scalar.dma_start(out=g_col[:], in_=gamma.rearrange("(p t) -> p t", t=4))
         nc.scalar.activation(warm[:], warm[:], ACT.Abs_reciprocal_sqrt)
         make_identity(nc, ident[:])
-        make_identity(nc, ident_bf[:])
+        make_identity(nc, minus_one[:])
+        nc.gpsimd.tensor_scalar(minus_one[:], minus_one[:], -1.0, 0.0, ALU.mult, ALU.add)
 
         load_q(0)
         load_ds(0, (0,))
@@ -94,9 +112,10 @@ def tile_ia3scaledqknormkeybackwardtoinput_x1_kernel(tc, ds, q, u, gamma, l, wk,
         load_wk(1)
         nc.sync.dma_start(out=l_col[:], in_=l.rearrange("(p t) -> p t", t=4))
         load_u(1)
-        for c in range(2, len(U_LOADS)):
-            load_ds(c)
-            load_u(c)
+        load_ds(2)
+        load_u(2)
+        load_ds(3)
+        load_u(3)
         load_ds(4)
 
         ssq = [keep.tile([P, w], F32, name="ssq%d" % c) for c, (a, w) in enumerate(ROOT_GROUPS)]
@@ -141,8 +160,6 @@ def tile_ia3scaledqknormkeybackwardtoinput_x1_kernel(tc, ds, q, u, gamma, l, wk,
             )
 
         dsg, dsc, dss = {}, {}, {}
-        one_c, one_s, u_sums, dzc, dzs = {}, {}, {}, {}, {}
-        stage = keep.tile([P, 4 * D], BF16, name="stage", align_bytes=64)
         pass0, pass1, both = slice(0, 1), slice(1, 2), slice(0, 2)
 
         def ds_interleave(k, copy, passes, lo, hi):
@@ -164,33 +181,10 @@ def tile_ia3scaledqknormkeybackwardtoinput_x1_kernel(tc, ds, q, u, gamma, l, wk,
                 in_=dsg[k][:, passes, keys, :].rearrange("p g c j -> p (g c j)"),
             )
 
-        def tile_interleave(i, copy, lo=0, hi=P):
-            c, off = place_in(DS_LOADS, i * P)
-            dst = stage[:, D : 3 * D].rearrange("p (g m j) -> p g m j", g=2, j=4)
-            copy(dst[:, :, lo:hi, :], ds_raw[c][:, :, :, off + lo : off + hi])
-
-        def runs_of_four(copy):
-            return lambda dst, src: copy(
-                dst.rearrange("p g (c i) j -> p g c j i", i=4), src.rearrange("p g j (c i) -> p g c j i", i=4)
-            )
-
-        def on_gpsimd(dst, src):
-            nc.gpsimd.tensor_scalar(dst, src.rearrange("p g j m -> p g m j"), 1.0, 0.0, ALU.mult, ALU.add)
-
-        def stage_quantize(s):
-            codes = work.tile([P, 3 * P], U32, name="stage_codes", align_bytes=64)
-            scales = work.tile([P, 3 * P], U8, name="stage_scales", align_bytes=64)
-            first = D * (s % 2)
-            nc.vector.quantize_mx(out=codes[:].bitcast(X4), scales=scales[:], in_=stage[:, first : first + 3 * D])
-            of_dz, of_ds = (slice(2 * P, 3 * P), slice(0, 2 * P)) if s % 2 else (slice(0, P), slice(P, 3 * P))
-            dzc[s - 1], dzs[s - 1] = codes[:, of_dz], scales[:, of_dz]
-            one_c[s + 3] = codes[:, of_ds].rearrange("p (g c) -> p g c", g=2)
-            one_s[s + 3] = scales[:, of_ds].rearrange("p (g c) -> p g c", g=2)
-
         gam = keep.tile([P, 4, P], F32, name="gam")
 
         def spread_gamma():
-            bank = psum.tile([P, 2, P], F32, bufs=1, name="turned")
+            bank = turned_bank([P, 2, P])
             words = g_col[:].bitcast(F32)
             for w in range(2):
                 nc.tensor.transpose(bank[:, w, :], words[:, w : w + 1].to_broadcast([P, P]), ident[:])
@@ -203,12 +197,6 @@ def tile_ia3scaledqknormkeybackwardtoinput_x1_kernel(tc, ds, q, u, gamma, l, wk,
         wkc = keep.tile([P, E], U32, name="wkc", align_bytes=64)
         wks = keep.tile([P, E], U8, name="wks", align_bytes=64)
         wb = {}
-
-        def rows_bank(shape):
-            return psum.tile(shape, F32, name="rows_bank")
-
-        def planes_bank(shape):
-            return psum.tile(shape, F32, bufs=3, name="planes_bank")
 
         def wk_turn(g):
             words = wk_raw[g][:].bitcast(F32)
@@ -229,17 +217,49 @@ def tile_ia3scaledqknormkeybackwardtoinput_x1_kernel(tc, ds, q, u, gamma, l, wk,
                 out=wkc[:, cols].bitcast(X4), scales=wks[:, cols], in_=wg[g][:].rearrange("p c k -> p (c k)")
             )
 
-        dk, big_g, minus_cu, coef, turned, dzg = {}, {}, {}, {}, {}, {}
+        stage = keep.tile([P, 4 * D], BF16, name="stage", align_bytes=64)
+        tile_c, tile_s, dzc, dzs = {}, {}, {}, {}
+
+        def tile_interleave(i):
+            c, off = place_in(DS_LOADS, i * P)
+            nc.gpsimd.tensor_scalar(
+                stage[:, D : 3 * D].rearrange("p (g m j) -> p g m j", g=2, j=4),
+                ds_raw[c][:, :, :, off : off + P].rearrange("p g j m -> p g m j"),
+                1.0,
+                0.0,
+                ALU.mult,
+                ALU.add,
+            )
+
+        def first_tile_interleave():
+            c, off = place_in(DS_LOADS, FIRST_SINGLE * P)
+            on_scalar(
+                stage[:, D : 3 * D].rearrange("p (g c i j) -> p g c j i", g=2, i=4, j=4),
+                ds_raw[c][:, :, :, off : off + P].rearrange("p g j (c i) -> p g c j i", i=4),
+            )
+
+        def stage_quantize(i):
+            codes = work.tile([P, 3 * P], U32, name="stage_codes", align_bytes=64)
+            scales = work.tile([P, 3 * P], U8, name="stage_scales", align_bytes=64)
+            if i % 2 == 0:
+                cols, of_ds, of_dz = slice(D, 4 * D), slice(0, PAIR), slice(PAIR, 3 * P)
+            else:
+                cols, of_dz, of_ds = slice(0, 3 * D), slice(0, P), slice(P, 3 * P)
+            nc.vector.quantize_mx(out=codes[:].bitcast(X4), scales=scales[:], in_=stage[:, cols])
+            dzc[i], dzs[i] = codes[:, of_dz], scales[:, of_dz]
+            tile_c[i + FIRST_SINGLE] = codes[:, of_ds].rearrange("p (g c) -> p g c", g=2)
+            tile_s[i + FIRST_SINGLE] = scales[:, of_ds].rearrange("p (g c) -> p g c", g=2)
+
+        dk, big_g, minus_u, minus_cu, coef, turned, dzg = {}, {}, {}, {}, {}, {}, {}
         row_sums, rows, plane_sums, plane_in, plane_codes = {}, {}, {}, {}, {}
         plane_scales = keep.tile([P, 2, M], U8, name="plane_scales", align_bytes=64)
 
-        def dk_bank(shape):
-            return psum.tile(shape, F32, bufs=1, name="dk")
-
         def first_product(i, passes=(0, 1), take=dk_bank):
-            k, j = divmod(i, 2)
-            cols = slice(j * P, (j + 1) * P)
-            codes, scales = (one_c[i], one_s[i]) if i in one_c else (dsc[k][:, :, cols], dss[k][:, :, cols])
+            if i < FIRST_SINGLE:
+                k, j = divmod(i, 2)
+                codes, scales = dsc[k][:, :, j * P : (j + 1) * P], dss[k][:, :, j * P : (j + 1) * P]
+            else:
+                codes, scales = tile_c[i], tile_s[i]
             if i not in dk:
                 dk[i] = take([P, D])
             for g in passes:
@@ -260,15 +280,15 @@ def tile_ia3scaledqknormkeybackwardtoinput_x1_kernel(tc, ds, q, u, gamma, l, wk,
             )
 
         def u_to_psum(i):
-            u_sums[i] = psum.tile([P, D], F32, bufs=1, name="u_bank")
-            nc.tensor.matmul(u_sums[i][:], ident_bf[:], u_rows(i), start=True, stop=True)
+            minus_u[i] = u_bank([P, D])
+            nc.tensor.matmul(minus_u[i][:], minus_one[:], u_rows(i), start=True, stop=True)
 
         def make_c(i):
             terms = work.tile([P, 4, P], BF16, bufs=1, name="terms")
             coef[i] = work.tile([P, 1], F32, bufs=TILES, name="coef")
             nc.vector.scalar_tensor_tensor(
                 terms[:],
-                u_sums[i][:].rearrange("m (p t) -> m t p", t=4) if i in u_sums else u_slots(i),
+                minus_u[i][:].rearrange("m (p t) -> m t p", t=4) if i in minus_u else u_slots(i),
                 column(r2, i),
                 big_g[i][:],
                 ALU.mult,
@@ -276,12 +296,21 @@ def tile_ia3scaledqknormkeybackwardtoinput_x1_kernel(tc, ds, q, u, gamma, l, wk,
                 accum_out=coef[i][:],
             )
 
-        def make_minus_cu(i, engine):
-            minus_cu[i] = work.tile([P, 4, P], F32, name="minus_cu")
-            engine.tensor_scalar(minus_cu[i][:], u_slots(i), coef[i][:], -1.0, ALU.mult, ALU.mult)
+        def make_minus_cu(i, engine, cols=slice(0, P)):
+            if i not in minus_cu:
+                minus_cu[i] = work.tile([P, 4, P], F32, name="minus_cu")
+            sign = 1.0 if i in minus_u else -1.0
+            engine.tensor_scalar(
+                minus_cu[i][:, :, cols], u_slots(i)[:, :, cols], coef[i][:], sign, ALU.mult, ALU.mult
+            )
 
-        def turn(i):
-            turned[i] = psum.tile([P, 4, P], F32, bufs=1, name="turned")
+        def rest_of_minus_cu(i):
+            minus_cu[i] = work.tile([P, 4, P], F32, name="minus_cu")
+            cols = slice(CU_VECTOR, P)
+            nc.scalar.activation(minus_cu[i][:, :, cols], u_slots(i)[:, :, cols], ACT.Copy, scale=coef[i][:])
+
+        def turn(i, take=turned_bank):
+            turned[i] = take([P, 4, P])
             for n, x in enumerate((big_g[i], minus_cu[i])):
                 for t in range(4):
                     nc.tensor.matmul(
@@ -294,8 +323,8 @@ def tile_ia3scaledqknormkeybackwardtoinput_x1_kernel(tc, ds, q, u, gamma, l, wk,
                     )
 
         def times_l(i):
-            if i + 4 < TILES:
-                first = 3 * D * ((i + 1) % 2)
+            if i + FIRST_SINGLE < TILES:
+                first = 3 * D if i % 2 == 0 else 0
                 dzg[i] = stage[:, first : first + D].rearrange("p (m t) -> p m t", t=4)
             else:
                 dzg[i] = work.tile([P, P, 4], BF16, name="dzg", align_bytes=64)[:]
@@ -311,14 +340,8 @@ def tile_ia3scaledqknormkeybackwardtoinput_x1_kernel(tc, ds, q, u, gamma, l, wk,
             dzs[i] = work.tile([P, P], U8, name="dz_scales", align_bytes=64)[:]
             nc.vector.quantize_mx(out=dzc[i].bitcast(X4), scales=dzs[i], in_=dzg[i].rearrange("p m t -> p (m t)"))
 
-        def turned_bank(shape):
-            return psum.tile(shape, F32, bufs=1, name="turned")
-
-        def u_bank(shape):
-            return psum.tile(shape, F32, bufs=1, name="u_bank")
-
-        def rows_product(i, takes=(rows_bank, rows_bank), halves=(0, 1)):
-            for g in halves:
+        def rows_product(i, takes=(rows_bank, rows_bank)):
+            for g in range(2):
                 cols = slice(g * 512, (g + 1) * 512)
                 row_sums[i, g] = takes[g]([P, 4, P])
                 nc.tensor.matmul_mx(
@@ -342,8 +365,8 @@ def tile_ia3scaledqknormkeybackwardtoinput_x1_kernel(tc, ds, q, u, gamma, l, wk,
                 in_=rows[i][:, halves, :, :].rearrange("m g p t -> m (g p t)"),
             )
 
-        def planes_product(i, takes=(planes_bank, planes_bank), halves=(0, 1)):
-            for g in halves:
+        def planes_product(i, takes=(planes_bank, planes_bank)):
+            for g in range(2):
                 plane_sums[i, g] = takes[g]([P, 4, P])
                 for t in range(4):
                     cols = slice(g * 512 + t * P, g * 512 + (t + 1) * P)
@@ -391,6 +414,33 @@ def tile_ia3scaledqknormkeybackwardtoinput_x1_kernel(tc, ds, q, u, gamma, l, wk,
                         in_=plane_scales[32 * quad : 32 * quad + 4, :, cols].bitcast(I32),
                     )
 
+        waiting = [(k, g) for k in range(len(PLANE_GROUPS)) for g in (1, 0)]
+
+        def next_planes():
+            k, g = waiting[0]
+            waiting.remove((k, g))
+            planes_quantize(k, g)
+            if g == 0:
+                planes_store(k)
+
+        def empty_banks(i):
+            ahead = i + 1 + SQUARES_AHEAD
+            group = place_in(ROOT_GROUPS, min(ahead, LAST))[0]
+            group_done = sum(ROOT_GROUPS[group]) == ahead + 1
+            if ahead < TILES:
+                sum_squares(ahead)
+            if i + 2 in minus_u and i > 0:
+                rest_of_minus_cu(i + 2)
+            rows_out(i, 1)
+            if group_done:
+                inverse_root(group)
+            rows_out(i, 0)
+            rows_store(i)
+            if group_done:
+                square_of_root(group)
+            planes_out(i, 1, on_scalar)
+            planes_out(i, 0, on_scalar)
+
         q_interleave(0)
         ds_interleave(0, on_vector, pass0, 0, P)
         q_quantize(0)
@@ -411,18 +461,19 @@ def tile_ia3scaledqknormkeybackwardtoinput_x1_kernel(tc, ds, q, u, gamma, l, wk,
         wk_turn(0)
         ds_quantize(0, pass1, slice(P, PAIR))
         first_product(1, (1,))
+
         u_to_psum(1)
         inverse_root(1)
         square_of_root(0)
         make_g(0)
-        ds_interleave(1, on_scalar, pass0, DS_VECTOR_EARLY, PAIR)
+        ds_interleave(1, on_scalar, pass0, DS_VECTOR, PAIR)
         square_of_root(1)
-        ds_interleave(1, on_vector, pass0, 0, DS_VECTOR_EARLY)
-        ds_interleave(1, on_scalar, pass1, DS_VECTOR_EARLY, PAIR)
+        ds_interleave(1, on_vector, pass0, 0, DS_VECTOR)
+        ds_interleave(1, on_scalar, pass1, DS_VECTOR, PAIR)
         make_c(0)
         make_g(1)
         make_minus_cu(0, nc.vector)
-        ds_interleave(1, on_vector, pass1, 0, DS_VECTOR_EARLY)
+        ds_interleave(1, on_vector, pass1, 0, DS_VECTOR)
         wk_out(0, 0)
         wk_out(0, 1)
         turn(0)
@@ -443,80 +494,51 @@ def tile_ia3scaledqknormkeybackwardtoinput_x1_kernel(tc, ds, q, u, gamma, l, wk,
         turn(1)
         make_g(2)
         first_product(3)
-        tile_interleave(4, runs_of_four(on_scalar))
+        first_tile_interleave()
         wk_quantize(1)
-        stage_quantize(1)
+        stage_quantize(0)
         rows_product(0)
         planes_product(0)
         sum_squares(4)
-        sum_squares(5)
-        rows_out(0, 1)
-        inverse_root(3)
-        rows_out(0, 0)
-        rows_store(0)
-        square_of_root(3)
-        planes_out(0, 1, on_scalar)
-        planes_out(0, 0, on_scalar)
-
-        waiting = [(k, g) for k in range(len(PLANE_GROUPS)) for g in (1, 0)]
-
-        def next_planes():
-            k, g = waiting[0]
-            waiting.remove((k, g))
-            planes_quantize(k, g)
-            if g == 0:
-                planes_store(k)
+        empty_banks(0)
 
         for s in range(2, LAST):
-            ds_work = s + 3 < TILES
-            if ds_work:
-                tile_interleave(s + 3, on_gpsimd)
+            ds_left = s - 1 + FIRST_SINGLE < TILES
+            if ds_left:
+                tile_interleave(s - 1 + FIRST_SINGLE)
             make_c(s)
-            if not ds_work:
+            if not ds_left:
                 make_minus_cu(s, nc.gpsimd)
+            if s > 2:
+                empty_banks(s - 2)
             make_g(s + 1)
             times_l(s - 1)
             if s + 2 < TILES:
                 first_product(s + 2)
-            if s + 4 < TILES and s % 2 == 1:
+            if s % 2 == 1 and s + FIRST_SINGLE < TILES:
                 u_to_psum(s + 1)
-            ready = sum(PLANE_GROUPS[waiting[0][0]]) + 2 <= s
-            if ds_work:
-                make_minus_cu(s, nc.vector)
+            planes_ready = sum(PLANE_GROUPS[waiting[0][0]]) + 2 <= s
+            if ds_left:
+                shared = s in minus_u and s > 2
+                make_minus_cu(s, nc.vector, slice(0, CU_VECTOR if shared else P))
+                turn(s)
+                if planes_ready:
+                    next_planes()
+                stage_quantize(s - 1)
             else:
                 next_planes()
-            turn(s)
-            if ds_work:
-                if ready:
-                    next_planes()
-                stage_quantize(s)
-            else:
+                turn(s, u_bank if s % 2 == 1 else turned_bank)
                 dz_quantize(s - 1)
             rows_product(s - 1)
-            if s == LAST - 1:
-                break
-            planes_product(s - 1)
-            ahead = s + AHEAD
-            group = place_in(ROOT_GROUPS, min(ahead, LAST))[0]
-            group_done = sum(ROOT_GROUPS[group]) == ahead + 1
-            if ahead < TILES:
-                sum_squares(ahead)
-            rows_out(s - 1, 1)
-            if group_done:
-                inverse_root(group)
-            rows_out(s - 1, 0)
-            rows_store(s - 1)
-            if group_done:
-                square_of_root(group)
-            planes_out(s - 1, 1, on_scalar)
-            planes_out(s - 1, 0, on_scalar)
+            if s < LAST - 1:
+                planes_product(s - 1)
 
         planes_product(LAST - 2, (planes_bank, dk_bank))
         make_c(LAST)
         times_l(LAST - 1)
         make_minus_cu(LAST, nc.vector)
         dz_quantize(LAST - 1)
-        turn(LAST)
+        turn(LAST, u_bank)
         next_planes()
         rows_out(LAST - 2, 0)
         rows_out(LAST - 2, 1)
@@ -526,8 +548,8 @@ def tile_ia3scaledqknormkeybackwardtoinput_x1_kernel(tc, ds, q, u, gamma, l, wk,
         planes_out(LAST - 2, 1, on_scalar)
         planes_product(LAST - 1)
         times_l(LAST)
-        left = sorted(waiting)
-        planes_quantize(*left[0])
+        last_group = len(PLANE_GROUPS) - 1
+        planes_quantize(last_group - 1, 0)
         dz_quantize(LAST)
         rows_product(LAST, (u_bank, turned_bank))
         planes_product(LAST, (planes_bank, dk_bank))
@@ -535,8 +557,8 @@ def tile_ia3scaledqknormkeybackwardtoinput_x1_kernel(tc, ds, q, u, gamma, l, wk,
         rows_store(LAST - 1, pass0)
         rows_out(LAST - 1, 1)
         rows_store(LAST - 1, pass1)
-        planes_quantize(*left[1])
-        planes_store(left[0][0])
+        planes_quantize(last_group - 1, 1)
+        planes_store(last_group - 1)
         planes_out(LAST - 1, 0, on_vector)
         rows_out(LAST, 0, on_vector)
         rows_store(LAST, pass0)
@@ -545,6 +567,6 @@ def tile_ia3scaledqknormkeybackwardtoinput_x1_kernel(tc, ds, q, u, gamma, l, wk,
         rows_store(LAST, pass1)
         planes_out(LAST, 0, on_vector)
         planes_out(LAST, 1, on_scalar)
-        planes_quantize(*left[2])
-        planes_quantize(*left[3])
-        planes_store(left[2][0])
+        planes_quantize(last_group, 0)
+        planes_quantize(last_group, 1)
+        planes_store(last_group)

@@ -283,6 +283,11 @@ def tile_ia3scaledqknormkeybackwardtoinput_x1_kernel(tc, ds, q, u, gamma, l, wk,
             minus_u[i] = u_bank([P, D])
             nc.tensor.matmul(minus_u[i][:], minus_one[:], u_rows(i), start=True, stop=True)
 
+        def warm_tensor():
+            idle = u_bank([P, D])
+            for n in range(4):
+                nc.tensor.matmul(idle[:], minus_one[:], q_raw[0][:, n, :], start=True, stop=True)
+
         def make_c(i):
             terms = work.tile([P, 4, P], BF16, bufs=1, name="terms")
             coef[i] = work.tile([P, 1], F32, bufs=TILES, name="coef")
@@ -448,6 +453,7 @@ def tile_ia3scaledqknormkeybackwardtoinput_x1_kernel(tc, ds, q, u, gamma, l, wk,
         ds_interleave(0, on_scalar, pass0, P, PAIR)
         q_interleave(1)
         ds_quantize(0, pass0)
+        warm_tensor()
         first_product(0, (0,))
         first_product(1, (0,), planes_bank)
         ds_interleave(0, on_vector, pass1, 0, P)

@@ -231,11 +231,11 @@ def tile_ia3scaledqknormkeybackwardtoinput_x1_kernel(tc, ds, q, u, gamma, l, wk,
                 ALU.add,
             )
 
-        def first_tile_interleave():
+        def first_tile_interleave(g):
             c, off = place_in(DS_LOADS, FIRST_SINGLE * P)
             on_scalar(
-                stage[:, D : 3 * D].rearrange("p (g c i j) -> p g c j i", g=2, i=4, j=4),
-                ds_raw[c][:, :, :, off : off + P].rearrange("p g j (c i) -> p g c j i", i=4),
+                stage[:, (1 + g) * D : (2 + g) * D].rearrange("p (c i j) -> p c j i", i=4, j=4),
+                ds_raw[c][:, g, :, off : off + P].rearrange("p j (c i) -> p c j i", i=4),
             )
 
         def stage_quantize(i):
@@ -500,7 +500,8 @@ def tile_ia3scaledqknormkeybackwardtoinput_x1_kernel(tc, ds, q, u, gamma, l, wk,
         turn(1)
         make_g(2)
         first_product(3)
-        first_tile_interleave()
+        first_tile_interleave(0)
+        first_tile_interleave(1)
         wk_quantize(1)
         stage_quantize(0)
         rows_product(0)

@@ -17,6 +17,7 @@ ACT = mybir.ActivationFunctionType
 
 P = 128
 EPS = 1e-6
+ALIGN = 256
 TILES = M // P
 LAST = TILES - 1
 PAIR = 2 * P
@@ -48,7 +49,7 @@ def tile_ia3scaledqknormkeybackwardtoinput_x1_kernel(tc, ds, q, u, gamma, l, wk,
         ctx.enter_context(tc.manual_schedule())
 
         def wide(shape, dtype):
-            return work.tile(shape, dtype, bufs=TILES, name="wide", align_bytes=64)
+            return work.tile(shape, dtype, bufs=TILES, name="wide", align_bytes=ALIGN)
 
         def dk_bank(shape):
             return psum.tile(shape, F32, bufs=1, name="dk")
@@ -66,13 +67,15 @@ def tile_ia3scaledqknormkeybackwardtoinput_x1_kernel(tc, ds, q, u, gamma, l, wk,
             return psum.tile(shape, F32, bufs=3, name="planes_bank")
 
         q_raw = [wide([P, 4, D], BF16) for g in range(2)]
-        ds_raw = [keep.tile([P, 2, 4, w], BF16, name="ds_raw%d" % c) for c, (a, w) in enumerate(DS_LOADS)]
-        u_raw = [keep.tile([P, w, D], BF16, name="u_raw%d" % c) for c, (a, w) in enumerate(U_LOADS)]
+        ds_raw = [
+            keep.tile([P, 2, 4, w], BF16, name="ds_raw%d" % c, align_bytes=ALIGN) for c, (a, w) in enumerate(DS_LOADS)
+        ]
+        u_raw = [keep.tile([P, w, D], BF16, name="u_raw%d" % c, align_bytes=ALIGN) for c, (a, w) in enumerate(U_LOADS)]
         wk_raw = [wide([P, 4 * D], BF16) for g in range(2)]
         l_col = keep.tile([P, 4], BF16, name="l_col")
         g_col = keep.tile([P, 4], BF16, name="g_col")
-        ident = keep.tile([P, P], F32, name="ident")
-        minus_one = keep.tile([P, P], BF16, name="minus_one")
+        ident = keep.tile([P, P], F32, name="ident", align_bytes=ALIGN)
+        minus_one = keep.tile([P, P], BF16, name="minus_one", align_bytes=ALIGN)
         warm = keep.tile([P, 1], F32, name="warm")
 
         def load_q(g):
@@ -134,7 +137,7 @@ def tile_ia3scaledqknormkeybackwardtoinput_x1_kernel(tc, ds, q, u, gamma, l, wk,
             return u_rows(i).rearrange("m (p t) -> m t p", t=4)
 
         def sum_squares(i):
-            squares = work.tile([P, D], BF16, bufs=4, name="squares")
+            squares = work.tile([P, D], BF16, bufs=4, name="squares", align_bytes=ALIGN)
             nc.scalar.activation(squares[:], u_rows(i), ACT.Square, accum_out=column(ssq, i))
 
         def inverse_root(c):
@@ -144,8 +147,8 @@ def tile_ia3scaledqknormkeybackwardtoinput_x1_kernel(tc, ds, q, u, gamma, l, wk,
             nc.scalar.activation(r2[c][:], r1[c][:], ACT.Square)
 
         qg = [wide([P, D, 4], BF16) for g in range(2)]
-        qc = keep.tile([P, 2, D], U32, name="qc", align_bytes=64)
-        qs = keep.tile([P, 2, D], U8, name="qs", align_bytes=64)
+        qc = keep.tile([P, 2, D], U32, name="qc", align_bytes=ALIGN)
+        qs = keep.tile([P, 2, D], U8, name="qs", align_bytes=ALIGN)
 
         def q_interleave(g):
             dst = qg[g][:].rearrange("p (t c) j -> p c j t", t=4)
@@ -165,7 +168,7 @@ def tile_ia3scaledqknormkeybackwardtoinput_x1_kernel(tc, ds, q, u, gamma, l, wk,
         def ds_interleave(k, copy, passes, lo, hi):
             c, off = place_in(DS_LOADS, k * PAIR)
             if k not in dsg:
-                dsg[k] = work.tile([P, 2, PAIR, 4], BF16, bufs=2, name="dsg", align_bytes=64)
+                dsg[k] = work.tile([P, 2, PAIR, 4], BF16, bufs=2, name="dsg", align_bytes=ALIGN)
             copy(
                 dsg[k][:, passes, lo:hi, :].rearrange("p g (c i) j -> p g c j i", i=4),
                 ds_raw[c][:, passes, :, off + lo : off + hi].rearrange("p g j (c i) -> p g c j i", i=4),
@@ -173,15 +176,15 @@ def tile_ia3scaledqknormkeybackwardtoinput_x1_kernel(tc, ds, q, u, gamma, l, wk,
 
         def ds_quantize(k, passes=both, keys=slice(0, PAIR)):
             if k not in dsc:
-                dsc[k] = work.tile([P, 2, PAIR], U32, name="dsc", align_bytes=64)
-                dss[k] = work.tile([P, 2, PAIR], U8, name="dss", align_bytes=64)
+                dsc[k] = work.tile([P, 2, PAIR], U32, name="dsc", align_bytes=ALIGN)
+                dss[k] = work.tile([P, 2, PAIR], U8, name="dss", align_bytes=ALIGN)
             nc.vector.quantize_mx(
                 out=dsc[k][:, passes, keys].rearrange("p g c -> p (g c)").bitcast(X4),
                 scales=dss[k][:, passes, keys].rearrange("p g c -> p (g c)"),
                 in_=dsg[k][:, passes, keys, :].rearrange("p g c j -> p (g c j)"),
             )
 
-        gam = keep.tile([P, 4, P], F32, name="gam")
+        gam = keep.tile([P, 4, P], F32, name="gam", align_bytes=ALIGN)
 
         def spread_gamma():
             bank = turned_bank([P, 2, P])
@@ -194,8 +197,8 @@ def tile_ia3scaledqknormkeybackwardtoinput_x1_kernel(tc, ds, q, u, gamma, l, wk,
             )
 
         wg = [wide([P, 512, 4], BF16) for g in range(2)]
-        wkc = keep.tile([P, E], U32, name="wkc", align_bytes=64)
-        wks = keep.tile([P, E], U8, name="wks", align_bytes=64)
+        wkc = keep.tile([P, E], U32, name="wkc", align_bytes=ALIGN)
+        wks = keep.tile([P, E], U8, name="wks", align_bytes=ALIGN)
         wb = {}
 
         def wk_turn(g):
@@ -217,7 +220,7 @@ def tile_ia3scaledqknormkeybackwardtoinput_x1_kernel(tc, ds, q, u, gamma, l, wk,
                 out=wkc[:, cols].bitcast(X4), scales=wks[:, cols], in_=wg[g][:].rearrange("p c k -> p (c k)")
             )
 
-        stage = keep.tile([P, 4 * D], BF16, name="stage", align_bytes=64)
+        stage = keep.tile([P, 4 * D], BF16, name="stage", align_bytes=ALIGN)
         tile_c, tile_s, dzc, dzs = {}, {}, {}, {}
 
         def tile_interleave(i):
@@ -239,8 +242,8 @@ def tile_ia3scaledqknormkeybackwardtoinput_x1_kernel(tc, ds, q, u, gamma, l, wk,
             )
 
         def stage_quantize(i):
-            codes = work.tile([P, 3 * P], U32, name="stage_codes", align_bytes=64)
-            scales = work.tile([P, 3 * P], U8, name="stage_scales", align_bytes=64)
+            codes = work.tile([P, 3 * P], U32, name="stage_codes", align_bytes=ALIGN)
+            scales = work.tile([P, 3 * P], U8, name="stage_scales", align_bytes=ALIGN)
             if i % 2 == 0:
                 cols, of_ds, of_dz = slice(D, 4 * D), slice(0, PAIR), slice(PAIR, 3 * P)
             else:
@@ -252,7 +255,7 @@ def tile_ia3scaledqknormkeybackwardtoinput_x1_kernel(tc, ds, q, u, gamma, l, wk,
 
         dk, big_g, minus_u, minus_cu, coef, turned, dzg = {}, {}, {}, {}, {}, {}, {}
         row_sums, rows, plane_sums, plane_in, plane_codes = {}, {}, {}, {}, {}
-        plane_scales = keep.tile([P, 2, M], U8, name="plane_scales", align_bytes=64)
+        plane_scales = keep.tile([P, 2, M], U8, name="plane_scales", align_bytes=ALIGN)
 
         def first_product(i, passes=(0, 1), take=dk_bank):
             if i < FIRST_SINGLE:
@@ -274,7 +277,7 @@ def tile_ia3scaledqknormkeybackwardtoinput_x1_kernel(tc, ds, q, u, gamma, l, wk,
                 )
 
         def make_g(i):
-            big_g[i] = work.tile([P, 4, P], F32, name="big_g")
+            big_g[i] = work.tile([P, 4, P], F32, name="big_g", align_bytes=ALIGN)
             nc.vector.scalar_tensor_tensor(
                 big_g[i][:], dk[i][:].rearrange("m (t p) -> m t p", t=4), column(r1, i), gam[:], ALU.mult, ALU.mult
             )
@@ -289,7 +292,7 @@ def tile_ia3scaledqknormkeybackwardtoinput_x1_kernel(tc, ds, q, u, gamma, l, wk,
                 nc.tensor.matmul(idle[:], minus_one[:], q_raw[0][:, n, :], start=True, stop=True)
 
         def make_c(i):
-            terms = work.tile([P, 4, P], BF16, bufs=1, name="terms")
+            terms = work.tile([P, 4, P], BF16, bufs=1, name="terms", align_bytes=ALIGN)
             coef[i] = work.tile([P, 1], F32, bufs=TILES, name="coef")
             nc.vector.scalar_tensor_tensor(
                 terms[:],
@@ -303,14 +306,14 @@ def tile_ia3scaledqknormkeybackwardtoinput_x1_kernel(tc, ds, q, u, gamma, l, wk,
 
         def make_minus_cu(i, engine, cols=slice(0, P)):
             if i not in minus_cu:
-                minus_cu[i] = work.tile([P, 4, P], F32, name="minus_cu")
+                minus_cu[i] = work.tile([P, 4, P], F32, name="minus_cu", align_bytes=ALIGN)
             sign = 1.0 if i in minus_u else -1.0
             engine.tensor_scalar(
                 minus_cu[i][:, :, cols], u_slots(i)[:, :, cols], coef[i][:], sign, ALU.mult, ALU.mult
             )
 
         def rest_of_minus_cu(i):
-            minus_cu[i] = work.tile([P, 4, P], F32, name="minus_cu")
+            minus_cu[i] = work.tile([P, 4, P], F32, name="minus_cu", align_bytes=ALIGN)
             cols = slice(CU_VECTOR, P)
             nc.scalar.activation(minus_cu[i][:, :, cols], u_slots(i)[:, :, cols], ACT.Copy, scale=coef[i][:])
 
@@ -332,7 +335,7 @@ def tile_ia3scaledqknormkeybackwardtoinput_x1_kernel(tc, ds, q, u, gamma, l, wk,
                 first = 3 * D if i % 2 == 0 else 0
                 dzg[i] = stage[:, first : first + D].rearrange("p (m t) -> p m t", t=4)
             else:
-                dzg[i] = work.tile([P, P, 4], BF16, name="dzg", align_bytes=64)[:]
+                dzg[i] = work.tile([P, P, 4], BF16, name="dzg", align_bytes=ALIGN)[:]
             nc.vector.tensor_tensor(
                 dzg[i],
                 turned[i][:].rearrange("p t m -> p m t"),
@@ -341,8 +344,8 @@ def tile_ia3scaledqknormkeybackwardtoinput_x1_kernel(tc, ds, q, u, gamma, l, wk,
             )
 
         def dz_quantize(i):
-            dzc[i] = work.tile([P, P], U32, name="dz_codes", align_bytes=64)[:]
-            dzs[i] = work.tile([P, P], U8, name="dz_scales", align_bytes=64)[:]
+            dzc[i] = work.tile([P, P], U32, name="dz_codes", align_bytes=ALIGN)[:]
+            dzs[i] = work.tile([P, P], U8, name="dz_scales", align_bytes=ALIGN)[:]
             nc.vector.quantize_mx(out=dzc[i].bitcast(X4), scales=dzs[i], in_=dzg[i].rearrange("p m t -> p (m t)"))
 
         def rows_product(i, takes=(rows_bank, rows_bank)):
@@ -389,7 +392,7 @@ def tile_ia3scaledqknormkeybackwardtoinput_x1_kernel(tc, ds, q, u, gamma, l, wk,
             k, j = place_in(PLANE_GROUPS, i)
             if j == 0:
                 plane_in[k, g] = work.tile(
-                    [P, PLANE_GROUPS[k][1] * P, 4], BF16, bufs=6, name="plane_in", align_bytes=64
+                    [P, PLANE_GROUPS[k][1] * P, 4], BF16, bufs=6, name="plane_in", align_bytes=ALIGN
                 )
             copy(plane_in[k, g][:, j * P : (j + 1) * P, :], plane_sums[i, g][:].rearrange("p t m -> p m t"))
 
@@ -397,7 +400,7 @@ def tile_ia3scaledqknormkeybackwardtoinput_x1_kernel(tc, ds, q, u, gamma, l, wk,
             a, w = PLANE_GROUPS[k]
             if k not in plane_codes:
                 plane_codes[k] = work.tile(
-                    [P, 2, w * P], U32, bufs=len(PLANE_GROUPS), name="plane_codes", align_bytes=64
+                    [P, 2, w * P], U32, bufs=len(PLANE_GROUPS), name="plane_codes", align_bytes=ALIGN
                 )
             nc.vector.quantize_mx(
                 out=plane_codes[k][:, g, :].bitcast(X4),

@@ -416,8 +416,9 @@ def tile_ia3scaledqknormkeybackwardtoinput_x1_kernel(tc, ds, q, u, gamma, l, wk,
             )
             if k in SCALE_STORES:
                 cols = slice(SCALE_STORES[k] * P, (a + w) * P)
+                queue = nc.scalar if a + w == TILES else nc.sync
                 for quad in range(4):
-                    nc.sync.dma_start(
+                    queue.dma_start(
                         out=out_2[:, 4 * quad : 4 * quad + 4, cols].rearrange("g r m -> r g m").bitcast(I32),
                         in_=plane_scales[32 * quad : 32 * quad + 4, :, cols].bitcast(I32),
                     )

@@ -367,8 +367,8 @@ def tile_ia3scaledqknormkeybackwardtoinput_x1_kernel(tc, ds, q, u, gamma, l, wk,
                 rows[i] = wide([P, 2, P, 4], F32)
             copy(rows[i][:, g, :, :], row_sums[i, g][:].rearrange("m t p -> m p t"))
 
-        def rows_store(i, halves=both):
-            nc.sync.dma_start(
+        def rows_store(i, halves=both, queue=nc.sync):
+            queue.dma_start(
                 out=out_0[i * P : (i + 1) * P, 512 * halves.start : 512 * halves.stop],
                 in_=rows[i][:, halves, :, :].rearrange("m g p t -> m (g p t)"),
             )
@@ -575,9 +575,9 @@ def tile_ia3scaledqknormkeybackwardtoinput_x1_kernel(tc, ds, q, u, gamma, l, wk,
         rows_store(LAST, pass0)
         planes_out(LAST - 1, 1, on_scalar)
         rows_out(LAST, 1)
-        rows_store(LAST, pass1)
         planes_out(LAST, 0, on_vector)
         planes_out(LAST, 1, on_scalar)
+        rows_store(LAST, pass1, nc.scalar)
         planes_quantize(last_group, 0)
         planes_quantize(last_group, 1)
         planes_store(last_group)

from contextlib import ExitStack

import concourse.mybir as mybir
from concourse.masks import make_identity

N, M, D, E = 1024, 2048, 512, 1024
FLOPS = 2 * N * M * D + 2 * M * D * E

F32 = mybir.dt.float32
BF16 = mybir.dt.bfloat16
U32 = mybir.dt.uint32
I32 = mybir.dt.int32
U8 = mybir.dt.uint8
X4 = mybir.dt.float8_e4m3fn_x4
ALU = mybir.AluOpType
ACT = mybir.ActivationFunctionType

P = 128
EPS = 1e-6
ALIGN = 256
TILES = M // P
LAST = TILES - 1
PAIR = 2 * P

DS_LOADS = [(0, 256), (256, 256), (512, 512), (1024, 512), (1536, 512)]
U_LOADS = [(0, 2), (2, 2), (4, 4), (8, 8)]
ROOT_GROUPS = [(0, 1), (1, 1)] + [(a, 2) for a in range(2, TILES, 2)]
PLANE_GROUPS = [(0, 3), (3, 4), (7, 3), (10, 2), (12, 2), (14, 2)]
SCALE_STORES = {2: 0, 5: 10}
Q_VECTOR = (96, 64)
DS_VECTOR = 64
FIRST_SINGLE = 4
SQUARES_AHEAD = 4
CU_VECTOR = 96


def place_in(groups, i):
    k = [n for n, (a, w) in enumerate(groups) if a <= i < a + w][0]
    return k, i - groups[k][0]


def tile_ia3scaledqknormkeybackwardtoinput_x1_kernel(tc, ds, q, u, gamma, l, wk, out_0, out_1, out_2):
    nc = tc.nc
    on_vector, on_scalar = nc.vector.tensor_copy, nc.scalar.copy
    with ExitStack() as ctx:
        keep = ctx.enter_context(tc.tile_pool(name="keep", bufs=1))
        work = ctx.enter_context(tc.tile_pool(name="work", bufs=3))
        psum = ctx.enter_context(tc.psum_pool(name="psum", bufs=2))
        ctx.enter_context(tc.manual_schedule())

        def wide(shape, dtype):
            return work.tile(shape, dtype, bufs=TILES, name="wide", align_bytes=ALIGN)

        def dk_bank(shape):
            return psum.tile(shape, F32, bufs=1, name="dk")

        def u_bank(shape):
            return psum.tile(shape, F32, bufs=1, name="u_bank")

        def turned_bank(shape):
            return psum.tile(shape, F32, bufs=1, name="turned")

        def rows_bank(shape):
            return psum.tile(shape, F32, bufs=2, name="rows_bank")

        def planes_bank(shape):
            return psum.tile(shape, F32, bufs=3, name="planes_bank")

        q_raw = [wide([P, 4, D], BF16) for g in range(2)]
        ds_raw = [
            keep.tile([P, 2, 4, w], BF16, name="ds_raw%d" % c, align_bytes=ALIGN) for c, (a, w) in enumerate(DS_LOADS)
        ]
        u_raw = [keep.tile([P, w, D], BF16, name="u_raw%d" % c, align_bytes=ALIGN) for c, (a, w) in enumerate(U_LOADS)]
        wk_raw = [wide([P, 4 * D], BF16) for g in range(2)]
        l_col = keep.tile([P, 4], BF16, name="l_col")
        g_col = keep.tile([P, 4], BF16, name="g_col")
        ident = keep.tile([P, P], F32, name="ident", align_bytes=ALIGN)
        minus_one = keep.tile([P, P], BF16, name="minus_one", align_bytes=ALIGN)
        warm = keep.tile([P, 1], F32, name="warm")

        def load_q(g):
            nc.sync.dma_start(out=q_raw[g][:], in_=q[512 * g : 512 * (g + 1), :].rearrange("(p j) d -> p j d", j=4))

        def load_ds(c, passes=(0, 1)):
            a, w = DS_LOADS[c]
            for g in passes:
                nc.sync.dma_start(
                    out=ds_raw[c][:, g, :, :],
                    in_=ds[512 * g : 512 * (g + 1), a : a + w].rearrange("(p j) m -> p j m", j=4),
                )

        def load_u(c):
            a, w = U_LOADS[c]
            nc.sync.dma_start(out=u_raw[c][:], in_=u[a * P : (a + w) * P, :].rearrange("(i p) d -> p i d", i=w))

        def load_wk(g):
            nc.sync.dma_start(
                out=wk_raw[g][:], in_=wk[512 * g : 512 * (g + 1), :].rearrange("(p t) d -> p (t d)", t=4)
            )

        nc.vector.memset(warm[:], 1.0)
        nc.scalar.dma_start(out=g_col[:], in_=gamma.rearrange("(p t) -> p t", t=4))
        nc.scalar.activation(warm[:], warm[:], ACT.Abs_reciprocal_sqrt)
        make_identity(nc, ident[:])
        make_identity(nc, minus_one[:])
        nc.gpsimd.tensor_scalar(minus_one[:], minus_one[:], -1.0, 0.0, ALU.mult, ALU.add)

        load_q(0)
        load_ds(0, (0,))
        load_q(1)
        load_ds(0, (1,))
        load_u(0)
        load_wk(0)
        load_ds(1)
        load_wk(1)
        nc.sync.dma_start(out=l_col[:], in_=l.rearrange("(p t) -> p t", t=4))
        load_u(1)
        load_ds(2)
        load_u(2)
        load_ds(3)
        load_u(3)
        load_ds(4)

        ssq = [keep.tile([P, w], F32, name="ssq%d" % c) for c, (a, w) in enumerate(ROOT_GROUPS)]
        r1 = [keep.tile([P, w], F32, name="r1_%d" % c) for c, (a, w) in enumerate(ROOT_GROUPS)]
        r2 = [keep.tile([P, w], F32, name="r2_%d" % c) for c, (a, w) in enumerate(ROOT_GROUPS)]

        def column(x, i):
            c, j = place_in(ROOT_GROUPS, i)
            return x[c][:, j : j + 1]

        def u_rows(i):
            c, j = place_in(U_LOADS, i)
            return u_raw[c][:, j, :]

        def u_slots(i):
            return u_rows(i).rearrange("m (p t) -> m t p", t=4)

        def sum_squares(i):
            squares = work.tile([P, D], BF16, bufs=4, name="squares", align_bytes=ALIGN)
            nc.scalar.activation(squares[:], u_rows(i), ACT.Square, accum_out=column(ssq, i))

        def inverse_root(c):
            nc.scalar.activation(r1[c][:], ssq[c][:], ACT.Abs_reciprocal_sqrt, bias=D * EPS)

        def square_of_root(c):
            nc.scalar.activation(r2[c][:], r1[c][:], ACT.Square)

        qg = [wide([P, D, 4], BF16) for g in range(2)]
        qc = keep.tile([P, 2, D], U32, name="qc", align_bytes=ALIGN)
        qs = keep.tile([P, 2, D], U8, name="qs", align_bytes=ALIGN)

        def q_interleave(g):
            dst = qg[g][:].rearrange("p (t c) j -> p c j t", t=4)
            src = q_raw[g][:].rearrange("p j (c t) -> p c j t", t=4)
            share = Q_VECTOR[g]
            on_vector(dst[:, 0:share, :, :], src[:, 0:share, :, :])
            on_scalar(dst[:, share:P, :, :], src[:, share:P, :, :])

        def q_quantize(g):
            nc.vector.quantize_mx(
                out=qc[:, g, :].bitcast(X4), scales=qs[:, g, :], in_=qg[g][:].rearrange("p c j -> p (c j)")
            )

        dsg, dsc, dss = {}, {}, {}
        pass0, pass1, both = slice(0, 1), slice(1, 2), slice(0, 2)

        def ds_interleave(k, copy, passes, lo, hi):
            c, off = place_in(DS_LOADS, k * PAIR)
            if k not in dsg:
                dsg[k] = work.tile([P, 2, PAIR, 4], BF16, bufs=2, name="dsg", align_bytes=ALIGN)
            copy(
                dsg[k][:, passes, lo:hi, :].rearrange("p g (c i) j -> p g c j i", i=4),
                ds_raw[c][:, passes, :, off + lo : off + hi].rearrange("p g j (c i) -> p g c j i", i=4),
            )

        def ds_quantize(k, passes=both, keys=slice(0, PAIR)):
            if k not in dsc:
                dsc[k] = work.tile([P, 2, PAIR], U32, name="dsc", align_bytes=ALIGN)
                dss[k] = work.tile([P, 2, PAIR], U8, name="dss", align_bytes=ALIGN)
            nc.vector.quantize_mx(
                out=dsc[k][:, passes, keys].rearrange("p g c -> p (g c)").bitcast(X4),
                scales=dss[k][:, passes, keys].rearrange("p g c -> p (g c)"),
                in_=dsg[k][:, passes, keys, :].rearrange("p g c j -> p (g c j)"),
            )

        gam = keep.tile([P, 4, P], F32, name="gam", align_bytes=ALIGN)

        def spread_gamma():
            bank = turned_bank([P, 2, P])
            words = g_col[:].bitcast(F32)
            for w in range(2):
                nc.tensor.transpose(bank[:, w, :], words[:, w : w + 1].to_broadcast([P, P]), ident[:])
            on_scalar(
                gam[:].rearrange("x (w e) p -> x w e p", e=2),
                bank[:].bitcast(BF16).rearrange("x w (p e) -> x w e p", e=2),
            )

        wg = [wide([P, 512, 4], BF16) for g in range(2)]
        wkc = keep.tile([P, E], U32, name="wkc", align_bytes=ALIGN)
        wks = keep.tile([P, E], U8, name="wks", align_bytes=ALIGN)
        wb = {}

        def wk_turn(g):
            words = wk_raw[g][:].bitcast(F32)
            for b, take in enumerate((rows_bank, planes_bank)):
                wb[g, b] = take([P, 2, 2, P])
                for a in range(2):
                    row = (2 * b + a) * 256
                    for w in range(2):
                        nc.tensor.transpose(wb[g, b][:, a, w, :], words[:, row + w : row + 256 : 2], ident[:])

        def wk_out(g, b):
            dst = wg[g][:, 256 * b : 256 * (b + 1), :].rearrange("p c k -> p (c k)").bitcast(F32)
            on_scalar(dst.rearrange("p (a c w) -> p a c w", a=2, w=2), wb[g, b][:].rearrange("p a w c -> p a c w"))

        def wk_quantize(g):
            cols = slice(512 * g, 512 * (g + 1))
            nc.vector.quantize_mx(
                out=wkc[:, cols].bitcast(X4), scales=wks[:, cols], in_=wg[g][:].rearrange("p c k -> p (c k)")
            )

        stage = keep.tile([P, 4 * D], BF16, name="stage", align_bytes=ALIGN)
        tile_c, tile_s, dzc, dzs = {}, {}, {}, {}

        def tile_interleave(i):
            c, off = place_in(DS_LOADS, i * P)
            nc.gpsimd.tensor_scalar(
                stage[:, D : 3 * D].rearrange("p (g m j) -> p g m j", g=2, j=4),
                ds_raw[c][:, :, :, off : off + P].rearrange("p g j m -> p g m j"),
                1.0,
                0.0,
                ALU.mult,
                ALU.add,
            )

        def first_tile_interleave(g):
            c, off = place_in(DS_LOADS, FIRST_SINGLE * P)
            on_scalar(
                stage[:, (1 + g) * D : (2 + g) * D].rearrange("p (c i j) -> p c j i", i=4, j=4),
                ds_raw[c][:, g, :, off : off + P].rearrange("p j (c i) -> p c j i", i=4),
            )

        def stage_quantize(i):
            codes = work.tile([P, 3 * P], U32, name="stage_codes", align_bytes=ALIGN)
            scales = work.tile([P, 3 * P], U8, name="stage_scales", align_bytes=ALIGN)
            if i % 2 == 0:
                cols, of_ds, of_dz = slice(D, 4 * D), slice(0, PAIR), slice(PAIR, 3 * P)
            else:
                cols, of_dz, of_ds = slice(0, 3 * D), slice(0, P), slice(P, 3 * P)
            nc.vector.quantize_mx(out=codes[:].bitcast(X4), scales=scales[:], in_=stage[:, cols])
            dzc[i], dzs[i] = codes[:, of_dz], scales[:, of_dz]
            tile_c[i + FIRST_SINGLE] = codes[:, of_ds].rearrange("p (g c) -> p g c", g=2)
            tile_s[i + FIRST_SINGLE] = scales[:, of_ds].rearrange("p (g c) -> p g c", g=2)

        dk, big_g, minus_u, minus_cu, coef, turned, dzg = {}, {}, {}, {}, {}, {}, {}
        row_sums, rows, plane_sums, plane_in, plane_codes = {}, {}, {}, {}, {}
        plane_scales = keep.tile([P, 2, M], U8, name="plane_scales", align_bytes=ALIGN)

        def first_product(i, passes=(0, 1), take=dk_bank):
            if i < FIRST_SINGLE:
                k, j = divmod(i, 2)
                codes, scales = dsc[k][:, :, j * P : (j + 1) * P], dss[k][:, :, j * P : (j + 1) * P]
            else:
                codes, scales = tile_c[i], tile_s[i]
            if i not in dk:
                dk[i] = take([P, D])
            for g in passes:
                nc.tensor.matmul_mx(
                    out=dk[i][:],
                    lhsT=codes[:, g, :].bitcast(X4),
                    lhsT_scale=scales[:, g, :],
                    rhs=qc[:, g, :].bitcast(X4),
                    rhs_scale=qs[:, g, :],
                    start=(g == 0),
                    stop=(g == 1),
                )

        def make_g(i):
            big_g[i] = work.tile([P, 4, P], F32, name="big_g", align_bytes=ALIGN)
            nc.vector.scalar_tensor_tensor(
                big_g[i][:], dk[i][:].rearrange("m (t p) -> m t p", t=4), column(r1, i), gam[:], ALU.mult, ALU.mult
            )

        def u_to_psum(i):
            minus_u[i] = u_bank([P, D])
            nc.tensor.matmul(minus_u[i][:], minus_one[:], u_rows(i), start=True, stop=True)

        def warm_tensor():
            idle = u_bank([P, D])
            for n in range(4):
                nc.tensor.matmul(idle[:], minus_one[:], q_raw[0][:, n, :], start=True, stop=True)

        def make_c(i):
            terms = work.tile([P, 4, P], BF16, bufs=1, name="terms", align_bytes=ALIGN)
            coef[i] = work.tile([P, 1], F32, bufs=TILES, name="coef")
            nc.vector.scalar_tensor_tensor(
                terms[:],
                minus_u[i][:].rearrange("m (p t) -> m t p", t=4) if i in minus_u else u_slots(i),
                column(r2, i),
                big_g[i][:],
                ALU.mult,
                ALU.mult,
                accum_out=coef[i][:],
            )

        def make_minus_cu(i, engine, cols=slice(0, P)):
            if i not in minus_cu:
                minus_cu[i] = work.tile([P, 4, P], F32, name="minus_cu", align_bytes=ALIGN)
            sign = 1.0 if i in minus_u else -1.0
            engine.tensor_scalar(
                minus_cu[i][:, :, cols], u_slots(i)[:, :, cols], coef[i][:], sign, ALU.mult, ALU.mult
            )

        def rest_of_minus_cu(i):
            minus_cu[i] = work.tile([P, 4, P], F32, name="minus_cu", align_bytes=ALIGN)
            cols = slice(CU_VECTOR, P)
            nc.scalar.activation(minus_cu[i][:, :, cols], u_slots(i)[:, :, cols], ACT.Copy, scale=coef[i][:])

        def turn(i, take=turned_bank):
            turned[i] = take([P, 4, P])
            for n, x in enumerate((big_g[i], minus_cu[i])):
                for t in range(4):
                    nc.tensor.matmul(
                        turned[i][:, t, :],
                        x[:, t, :],
                        ident[:],
                        start=(n == 0 and t == 0),
                        stop=(n == 1 and t == 3),
                        is_transpose=True,
                    )

        def times_l(i):
            if i + FIRST_SINGLE < TILES:
                first = 3 * D if i % 2 == 0 else 0
                dzg[i] = stage[:, first : first + D].rearrange("p (m t) -> p m t", t=4)
            else:
                dzg[i] = work.tile([P, P, 4], BF16, name="dzg", align_bytes=ALIGN)[:]
            nc.vector.tensor_tensor(
                dzg[i],
                turned[i][:].rearrange("p t m -> p m t"),
                l_col[:].unsqueeze(1).to_broadcast([P, P, 4]),
                ALU.mult,
            )

        def dz_quantize(i):
            dzc[i] = work.tile([P, P], U32, name="dz_codes", align_bytes=ALIGN)[:]
            dzs[i] = work.tile([P, P], U8, name="dz_scales", align_bytes=ALIGN)[:]
            nc.vector.quantize_mx(out=dzc[i].bitcast(X4), scales=dzs[i], in_=dzg[i].rearrange("p m t -> p (m t)"))

        def rows_product(i, takes=(rows_bank, rows_bank)):
            for g in range(2):
                cols = slice(g * 512, (g + 1) * 512)
                row_sums[i, g] = takes[g]([P, 4, P])
                nc.tensor.matmul_mx(
                    out=row_sums[i, g][:].rearrange("m t p -> m (t p)"),
                    lhsT=dzc[i].bitcast(X4),
                    lhsT_scale=dzs[i],
                    rhs=wkc[:, cols].bitcast(X4),
                    rhs_scale=wks[:, cols],
                    start=True,
                    stop=True,
                )

        def rows_out(i, g, copy=on_scalar):
            if i not in rows:
                rows[i] = wide([P, 2, P, 4], F32)
            copy(rows[i][:, g, :, :], row_sums[i, g][:].rearrange("m t p -> m p t"))

        def rows_store(i, halves=both, queue=nc.sync):
            queue.dma_start(
                out=out_0[i * P : (i + 1) * P, 512 * halves.start : 512 * halves.stop],
                in_=rows[i][:, halves, :, :].rearrange("m g p t -> m (g p t)"),
            )

        def planes_product(i, takes=(planes_bank, planes_bank)):
            for g in range(2):
                plane_sums[i, g] = takes[g]([P, 4, P])
                for t in range(4):
                    cols = slice(g * 512 + t * P, g * 512 + (t + 1) * P)
                    nc.tensor.matmul_mx(
                        out=plane_sums[i, g][:, t, :],
                        lhsT=wkc[:, cols].bitcast(X4),
                        lhsT_scale=wks[:, cols],
                        rhs=dzc[i].bitcast(X4),
                        rhs_scale=dzs[i],
                        start=True,
                        stop=True,
                    )

        def planes_out(i, g, copy):
            k, j = place_in(PLANE_GROUPS, i)
            if j == 0:
                plane_in[k, g] = work.tile(
                    [P, PLANE_GROUPS[k][1] * P, 4], BF16, bufs=6, name="plane_in", align_bytes=ALIGN
                )
            copy(plane_in[k, g][:, j * P : (j + 1) * P, :], plane_sums[i, g][:].rearrange("p t m -> p m t"))

        def planes_quantize(k, g):
            a, w = PLANE_GROUPS[k]
            if k not in plane_codes:
                plane_codes[k] = work.tile(
                    [P, 2, w * P], U32, bufs=len(PLANE_GROUPS), name="plane_codes", align_bytes=ALIGN
                )
            nc.vector.quantize_mx(
                out=plane_codes[k][:, g, :].bitcast(X4),
                scales=plane_scales[:, g, a * P : (a + w) * P],
                in_=plane_in[k, g][:].rearrange("p m t -> p (m t)"),
            )

        def planes_store(k):
            a, w = PLANE_GROUPS[k]
            nc.sync.dma_start(
                out=out_1[:, :, a * P : (a + w) * P, :].rearrange("g p m t -> p g (m t)").bitcast(I32),
                in_=plane_codes[k][:].bitcast(I32),
            )
            if k in SCALE_STORES:
                cols = slice(SCALE_STORES[k] * P, (a + w) * P)
                queue = nc.scalar if a + w == TILES else nc.sync
                for quad in range(4):
                    queue.dma_start(
                        out=out_2[:, 4 * quad : 4 * quad + 4, cols].rearrange("g r m -> r g m").bitcast(I32),
                        in_=plane_scales[32 * quad : 32 * quad + 4, :, cols].bitcast(I32),
                    )

        waiting = [(k, g) for k in range(len(PLANE_GROUPS)) for g in (1, 0)]

        def next_planes():
            k, g = waiting[0]
            waiting.remove((k, g))
            planes_quantize(k, g)
            if g == 0:
                planes_store(k)

        def empty_banks(i):
            ahead = i + 1 + SQUARES_AHEAD
            group = place_in(ROOT_GROUPS, min(ahead, LAST))[0]
            group_done = sum(ROOT_GROUPS[group]) == ahead + 1
            if ahead < TILES:
                sum_squares(ahead)
            if i + 2 in minus_u and i > 0:
                rest_of_minus_cu(i + 2)
            rows_out(i, 1)
            if group_done:
                inverse_root(group)
            rows_out(i, 0)
            rows_store(i)
            if group_done:
                square_of_root(group)
            planes_out(i, 1, on_scalar)
            planes_out(i, 0, on_scalar)

        q_interleave(0)
        ds_interleave(0, on_vector, pass0, 0, P)
        q_quantize(0)
        spread_gamma()
        ds_interleave(0, on_scalar, pass0, P, PAIR)
        q_interleave(1)
        ds_quantize(0, pass0)
        warm_tensor()
        first_product(0, (0,))
        first_product(1, (0,), planes_bank)
        ds_interleave(0, on_vector, pass1, 0, P)
        q_quantize(1)
        sum_squares(0)
        sum_squares(1)
        ds_quantize(0, pass1, slice(0, P))
        first_product(0, (1,))
        inverse_root(0)
        ds_interleave(0, on_vector, pass1, P, PAIR)
        wk_turn(0)
        ds_quantize(0, pass1, slice(P, PAIR))
        first_product(1, (1,))

        u_to_psum(1)
        inverse_root(1)
        square_of_root(0)
        make_g(0)
        ds_interleave(1, on_scalar, pass0, DS_VECTOR, PAIR)
        square_of_root(1)
        ds_interleave(1, on_vector, pass0, 0, DS_VECTOR)
        ds_interleave(1, on_scalar, pass1, DS_VECTOR, PAIR)
        make_c(0)
        make_g(1)
        make_minus_cu(0, nc.vector)
        ds_interleave(1, on_vector, pass1, 0, DS_VECTOR)
        wk_out(0, 0)
        wk_out(0, 1)
        turn(0)
        wk_turn(1)
        make_c(1)
        ds_quantize(1)
        first_product(2)
        sum_squares(2)
        sum_squares(3)
        wk_out(1, 0)
        inverse_root(2)
        wk_out(1, 1)
        square_of_root(2)
        make_minus_cu(1, nc.vector)
        wk_quantize(0)
        times_l(0)
        u_to_psum(2)
        turn(1)
        make_g(2)
        first_product(3)
        first_tile_interleave(0)
        first_tile_interleave(1)
        wk_quantize(1)
        stage_quantize(0)
        rows_product(0)
        planes_product(0)
        sum_squares(4)
        empty_banks(0)

        for s in range(2, LAST):
            ds_left = s - 1 + FIRST_SINGLE < TILES
            if ds_left:
                tile_interleave(s - 1 + FIRST_SINGLE)
            make_c(s)
            if not ds_left:
                make_minus_cu(s, nc.gpsimd)
            if s > 2:
                empty_banks(s - 2)
            make_g(s + 1)
            times_l(s - 1)
            if s + 2 < TILES:
                first_product(s + 2)
            if s % 2 == 1 and s + FIRST_SINGLE < TILES:
                u_to_psum(s + 1)
            planes_ready = sum(PLANE_GROUPS[waiting[0][0]]) + 2 <= s
            if ds_left:
                shared = s in minus_u and s > 2
                make_minus_cu(s, nc.vector, slice(0, CU_VECTOR if shared else P))
                turn(s)
                if planes_ready:
                    next_planes()
                stage_quantize(s - 1)
            else:
                next_planes()
                turn(s, u_bank if s % 2 == 1 else turned_bank)
                dz_quantize(s - 1)
            rows_product(s - 1)
            if s < LAST - 1:
                planes_product(s - 1)

        planes_product(LAST - 2, (planes_bank, dk_bank))
        make_c(LAST)
        times_l(LAST - 1)
        make_minus_cu(LAST, nc.vector)
        dz_quantize(LAST - 1)
        turn(LAST, u_bank)
        next_planes()
        rows_out(LAST - 2, 0)
        rows_out(LAST - 2, 1)
        rows_store(LAST - 2)
        planes_out(LAST - 2, 0, on_vector)
        rows_product(LAST - 1)
        planes_out(LAST - 2, 1, on_scalar)
        planes_product(LAST - 1)
        times_l(LAST)
        last_group = len(PLANE_GROUPS) - 1
        planes_quantize(last_group - 1, 0)
        dz_quantize(LAST)
        rows_product(LAST, (u_bank, turned_bank))
        planes_product(LAST, (planes_bank, dk_bank))
        rows_out(LAST - 1, 0)
        rows_store(LAST - 1, pass0)
        rows_out(LAST - 1, 1)
        rows_store(LAST - 1, pass1)
        planes_quantize(last_group - 1, 1)
        planes_store(last_group - 1)
        planes_out(LAST - 1, 0, on_vector)
        rows_out(LAST, 0, on_vector)
        rows_store(LAST, pass0)
        planes_out(LAST - 1, 1, on_scalar)
        rows_out(LAST, 1)
        planes_out(LAST, 0, on_vector)
        planes_out(LAST, 1, on_scalar)
        rows_store(LAST, pass1, nc.scalar)
        planes_quantize(last_group, 0)
        planes_quantize(last_group, 1)
        planes_store(last_group)
